import numpy as np
import ml_dtypes


def mxq(x, axis, fmt="e4m3"):
    dtype, down = {"e4m3": (ml_dtypes.float8_e4m3fn, 7), "e5m2": (ml_dtypes.float8_e5m2, 14)}[fmt]
    v = np.moveaxis(np.asarray(x, np.float32).astype(ml_dtypes.bfloat16).astype(np.float64), axis, -1)
    blocks = v.reshape(v.shape[:-1] + (-1, 32))
    amax = np.abs(blocks).max(-1, keepdims=True)
    byte = np.maximum(np.where(amax > 0, np.frexp(amax)[1] - 1 + 127, 0) - down, 1)
    scale = np.exp2(byte - 127.0)
    codes = (blocks / scale).astype(np.float32).astype(dtype).astype(np.float64)
    return np.moveaxis((codes * scale).reshape(v.shape), -1, axis)


WIDE = False


def mx_kscale(k):
    if not WIDE:
        return np.ones(k)
    levels = np.array([10, -10, 5, -5, 0])
    if k % 512:
        return np.exp2(np.random.permutation(np.resize(levels, k // 32))).repeat(32)
    a = np.empty((k // 512, 16))
    for p in range(k // 512):
        a[p, :8] = np.random.permutation(np.resize(levels, 8))
        for g in range(8):
            far = levels[np.abs(levels - a[p, g]) >= 10]
            a[p, g + 8] = far[np.random.randint(len(far))]
    return np.exp2(a.ravel()).repeat(32)


def f64(x):
    return np.asarray(x).astype(np.float64)


def striped(idx):
    return np.tile(idx.reshape(-1, 16).T, (8, 1)).astype(np.uint16)


def unstriped(offs):
    return offs[:16].T.reshape(-1).astype(np.int64)


E2M1 = np.array([0.0, 0.5, 1.0, 1.5, 2.0, 3.0, 4.0, 6.0, -0.0, -0.5, -1.0, -1.5, -2.0, -3.0, -4.0, -6.0])


def pack_weight(w, fmt):
    k, n = w.shape
    w = f64(np.asarray(w, np.float32).astype(ml_dtypes.bfloat16)).reshape(k // 32, 32, n)
    amax = np.abs(w).max(1)
    if fmt == "e4m3":
        byte = np.frexp(amax)[1] - 1 + 127 - 7
    else:
        mant, ex = np.frexp(amax / 6.0)
        byte = np.where(mant > 0.5, ex, ex - 1) + 127
    byte = np.clip(np.where(amax > 0, byte, 1), 1, 254)
    scaled = (w * np.exp2(127.0 - byte)[:, None, :]).reshape(k, n).astype(np.float32)
    by_word = np.ascontiguousarray(scaled.reshape(k // 512, 128, 4, n).transpose(0, 1, 3, 2))
    if fmt == "e4m3":
        words = by_word.astype(ml_dtypes.float8_e4m3fn).view(np.uint8)
    else:
        c = by_word.astype(ml_dtypes.float4_e2m1fn).view(np.uint8) & 0xF
        words = (c[..., 0::2] | (c[..., 1::2] << 4)).reshape(k // 512, 128, 2 * n)
    return np.ascontiguousarray(words), np.ascontiguousarray(byte.astype(np.uint8).reshape(k // 512, 16, n))


def unpack_weight(words, scales, fmt):
    g, _, n = scales.shape
    words = np.ascontiguousarray(words).reshape(g, 128, n, -1)
    if fmt == "e4m3":
        vals = words.view(ml_dtypes.float8_e4m3fn).astype(np.float64)
    else:
        nib = np.empty((g, 128, n, 4), np.uint8)
        nib[..., 0::2] = words & 0xF
        nib[..., 1::2] = words >> 4
        vals = E2M1[nib]
    vals = vals * np.repeat(np.exp2(scales.astype(np.float64) - 127.0), 8, axis=1)[..., None]
    return vals.transpose(0, 1, 3, 2).reshape(g * 512, n)


def gelu(v):
    return 0.5 * v * (1.0 + np.tanh(np.sqrt(2.0 / np.pi) * (v + 0.044715 * v**3)))


K, T, S, T2, H, N = 1024, 2048, 1024, 2048, 512, 384

def setup_inputs():
    n = np.random.standard_normal
    s = mx_kscale(K)[:, None]
    u = mx_kscale(H)[:, None]
    tab_words, tab_scales = pack_weight(n((K, T)) * s, "e4m3")
    w1_words, w1_scales = pack_weight(n((K, H)) / np.sqrt(K) / s * u.T, "e2m1")
    w2 = n((K, H)) / np.sqrt(K) / s * u.T
    w3 = 0.7 * n((H, N)) / np.sqrt(H) / u
    w4_words, w4_scales = pack_weight(0.6 * n((H, N)) / np.sqrt(H) / u, "e2m1")
    return {
        "tab_words": tab_words, "tab_scales": tab_scales,
        "offs": striped(np.random.permutation(T)[:S]),
        "offs2": striped(np.random.permutation(T2)[:S]),
        "offs3": striped(np.random.permutation(T2)[:S]),
        "w1_words": w1_words, "w1_scales": w1_scales,
        "w2": w2.astype(np.float32),
        "wg1": np.exp(0.3 * n((128, S))).astype(np.float32),
        "wg2": np.exp(0.3 * n((128, S))).astype(np.float32),
        "allot": (np.exp(0.3 * n((H, T2))) * u).astype(np.float32),
        "w3": w3.astype(np.float32),
        "w4_words": w4_words, "w4_scales": w4_scales,
    }

def reference(tab_words, tab_scales, offs, offs2, offs3, w1_words, w1_scales, w2, wg1, wg2, allot, w3, w4_words, w4_scales):
    v = unpack_weight(tab_words, tab_scales, "e4m3")[:, unstriped(offs)]
    h1 = unpack_weight(w1_words, w1_scales, "e2m1").T @ v
    h2 = mxq(f64(w2), 0, "e4m3").T @ v
    bid = np.zeros((H, T2))
    bid[:, unstriped(offs2)] = np.tile(f64(wg1), (H // 128, 1)) * h1
    ask = np.zeros((H, T2))
    ask[:, unstriped(offs3)] = np.tile(f64(wg2), (H // 128, 1)) * h2
    z = np.maximum(f64(allot) - bid, ask)
    zq = mxq(z, 0, "e4m3")
    bounded = np.tanh(mxq(f64(w3), 0, "e4m3").T @ zq)
    linear = unpack_weight(w4_words, w4_scales, "e2m1").T @ zq
    return bounded + linear

@@ -1,0 +1,334 @@
+from contextlib import ExitStack
+
+import concourse.mybir as mybir
+from concourse.masks import make_identity
+
+K, T, S, T2, H, N = 1024, 2048, 1024, 2048, 512, 384
+FLOPS = 2 * (2 * K * H * S + 2 * H * N * T2)
+
+F32 = mybir.dt.float32
+BF16 = mybir.dt.bfloat16
+I32 = mybir.dt.int32
+U32 = mybir.dt.uint32
+U16 = mybir.dt.uint16
+U8 = mybir.dt.uint8
+FP8X4 = mybir.dt.float8_e4m3fn_x4
+FP4X4 = mybir.dt.float4_e2m1fn_x4
+ACT = mybir.ActivationFunctionType
+ALU = mybir.AluOpType
+
+P = 128
+PACK = 4
+PASSES = K // (P * PACK)
+BANK = 512
+HALVES = S // BANK
+CHUNKS = T2 // BANK
+BLOCKS = BANK // P
+WIDE = 2 * BANK
+QUADS = 4
+N_TILES = N // P
+LIST_COLS = S // 16
+HALF_COLS = LIST_COLS // HALVES
+
+
+def tile_list_canal_week_clearing_kernel(
+    tc, tab_words, tab_scales, offs, offs2, offs3, w1_words, w1_scales, w2, wg1, wg2, allot, w3, w4_words, w4_scales, out
+):
+    nc = tc.nc
+    with ExitStack() as ctx:
+        lists = ctx.enter_context(tc.tile_pool(name="lists", bufs=1))
+        sb = ctx.enter_context(tc.tile_pool(name="sb", bufs=1))
+        ring = ctx.enter_context(tc.tile_pool(name="ring", bufs=4))
+        ps = ctx.enter_context(tc.psum_pool(name="ps", bufs=2))
+
+        def held(shape, dtype, name, tag=None):
+            return sb.tile(shape, dtype, name=name, tag=tag or name, align_bytes=64)
+
+        def bank(name, tag, width=BANK, dtype=F32):
+            return ps.tile([P, width], dtype, name=name, tag=tag, bufs=4 if tag == "d" else 2)
+
+        pick = lists.tile([P, LIST_COLS], U16, name="pick")
+        bid_at = lists.tile([P, LIST_COLS], U16, name="bid_at")
+        ask_at = lists.tile([P, LIST_COLS], U16, name="ask_at")
+
+        tab_plane = held([P, T], U8, "tab_plane")
+        w1_plane_raw = held([P, PASSES, H], U8, "w1_plane_raw")
+        v_plane_moved = held([P, S], U8, "v_plane_moved")
+        w4_plane = held([P, N], U8, "w4_plane")
+        nc.vector.memset(tab_plane[:].bitcast(I32), 0)
+        nc.vector.memset(w1_plane_raw[:].rearrange("p a c -> p (a c)").bitcast(I32), 0)
+        nc.vector.memset(v_plane_moved[:].bitcast(I32), 0)
+        nc.vector.memset(w4_plane[:].bitcast(I32), 0)
+        bid_pages = [held([P, T2], F32, "bid_page0"), held([P, T2], F32, "bid_page1")]
+        for page in bid_pages:
+            nc.vector.memset(page[:], 0.0)
+        ident = held([P, P], F32, "ident")
+        make_identity(nc, ident[:])
+        ident_bf = held([P, P], BF16, "ident_bf")
+        make_identity(nc, ident_bf[:])
+
+        def load_words(a):
+            words = held([P, T], I32, "tab_w%d" % a)
+            nc.sync.dma_start(words[:], tab_words[a].rearrange("p t i -> p (t i)").bitcast(I32))
+            return words
+
+        def load_wg(wg, slots, name):
+            dst = held([P, len(slots), S], F32, name)
+            rows = wg.rearrange("(q t) j -> q t j", t=PACK)[:, slots[0] : slots[-1] + 1, :]
+            for quad in (0, 2, 1, 3):
+                nc.sync.dma_start(dst[32 * quad : 32 * quad + 32, :, :], rows)
+            return [dst[:, i, :] for i in range(len(slots))]
+
+        def load_allot(t):
+            dst = held([P, T2], F32, "allot%d" % t)
+            nc.sync.dma_start(dst[:], allot.rearrange("(p t) m -> t p m", t=PACK)[t])
+            return dst
+
+        nc.sync.dma_start(pick[:], offs)
+        w1_raw = held([P, PASSES, 2 * H], U8, "w1_raw")
+        nc.sync.dma_start(w1_raw[:].bitcast(I32), w1_words.rearrange("a p n -> p a n").bitcast(I32))
+        for q in range(QUADS):
+            nc.scalar.dma_start(
+                tab_plane[32 * q : 32 * q + 4 * PASSES, :].bitcast(I32), tab_scales[:, 4 * q : 4 * q + 4, :].bitcast(I32)
+            )
+        warm = held([P, 1], F32, "warm")
+        nc.scalar.activation(warm[:], ident[:, 0:1], ACT.Tanh)
+        tab_w = [load_words(0)]
+        for q in range(QUADS):
+            nc.sync.dma_start(
+                w1_plane_raw[32 * q : 32 * q + 4, :, :].bitcast(I32),
+                w1_scales[:, 4 * q : 4 * q + 4, :].rearrange("a r c -> r a c").bitcast(I32),
+            )
+        tab_w.append(load_words(1))
+        nc.sync.dma_start(bid_at[:], offs2)
+        wg1_sb = load_wg(wg1, [0], "wg1_a") + load_wg(wg1, [1, 2], "wg1_b")
+        allot_sb = [load_allot(0), load_allot(1)]
+        w2_raw = []
+        for a in range(PASSES):
+            raw = held([P, PACK, H], F32, "w2_raw%d" % a)
+            nc.sync.dma_start(raw[:], w2[512 * a : 512 * (a + 1), :].rearrange("(p j) c -> p j c", j=PACK))
+            w2_raw.append(raw)
+        allot_sb.append(load_allot(2))
+        w3_raw = held([P, PACK, N], F32, "w3_raw")
+        nc.sync.dma_start(w3_raw[:], w3.rearrange("(p j) n -> p j n", j=PACK))
+        wg1_sb = wg1_sb + load_wg(wg1, [3], "wg1_c")
+        nc.sync.dma_start(ask_at[:], offs3)
+        wg2_sb = load_wg(wg2, [0, 1], "wg2_a") + load_wg(wg2, [2, 3], "wg2_b")
+        allot_sb.append(load_allot(3))
+        w4_codes = held([P, 2 * N], U8, "w4_codes")
+        nc.sync.dma_start(w4_codes[:].bitcast(I32), w4_words[0].bitcast(I32))
+        for q in range(QUADS):
+            nc.sync.dma_start(w4_plane[32 * q : 32 * q + 4, :].bitcast(I32), w4_scales[0, 4 * q : 4 * q + 4, :].bitcast(I32))
+
+        v_plane = held([P, S], U8, "v_plane")
+        nc.vector.tensor_copy(v_plane[:], tab_plane[:].indirect(pick[:]))
+        nc.scalar.dma_start(v_plane_moved[0:112, :].bitcast(I32), v_plane[4:116, :].bitcast(I32))
+
+        w1_codes = held([P, PASSES, 2 * H], U8, "w1_codes")
+        nc.vector.tensor_copy(
+            w1_codes[:].bitcast(U16).rearrange("p a (t g i) -> p a g t i", t=PACK, i=8),
+            w1_raw[:].bitcast(U16).rearrange("p a (g i t) -> p a g t i", t=PACK, i=8),
+        )
+        w1_plane = held([P, PASSES, H], U8, "w1_plane")
+        nc.vector.tensor_copy(
+            w1_plane[:].rearrange("p a (t g i) -> p a g t i", t=PACK, i=16),
+            w1_plane_raw[:].rearrange("p a (g i t) -> p a g t i", t=PACK, i=16),
+        )
+
+        v_codes = {}
+        for a in range(PASSES):
+            for half in range(HALVES):
+                picked = held([P, BANK], I32, "v_codes%d_%d" % (a, half))
+                nc.vector.tensor_copy(
+                    picked[:].bitcast(U32),
+                    tab_w[a][:].bitcast(U32).indirect(pick[:, half * HALF_COLS : (half + 1) * HALF_COLS]),
+                )
+                v_codes[a, half] = picked
+
+        h1 = []
+        for t in range(PACK):
+            scores = held([P, S], F32, "h1_%d" % t)
+            for half in range(HALVES):
+                cols = slice(half * BANK, (half + 1) * BANK)
+                acc = bank("h1_acc", "h")
+                for a in range(PASSES):
+                    nc.tensor.matmul_mx(
+                        out=acc[:],
+                        lhsT=w1_codes[:, a, 2 * P * t : 2 * P * (t + 1)].bitcast(FP4X4),
+                        lhsT_scale=w1_plane[:, a, P * t : P * (t + 1)],
+                        rhs=v_codes[a, half][:].bitcast(FP8X4),
+                        rhs_scale=(v_plane, v_plane_moved)[a][:, cols],
+                        start=(a == 0),
+                        stop=(a == PASSES - 1),
+                    )
+                nc.scalar.activation(scores[:, cols], acc[:], ACT.Copy, scale=-1.0)
+            h1.append(scores)
+
+        late_page = held([P, T2], F32, "bid_page2", tag="tab_w1")
+        nc.gpsimd.memset(late_page[:], 0.0)
+        bid_pages.append(late_page)
+
+        left_t = []
+
+        def place_bid(t):
+            page = bid_pages[t % len(bid_pages)]
+            if t == 0:
+                for half in range(HALVES):
+                    cols = slice(half * BANK, (half + 1) * BANK)
+                    at = bid_at[:, half * HALF_COLS : (half + 1) * HALF_COLS]
+                    nc.vector.tensor_tensor(page[:].indirect(at), h1[t][:, cols], wg1_sb[t][:, cols], ALU.mult)
+            else:
+                nc.vector.tensor_tensor(page[:].indirect(bid_at[:]), h1[t][:], wg1_sb[t], ALU.mult)
+            turned = held([P, T2], BF16, "left_t%d" % t, tag=("allot%d" % (t - 1) if t else None))
+            for c in range(CHUNKS):
+                acc = bank("left_acc", "s1")
+                for s, source in enumerate((allot_sb[t], page)):
+                    for i in range(BLOCKS):
+                        m0 = c * BANK + i * P
+                        nc.tensor.matmul(
+                            acc[:, i * P : (i + 1) * P],
+                            source[:, m0 : m0 + P],
+                            ident[:],
+                            start=(s == 0 and i == 0),
+                            stop=(s == 1 and i == BLOCKS - 1),
+                            is_transpose=True,
+                        )
+                nc.scalar.copy(turned[:, c * BANK : (c + 1) * BANK], acc[:])
+            left_t.append(turned)
+
+        def turn_back(t, g):
+            acc = bank("left", "d", WIDE, BF16)
+            for i in range(WIDE // P):
+                m0 = g * WIDE + i * P
+                nc.tensor.transpose(acc[:, i * P : (i + 1) * P], left_t[t][:, m0 : m0 + P], ident_bf[:])
+            return acc
+
+        for t in range(PACK - 1):
+            place_bid(t)
+
+        w2_codes, w2_plane = [], []
+        for a in range(PASSES):
+            rounded = held([P, PACK * H], BF16, "w2_bf%d" % a)
+            nc.scalar.copy(
+                rounded[:].rearrange("p (t m j) -> p m t j", t=PACK, j=PACK),
+                w2_raw[a][:].rearrange("p j (m t) -> p m t j", t=PACK),
+            )
+            codes = held([P, H], U32, "w2_codes%d" % a)
+            plane = held([P, H], U8, "w2_plane%d" % a)
+            nc.vector.quantize_mx(out=codes[:].bitcast(FP8X4), scales=plane[:], in_=rounded[:])
+            w2_codes.append(codes)
+            w2_plane.append(plane)
+        w3_bf = held([P, PACK * N], BF16, "w3_bf")
+        nc.scalar.copy(
+            w3_bf[:].rearrange("p (g i j) -> p g j i", i=4, j=PACK),
+            w3_raw[:].rearrange("p j (g i) -> p g j i", i=4),
+        )
+        w3_codes = held([P, N], U32, "w3_codes")
+        w3_plane = held([P, N], U8, "w3_plane")
+        for n0, n1 in ((0, 256), (256, N)):
+            nc.vector.quantize_mx(
+                out=w3_codes[:, n0:n1].bitcast(FP8X4), scales=w3_plane[:, n0:n1], in_=w3_bf[:, PACK * n0 : PACK * n1]
+            )
+
+        place_bid(PACK - 1)
+
+        h2 = []
+        for t in range(PACK):
+            scores = held([P, S], F32, "h2_%d" % t)
+            for half in range(HALVES):
+                cols = slice(half * BANK, (half + 1) * BANK)
+                acc = bank("h2_acc", "h")
+                for a in range(PASSES):
+                    nc.tensor.matmul_mx(
+                        out=acc[:],
+                        lhsT=w2_codes[a][:, P * t : P * (t + 1)].bitcast(FP8X4),
+                        lhsT_scale=w2_plane[a][:, P * t : P * (t + 1)],
+                        rhs=v_codes[a, half][:].bitcast(FP8X4),
+                        rhs_scale=v_plane[4 * a :, cols],
+                        start=(a == 0),
+                        stop=(a == PASSES - 1),
+                    )
+                nc.scalar.copy(scores[:, cols], acc[:])
+            h2.append(scores)
+
+        ask_pages = [held([P, T2], F32, "ask_page0", tag="wg1_a"), held([P, T2], F32, "ask_page1", tag="wg1_c")]
+        for page in ask_pages:
+            nc.gpsimd.memset(page[:], 0.0)
+
+        z_low = held([P, 2, T2], BF16, "z_low", tag="wg1_b")
+        z_high = [held([P, 2, BANK], BF16, "z_high%d" % c) for c in range(CHUNKS)]
+        woven_tags = ["w2_raw0", "w2_raw1", "w2_bf0", "w2_bf1"]
+        woven = [held([P, BANK, PACK], BF16, "woven%d" % c, tag=woven_tags[c]) for c in range(CHUNKS)]
+
+        left, floor = [], []
+
+        def place_ask(t):
+            left.append([turn_back(t, g) for g in range(T2 // WIDE)])
+            page = ask_pages[t % 2]
+            nc.vector.tensor_tensor(page[:].indirect(ask_at[:]), h2[t][:], wg2_sb[t], ALU.mult)
+            if t == PACK - 1:
+                floor.append(page)
+                return
+            rounded = held([P, T2], BF16, "ask_bf%d" % t, tag="ask_bf%d" % (t % 2))
+            for g in range(T2 // WIDE):
+                nc.scalar.copy(rounded[:, g * WIDE : (g + 1) * WIDE], page[:, g * WIDE : (g + 1) * WIDE])
+            floor.append(rounded)
+
+        def clear_wide(t):
+            for g in range(T2 // WIDE):
+                cols = slice(g * WIDE, (g + 1) * WIDE)
+                nc.vector.tensor_tensor(z_low[:, t, cols], left[t][g][:], floor[t][:, cols], ALU.max)
+
+        def clear_high(t, c):
+            half = slice((c % 2) * BANK, (c % 2 + 1) * BANK)
+            nc.vector.tensor_tensor(
+                z_high[c][:, t - 2, :], left[t][c // 2][:, half], floor[t][:, c * BANK : (c + 1) * BANK], ALU.max
+            )
+
+        place_ask(0)
+        place_ask(1)
+        clear_wide(0)
+        place_ask(2)
+        clear_wide(1)
+        for c in range(CHUNKS):
+            nc.scalar.copy(woven[c][:, :, 0:2], z_low[:, :, c * BANK : (c + 1) * BANK].rearrange("p t m -> p m t"))
+        place_ask(3)
+
+        result_tags = ["h1_0", "h1_1", "h1_2", "h1_3", "h2_0", "h2_1", "h2_2", "h2_3", "allot3", "left_t0", "w3_raw", "w3_bf"]
+        for c in range(CHUNKS):
+            clear_high(2, c)
+            clear_high(3, c)
+            weave = nc.vector.tensor_copy if c == 0 else nc.scalar.copy
+            weave(woven[c][:, :, 2:4], z_high[c][:].rearrange("p t m -> p m t"))
+            z_codes = held([P, BANK], U32, "z_codes%d" % c)
+            z_plane = held([P, BANK], U8, "z_plane%d" % c)
+            nc.vector.quantize_mx(
+                out=z_codes[:].bitcast(FP8X4), scales=z_plane[:], in_=woven[c][:].rearrange("p m t -> p (m t)")
+            )
+            for i in range(N_TILES):
+                rows = slice(i * P, (i + 1) * P)
+                bounded = bank("bounded", ("h", "s1")[(c * N_TILES + i) % 2])
+                nc.tensor.matmul_mx(
+                    out=bounded[:],
+                    lhsT=w3_codes[:, rows].bitcast(FP8X4),
+                    lhsT_scale=w3_plane[:, rows],
+                    rhs=z_codes[:].bitcast(FP8X4),
+                    rhs_scale=z_plane[:],
+                    start=True,
+                    stop=True,
+                )
+                linear = bank("linear", "d")
+                nc.tensor.matmul_mx(
+                    out=linear[:],
+                    lhsT=w4_codes[:, 2 * P * i : 2 * P * (i + 1)].bitcast(FP4X4),
+                    lhsT_scale=w4_plane[:, rows],
+                    rhs=z_codes[:].bitcast(FP8X4),
+                    rhs_scale=z_plane[:],
+                    start=True,
+                    stop=True,
+                )
+                squashed = ring.tile([P, BANK], F32, name="squashed")
+                nc.scalar.activation(squashed[:], bounded[:], ACT.Tanh)
+                result = held([P, BANK], F32, "result%d_%d" % (c, i), tag=result_tags[c * N_TILES + i])
+                nc.vector.tensor_tensor(result[:], linear[:], squashed[:], ALU.add)
+                nc.sync.dma_start(out[rows, c * BANK : (c + 1) * BANK], result[:])

@@ -55,13 +55,12 @@ def tile_list_canal_week_clearing_kernel(
         w1_plane_raw = held([P, PASSES, H], U8, "w1_plane_raw")
         v_plane_moved = held([P, S], U8, "v_plane_moved")
         w4_plane = held([P, N], U8, "w4_plane")
-        nc.vector.memset(tab_plane[:].bitcast(I32), 0)
+        nc.gpsimd.memset(tab_plane[:].bitcast(I32), 0)
         nc.vector.memset(w1_plane_raw[:].rearrange("p a c -> p (a c)").bitcast(I32), 0)
         nc.vector.memset(v_plane_moved[:].bitcast(I32), 0)
         nc.vector.memset(w4_plane[:].bitcast(I32), 0)
-        bid_pages = [held([P, T2], F32, "bid_page0"), held([P, T2], F32, "bid_page1")]
-        for page in bid_pages:
-            nc.vector.memset(page[:], 0.0)
+        bid_pages = [held([P, T2], F32, "bid_page0")]
+        nc.vector.memset(bid_pages[0][:].bitcast(I32), 0)
         ident = held([P, P], F32, "ident")
         make_identity(nc, ident[:])
         ident_bf = held([P, P], BF16, "ident_bf")
@@ -88,29 +87,30 @@ def tile_list_canal_week_clearing_kernel(
         w1_raw = held([P, PASSES, 2 * H], U8, "w1_raw")
         nc.sync.dma_start(w1_raw[:].bitcast(I32), w1_words.rearrange("a p n -> p a n").bitcast(I32))
         for q in range(QUADS):
-            nc.scalar.dma_start(
+            (nc.sync if q < 2 else nc.scalar).dma_start(
                 tab_plane[32 * q : 32 * q + 4 * PASSES, :].bitcast(I32), tab_scales[:, 4 * q : 4 * q + 4, :].bitcast(I32)
             )
-        warm = held([P, 1], F32, "warm")
-        nc.scalar.activation(warm[:], ident[:, 0:1], ACT.Tanh)
         tab_w = [load_words(0)]
         for q in range(QUADS):
-            nc.sync.dma_start(
+            nc.scalar.dma_start(
                 w1_plane_raw[32 * q : 32 * q + 4, :, :].bitcast(I32),
                 w1_scales[:, 4 * q : 4 * q + 4, :].rearrange("a r c -> r a c").bitcast(I32),
             )
+        warm = held([P, 1], F32, "warm")
+        nc.scalar.activation(warm[:], ident[:, 0:1], ACT.Tanh)
         tab_w.append(load_words(1))
         nc.sync.dma_start(bid_at[:], offs2)
         wg1_sb = load_wg(wg1, [0], "wg1_a") + load_wg(wg1, [1, 2], "wg1_b")
-        allot_sb = [load_allot(0), load_allot(1)]
+        allot_sb = [load_allot(0)]
+        w3_raw = held([P, PACK, N], F32, "w3_raw")
+        nc.sync.dma_start(w3_raw[:], w3.rearrange("(p j) n -> p j n", j=PACK))
         w2_raw = []
         for a in range(PASSES):
             raw = held([P, PACK, H], F32, "w2_raw%d" % a)
             nc.sync.dma_start(raw[:], w2[512 * a : 512 * (a + 1), :].rearrange("(p j) c -> p j c", j=PACK))
             w2_raw.append(raw)
+        allot_sb.append(load_allot(1))
         allot_sb.append(load_allot(2))
-        w3_raw = held([P, PACK, N], F32, "w3_raw")
-        nc.sync.dma_start(w3_raw[:], w3.rearrange("(p j) n -> p j n", j=PACK))
         wg1_sb = wg1_sb + load_wg(wg1, [3], "wg1_c")
         nc.sync.dma_start(ask_at[:], offs3)
         wg2_sb = load_wg(wg2, [0, 1], "wg2_a") + load_wg(wg2, [2, 3], "wg2_b")
@@ -164,14 +164,16 @@ def tile_list_canal_week_clearing_kernel(
                 nc.scalar.activation(scores[:, cols], acc[:], ACT.Copy, scale=-1.0)
             h1.append(scores)
 
-        late_page = held([P, T2], F32, "bid_page2", tag="tab_w1")
-        nc.gpsimd.memset(late_page[:], 0.0)
-        bid_pages.append(late_page)
+        for name, tag in (("bid_page1", "tab_w1"), ("bid_page2", "h1_0")):
+            late_page = held([P, T2], F32, name, tag=tag)
+            bid_pages.append(late_page)
 
         left_t = []
 
         def place_bid(t):
             page = bid_pages[t % len(bid_pages)]
+            if t in (1, 2):
+                nc.gpsimd.memset(page[:], 0.0)
             if t == 0:
                 for half in range(HALVES):
                     cols = slice(half * BANK, (half + 1) * BANK)
@@ -179,6 +181,9 @@ def tile_list_canal_week_clearing_kernel(
                     nc.vector.tensor_tensor(page[:].indirect(at), h1[t][:, cols], wg1_sb[t][:, cols], ALU.mult)
             else:
                 nc.vector.tensor_tensor(page[:].indirect(bid_at[:]), h1[t][:], wg1_sb[t], ALU.mult)
+
+        def take_off(t):
+            page = bid_pages[t % len(bid_pages)]
             turned = held([P, T2], BF16, "left_t%d" % t, tag=("allot%d" % (t - 1) if t else None))
             for c in range(CHUNKS):
                 acc = bank("left_acc", "s1")
@@ -203,8 +208,10 @@ def tile_list_canal_week_clearing_kernel(
                 nc.tensor.transpose(acc[:, i * P : (i + 1) * P], left_t[t][:, m0 : m0 + P], ident_bf[:])
             return acc
 
-        for t in range(PACK - 1):
-            place_bid(t)
+        place_bid(0)
+        take_off(0)
+        place_bid(1)
+        place_bid(2)
 
         w2_codes, w2_plane = [], []
         for a in range(PASSES):
@@ -250,6 +257,9 @@ def tile_list_canal_week_clearing_kernel(
                     )
                 nc.scalar.copy(scores[:, cols], acc[:])
             h2.append(scores)
+
+        for t in range(1, PACK):
+            take_off(t)
 
         ask_pages = [held([P, T2], F32, "ask_page0", tag="wg1_a"), held([P, T2], F32, "ask_page1", tag="wg1_c")]
         for page in ask_pages:

@@ -38,7 +38,7 @@ def tile_list_canal_week_clearing_kernel(
     with ExitStack() as ctx:
         lists = ctx.enter_context(tc.tile_pool(name="lists", bufs=1))
         sb = ctx.enter_context(tc.tile_pool(name="sb", bufs=1))
-        ring = ctx.enter_context(tc.tile_pool(name="ring", bufs=4))
+        ring = ctx.enter_context(tc.tile_pool(name="ring", bufs=3))
         ps = ctx.enter_context(tc.psum_pool(name="ps", bufs=2))
 
         def held(shape, dtype, name, tag=None):
@@ -59,8 +59,9 @@ def tile_list_canal_week_clearing_kernel(
         nc.vector.memset(w1_plane_raw[:].rearrange("p a c -> p (a c)").bitcast(I32), 0)
         nc.vector.memset(v_plane_moved[:].bitcast(I32), 0)
         nc.vector.memset(w4_plane[:].bitcast(I32), 0)
-        bid_pages = [held([P, T2], F32, "bid_page0")]
-        nc.vector.memset(bid_pages[0][:].bitcast(I32), 0)
+        bid_pages = [held([P, T2], F32, "bid_page0"), held([P, T2], F32, "bid_page1")]
+        for page in bid_pages:
+            nc.vector.memset(page[:].bitcast(I32), 0)
         ident = held([P, P], F32, "ident")
         make_identity(nc, ident[:])
         ident_bf = held([P, P], BF16, "ident_bf")
@@ -164,16 +165,14 @@ def tile_list_canal_week_clearing_kernel(
                 nc.scalar.activation(scores[:, cols], acc[:], ACT.Copy, scale=-1.0)
             h1.append(scores)
 
-        for name, tag in (("bid_page1", "tab_w1"), ("bid_page2", "h1_0")):
-            late_page = held([P, T2], F32, name, tag=tag)
-            bid_pages.append(late_page)
+        bid_pages.append(held([P, T2], F32, "bid_page2", tag="h1_0"))
 
         left_t = []
 
         def place_bid(t):
             page = bid_pages[t % len(bid_pages)]
-            if t in (1, 2):
-                nc.gpsimd.memset(page[:], 0.0)
+            if t == 2:
+                nc.vector.memset(page[:].bitcast(I32), 0)
             if t == 0:
                 for half in range(HALVES):
                     cols = slice(half * BANK, (half + 1) * BANK)
@@ -263,7 +262,7 @@ def tile_list_canal_week_clearing_kernel(
 
         ask_pages = [held([P, T2], F32, "ask_page0", tag="wg1_a"), held([P, T2], F32, "ask_page1", tag="wg1_c")]
         for page in ask_pages:
-            nc.gpsimd.memset(page[:], 0.0)
+            nc.vector.memset(page[:].bitcast(I32), 0)
 
         z_low = held([P, 2, T2], BF16, "z_low", tag="wg1_b")
         z_high = [held([P, 2, BANK], BF16, "z_high%d" % c) for c in range(CHUNKS)]

@@ -38,7 +38,7 @@ def tile_list_canal_week_clearing_kernel(
     with ExitStack() as ctx:
         lists = ctx.enter_context(tc.tile_pool(name="lists", bufs=1))
         sb = ctx.enter_context(tc.tile_pool(name="sb", bufs=1))
-        ring = ctx.enter_context(tc.tile_pool(name="ring", bufs=3))
+        ring = ctx.enter_context(tc.tile_pool(name="ring", bufs=4))
         ps = ctx.enter_context(tc.psum_pool(name="ps", bufs=2))
 
         def held(shape, dtype, name, tag=None):
@@ -59,13 +59,8 @@ def tile_list_canal_week_clearing_kernel(
         nc.vector.memset(w1_plane_raw[:].rearrange("p a c -> p (a c)").bitcast(I32), 0)
         nc.vector.memset(v_plane_moved[:].bitcast(I32), 0)
         nc.vector.memset(w4_plane[:].bitcast(I32), 0)
-        bid_pages = [held([P, T2], F32, "bid_page0"), held([P, T2], F32, "bid_page1")]
-        for page in bid_pages:
-            nc.vector.memset(page[:].bitcast(I32), 0)
-        ident = held([P, P], F32, "ident")
-        make_identity(nc, ident[:])
-        ident_bf = held([P, P], BF16, "ident_bf")
-        make_identity(nc, ident_bf[:])
+        bid_pages = [held([P, T2], F32, "bid_page0")]
+        nc.vector.memset(bid_pages[0][:].bitcast(I32), 0)
 
         def load_words(a):
             words = held([P, T], I32, "tab_w%d" % a)
@@ -84,38 +79,47 @@ def tile_list_canal_week_clearing_kernel(
             nc.sync.dma_start(dst[:], allot.rearrange("(p t) m -> t p m", t=PACK)[t])
             return dst
 
+        def load_w2(a):
+            raw = held([P, PACK, H], F32, "w2_raw%d" % a)
+            nc.sync.dma_start(raw[:], w2[512 * a : 512 * (a + 1), :].rearrange("(p j) c -> p j c", j=PACK))
+            return raw
+
+        ident = held([P, P], F32, "ident")
+        make_identity(nc, ident[:])
+        ident_bf = held([P, P], BF16, "ident_bf")
+        make_identity(nc, ident_bf[:])
+        warm = held([P, 1], F32, "warm")
+        nc.scalar.activation(warm[:], bid_pages[0][:, 0:1], ACT.Tanh)
+
         nc.sync.dma_start(pick[:], offs)
         w1_raw = held([P, PASSES, 2 * H], U8, "w1_raw")
         nc.sync.dma_start(w1_raw[:].bitcast(I32), w1_words.rearrange("a p n -> p a n").bitcast(I32))
+        nc.sync.dma_start(bid_at[:], offs2)
+        nc.sync.dma_start(ask_at[:], offs3)
         for q in range(QUADS):
-            (nc.sync if q < 2 else nc.scalar).dma_start(
+            nc.sync.dma_start(
                 tab_plane[32 * q : 32 * q + 4 * PASSES, :].bitcast(I32), tab_scales[:, 4 * q : 4 * q + 4, :].bitcast(I32)
             )
         tab_w = [load_words(0)]
         for q in range(QUADS):
-            nc.scalar.dma_start(
+            nc.sync.dma_start(
                 w1_plane_raw[32 * q : 32 * q + 4, :, :].bitcast(I32),
                 w1_scales[:, 4 * q : 4 * q + 4, :].rearrange("a r c -> r a c").bitcast(I32),
             )
-        warm = held([P, 1], F32, "warm")
-        nc.scalar.activation(warm[:], ident[:, 0:1], ACT.Tanh)
         tab_w.append(load_words(1))
-        nc.sync.dma_start(bid_at[:], offs2)
-        wg1_sb = load_wg(wg1, [0], "wg1_a") + load_wg(wg1, [1, 2], "wg1_b")
+        wg1_sb = load_wg(wg1, [0], "wg1_0") + load_wg(wg1, [1], "wg1_1")
+        w2_raw = [load_w2(0)]
         allot_sb = [load_allot(0)]
+        w2_raw.append(load_w2(1))
         w3_raw = held([P, PACK, N], F32, "w3_raw")
         nc.sync.dma_start(w3_raw[:], w3.rearrange("(p j) n -> p j n", j=PACK))
-        w2_raw = []
-        for a in range(PASSES):
-            raw = held([P, PACK, H], F32, "w2_raw%d" % a)
-            nc.sync.dma_start(raw[:], w2[512 * a : 512 * (a + 1), :].rearrange("(p j) c -> p j c", j=PACK))
-            w2_raw.append(raw)
         allot_sb.append(load_allot(1))
+        wg1_sb = wg1_sb + load_wg(wg1, [2], "wg1_2")
         allot_sb.append(load_allot(2))
-        wg1_sb = wg1_sb + load_wg(wg1, [3], "wg1_c")
-        nc.sync.dma_start(ask_at[:], offs3)
-        wg2_sb = load_wg(wg2, [0, 1], "wg2_a") + load_wg(wg2, [2, 3], "wg2_b")
+        wg1_sb = wg1_sb + load_wg(wg1, [3], "wg1_3")
+        wg2_sb = load_wg(wg2, [0, 1], "wg2_a")
         allot_sb.append(load_allot(3))
+        wg2_sb = wg2_sb + load_wg(wg2, [2, 3], "wg2_b")
         w4_codes = held([P, 2 * N], U8, "w4_codes")
         nc.sync.dma_start(w4_codes[:].bitcast(I32), w4_words[0].bitcast(I32))
         for q in range(QUADS):
@@ -130,7 +134,7 @@ def tile_list_canal_week_clearing_kernel(
             w1_codes[:].bitcast(U16).rearrange("p a (t g i) -> p a g t i", t=PACK, i=8),
             w1_raw[:].bitcast(U16).rearrange("p a (g i t) -> p a g t i", t=PACK, i=8),
         )
-        w1_plane = held([P, PASSES, H], U8, "w1_plane")
+        w1_plane = held([P, PASSES, H], U8, "w1_plane", tag="tab_w0")
         nc.vector.tensor_copy(
             w1_plane[:].rearrange("p a (t g i) -> p a g t i", t=PACK, i=16),
             w1_plane_raw[:].rearrange("p a (g i t) -> p a g t i", t=PACK, i=16),
@@ -165,14 +169,16 @@ def tile_list_canal_week_clearing_kernel(
                 nc.scalar.activation(scores[:, cols], acc[:], ACT.Copy, scale=-1.0)
             h1.append(scores)
 
-        bid_pages.append(held([P, T2], F32, "bid_page2", tag="h1_0"))
+        for name, tag in (("bid_page1", "tab_w1"), ("bid_page2", "h1_0")):
+            late_page = held([P, T2], F32, name, tag=tag)
+            bid_pages.append(late_page)
 
         left_t = []
 
         def place_bid(t):
             page = bid_pages[t % len(bid_pages)]
-            if t == 2:
-                nc.vector.memset(page[:].bitcast(I32), 0)
+            if t in (1, 2):
+                nc.gpsimd.memset(page[:], 0.0)
             if t == 0:
                 for half in range(HALVES):
                     cols = slice(half * BANK, (half + 1) * BANK)
@@ -183,7 +189,7 @@ def tile_list_canal_week_clearing_kernel(
 
         def take_off(t):
             page = bid_pages[t % len(bid_pages)]
-            turned = held([P, T2], BF16, "left_t%d" % t, tag=("allot%d" % (t - 1) if t else None))
+            turned = held([P, T2], BF16, "left_t%d" % t, tag=(None, "allot0", "allot1", "h2_1")[t])
             for c in range(CHUNKS):
                 acc = bank("left_acc", "s1")
                 for s, source in enumerate((allot_sb[t], page)):
@@ -210,6 +216,7 @@ def tile_list_canal_week_clearing_kernel(
         place_bid(0)
         take_off(0)
         place_bid(1)
+        take_off(1)
         place_bid(2)
 
         w2_codes, w2_plane = [], []
@@ -219,7 +226,7 @@ def tile_list_canal_week_clearing_kernel(
                 rounded[:].rearrange("p (t m j) -> p m t j", t=PACK, j=PACK),
                 w2_raw[a][:].rearrange("p j (m t) -> p m t j", t=PACK),
             )
-            codes = held([P, H], U32, "w2_codes%d" % a)
+            codes = held([P, H], U32, "w2_codes%d" % a, tag=("h1_2" if a == 1 else None))
             plane = held([P, H], U8, "w2_plane%d" % a)
             nc.vector.quantize_mx(out=codes[:].bitcast(FP8X4), scales=plane[:], in_=rounded[:])
             w2_codes.append(codes)
@@ -229,14 +236,12 @@ def tile_list_canal_week_clearing_kernel(
             w3_bf[:].rearrange("p (g i j) -> p g j i", i=4, j=PACK),
             w3_raw[:].rearrange("p j (g i) -> p g j i", i=4),
         )
-        w3_codes = held([P, N], U32, "w3_codes")
+        w3_codes = held([P, N], U32, "w3_codes", tag="wg1_2")
         w3_plane = held([P, N], U8, "w3_plane")
         for n0, n1 in ((0, 256), (256, N)):
             nc.vector.quantize_mx(
                 out=w3_codes[:, n0:n1].bitcast(FP8X4), scales=w3_plane[:, n0:n1], in_=w3_bf[:, PACK * n0 : PACK * n1]
             )
-
-        place_bid(PACK - 1)
 
         h2 = []
         for t in range(PACK):
@@ -244,27 +249,27 @@ def tile_list_canal_week_clearing_kernel(
             for half in range(HALVES):
                 cols = slice(half * BANK, (half + 1) * BANK)
                 acc = bank("h2_acc", "h")
-                for a in range(PASSES):
+                for a in reversed(range(PASSES)):
                     nc.tensor.matmul_mx(
                         out=acc[:],
                         lhsT=w2_codes[a][:, P * t : P * (t + 1)].bitcast(FP8X4),
                         lhsT_scale=w2_plane[a][:, P * t : P * (t + 1)],
                         rhs=v_codes[a, half][:].bitcast(FP8X4),
                         rhs_scale=v_plane[4 * a :, cols],
-                        start=(a == 0),
-                        stop=(a == PASSES - 1),
+                        start=(a == PASSES - 1),
+                        stop=(a == 0),
                     )
                 nc.scalar.copy(scores[:, cols], acc[:])
             h2.append(scores)
 
-        for t in range(1, PACK):
-            take_off(t)
+        place_bid(PACK - 1)
+        take_off(2)
 
-        ask_pages = [held([P, T2], F32, "ask_page0", tag="wg1_a"), held([P, T2], F32, "ask_page1", tag="wg1_c")]
+        ask_pages = [held([P, T2], F32, "ask_page0", tag="wg1_0"), held([P, T2], F32, "ask_page1", tag="wg1_3")]
         for page in ask_pages:
-            nc.vector.memset(page[:].bitcast(I32), 0)
+            nc.gpsimd.memset(page[:], 0.0)
 
-        z_low = held([P, 2, T2], BF16, "z_low", tag="wg1_b")
+        z_low = held([P, 2, T2], BF16, "z_low", tag="wg1_1")
         z_high = [held([P, 2, BANK], BF16, "z_high%d" % c) for c in range(CHUNKS)]
         woven_tags = ["w2_raw0", "w2_raw1", "w2_bf0", "w2_bf1"]
         woven = [held([P, BANK, PACK], BF16, "woven%d" % c, tag=woven_tags[c]) for c in range(CHUNKS)]
@@ -272,7 +277,6 @@ def tile_list_canal_week_clearing_kernel(
         left, floor = [], []
 
         def place_ask(t):
-            left.append([turn_back(t, g) for g in range(T2 // WIDE)])
             page = ask_pages[t % 2]
             nc.vector.tensor_tensor(page[:].indirect(ask_at[:]), h2[t][:], wg2_sb[t], ALU.mult)
             if t == PACK - 1:
@@ -294,16 +298,25 @@ def tile_list_canal_week_clearing_kernel(
                 z_high[c][:, t - 2, :], left[t][c // 2][:, half], floor[t][:, c * BANK : (c + 1) * BANK], ALU.max
             )
 
+        def bring_back(t):
+            left.append([turn_back(t, g) for g in range(T2 // WIDE)])
+
+        bring_back(0)
+        bring_back(1)
         place_ask(0)
         place_ask(1)
         clear_wide(0)
+        bring_back(2)
+        take_off(3)
         place_ask(2)
         clear_wide(1)
+        bring_back(3)
         for c in range(CHUNKS):
             nc.scalar.copy(woven[c][:, :, 0:2], z_low[:, :, c * BANK : (c + 1) * BANK].rearrange("p t m -> p m t"))
         place_ask(3)
 
         result_tags = ["h1_0", "h1_1", "h1_2", "h1_3", "h2_0", "h2_1", "h2_2", "h2_3", "allot3", "left_t0", "w3_raw", "w3_bf"]
+        z_packed = []
         for c in range(CHUNKS):
             clear_high(2, c)
             clear_high(3, c)
@@ -314,6 +327,9 @@ def tile_list_canal_week_clearing_kernel(
             nc.vector.quantize_mx(
                 out=z_codes[:].bitcast(FP8X4), scales=z_plane[:], in_=woven[c][:].rearrange("p m t -> p (m t)")
             )
+            z_packed.append((z_codes, z_plane))
+        for c in range(CHUNKS):
+            z_codes, z_plane = z_packed[c]
             for i in range(N_TILES):
                 rows = slice(i * P, (i + 1) * P)
                 bounded = bank("bounded", ("h", "s1")[(c * N_TILES + i) % 2])

@@ -28,7 +28,7 @@ WIDE = 2 * BANK
 QUADS = 4
 N_TILES = N // P
 LIST_COLS = S // 16
-HALF_COLS = LIST_COLS // HALVES
+LEAD = 256
 
 
 def tile_list_canal_week_clearing_kernel(
@@ -45,38 +45,41 @@ def tile_list_canal_week_clearing_kernel(
             return sb.tile(shape, dtype, name=name, tag=tag or name, align_bytes=64)
 
         def bank(name, tag, width=BANK, dtype=F32):
-            return ps.tile([P, width], dtype, name=name, tag=tag, bufs=4 if tag == "d" else 2)
+            return ps.tile([P, width], dtype, name=name, tag=tag, bufs=4)
 
         pick = lists.tile([P, LIST_COLS], U16, name="pick")
         bid_at = lists.tile([P, LIST_COLS], U16, name="bid_at")
         ask_at = lists.tile([P, LIST_COLS], U16, name="ask_at")
 
         tab_plane = held([P, T], U8, "tab_plane")
-        w1_plane_raw = held([P, PASSES, H], U8, "w1_plane_raw")
+        w1_plane = held([P, PASSES, H], U8, "w1_plane")
         v_plane_moved = held([P, S], U8, "v_plane_moved")
         w4_plane = held([P, N], U8, "w4_plane")
         nc.gpsimd.memset(tab_plane[:].bitcast(I32), 0)
-        nc.vector.memset(w1_plane_raw[:].rearrange("p a c -> p (a c)").bitcast(I32), 0)
+        nc.vector.memset(w1_plane[:].rearrange("p a c -> p (a c)").bitcast(I32), 0)
         nc.vector.memset(v_plane_moved[:].bitcast(I32), 0)
         nc.vector.memset(w4_plane[:].bitcast(I32), 0)
-        bid_pages = [held([P, T2], F32, "bid_page0")]
+        bid_pages = [held([P, T2], F32, "bid_page%d" % i) for i in range(2)]
         nc.vector.memset(bid_pages[0][:].bitcast(I32), 0)
+        ident = held([P, P], F32, "ident")
+        make_identity(nc, ident[:])
+        nc.gpsimd.memset(bid_pages[1][:], 0.0)
 
         def load_words(a):
             words = held([P, T], I32, "tab_w%d" % a)
             nc.sync.dma_start(words[:], tab_words[a].rearrange("p t i -> p (t i)").bitcast(I32))
             return words
 
-        def load_wg(wg, slots, name):
-            dst = held([P, len(slots), S], F32, name)
-            rows = wg.rearrange("(q t) j -> q t j", t=PACK)[:, slots[0] : slots[-1] + 1, :]
+        def load_wg2(slots, name, tag=None):
+            dst = held([P, len(slots), S], F32, name, tag=tag)
+            rows = wg2.rearrange("(q t) j -> q t j", t=PACK)[:, slots[0] : slots[-1] + 1, :]
             for quad in (0, 2, 1, 3):
                 nc.sync.dma_start(dst[32 * quad : 32 * quad + 32, :, :], rows)
             return [dst[:, i, :] for i in range(len(slots))]
 
-        def load_allot(t):
-            dst = held([P, T2], F32, "allot%d" % t)
-            nc.sync.dma_start(dst[:], allot.rearrange("(p t) m -> t p m", t=PACK)[t])
+        def load_allot(s):
+            dst = held([P, T2], F32, "allot%d" % s)
+            nc.sync.dma_start(dst[:], allot[P * s : P * (s + 1), :])
             return dst
 
         def load_w2(a):
@@ -84,159 +87,143 @@ def tile_list_canal_week_clearing_kernel(
             nc.sync.dma_start(raw[:], w2[512 * a : 512 * (a + 1), :].rearrange("(p j) c -> p j c", j=PACK))
             return raw
 
-        ident = held([P, P], F32, "ident")
-        make_identity(nc, ident[:])
-        ident_bf = held([P, P], BF16, "ident_bf")
-        make_identity(nc, ident_bf[:])
-        warm = held([P, 1], F32, "warm")
-        nc.scalar.activation(warm[:], bid_pages[0][:, 0:1], ACT.Tanh)
-
         nc.sync.dma_start(pick[:], offs)
-        w1_raw = held([P, PASSES, 2 * H], U8, "w1_raw")
-        nc.sync.dma_start(w1_raw[:].bitcast(I32), w1_words.rearrange("a p n -> p a n").bitcast(I32))
         nc.sync.dma_start(bid_at[:], offs2)
         nc.sync.dma_start(ask_at[:], offs3)
         for q in range(QUADS):
             nc.sync.dma_start(
                 tab_plane[32 * q : 32 * q + 4 * PASSES, :].bitcast(I32), tab_scales[:, 4 * q : 4 * q + 4, :].bitcast(I32)
             )
-        tab_w = [load_words(0)]
+        tab_w = [load_words(0), load_words(1)]
+        w1_codes = held([P, PASSES, 2 * H], U8, "w1_codes")
+        nc.sync.dma_start(w1_codes[:].bitcast(I32), w1_words.rearrange("a p n -> p a n").bitcast(I32))
         for q in range(QUADS):
             nc.sync.dma_start(
-                w1_plane_raw[32 * q : 32 * q + 4, :, :].bitcast(I32),
+                w1_plane[32 * q : 32 * q + 4, :, :].bitcast(I32),
                 w1_scales[:, 4 * q : 4 * q + 4, :].rearrange("a r c -> r a c").bitcast(I32),
             )
-        tab_w.append(load_words(1))
-        wg1_sb = load_wg(wg1, [0], "wg1_0") + load_wg(wg1, [1], "wg1_1")
-        w2_raw = [load_w2(0)]
+        wg1_sb = held([P, S], F32, "wg1")
+        nc.sync.dma_start(wg1_sb[:], wg1)
         allot_sb = [load_allot(0)]
+        w2_raw = [load_w2(0)]
+        allot_sb.append(load_allot(1))
         w2_raw.append(load_w2(1))
         w3_raw = held([P, PACK, N], F32, "w3_raw")
         nc.sync.dma_start(w3_raw[:], w3.rearrange("(p j) n -> p j n", j=PACK))
-        allot_sb.append(load_allot(1))
-        wg1_sb = wg1_sb + load_wg(wg1, [2], "wg1_2")
-        allot_sb.append(load_allot(2))
-        wg1_sb = wg1_sb + load_wg(wg1, [3], "wg1_3")
-        wg2_sb = load_wg(wg2, [0, 1], "wg2_a")
-        allot_sb.append(load_allot(3))
-        wg2_sb = wg2_sb + load_wg(wg2, [2, 3], "wg2_b")
+        allot_sb = allot_sb + [load_allot(2), load_allot(3)]
+        wg2_sb = load_wg2([0, 1, 2], "wg2_a") + load_wg2([3], "wg2_b")
         w4_codes = held([P, 2 * N], U8, "w4_codes")
         nc.sync.dma_start(w4_codes[:].bitcast(I32), w4_words[0].bitcast(I32))
         for q in range(QUADS):
             nc.sync.dma_start(w4_plane[32 * q : 32 * q + 4, :].bitcast(I32), w4_scales[0, 4 * q : 4 * q + 4, :].bitcast(I32))
 
+        def listed(offsets, j0, j1):
+            return offsets[:, j0 // 16 : j1 // 16]
+
         v_plane = held([P, S], U8, "v_plane")
-        nc.vector.tensor_copy(v_plane[:], tab_plane[:].indirect(pick[:]))
-        nc.scalar.dma_start(v_plane_moved[0:112, :].bitcast(I32), v_plane[4:116, :].bitcast(I32))
+        for half in range(HALVES):
+            cols = slice(half * BANK, (half + 1) * BANK)
+            nc.vector.tensor_copy(v_plane[:, cols], tab_plane[:].indirect(listed(pick, cols.start, cols.stop)))
+            nc.scalar.dma_start(v_plane_moved[0:112, cols].bitcast(I32), v_plane[4:116, cols].bitcast(I32))
 
-        w1_codes = held([P, PASSES, 2 * H], U8, "w1_codes")
-        nc.vector.tensor_copy(
-            w1_codes[:].bitcast(U16).rearrange("p a (t g i) -> p a g t i", t=PACK, i=8),
-            w1_raw[:].bitcast(U16).rearrange("p a (g i t) -> p a g t i", t=PACK, i=8),
-        )
-        w1_plane = held([P, PASSES, H], U8, "w1_plane", tag="tab_w0")
-        nc.vector.tensor_copy(
-            w1_plane[:].rearrange("p a (t g i) -> p a g t i", t=PACK, i=16),
-            w1_plane_raw[:].rearrange("p a (g i t) -> p a g t i", t=PACK, i=16),
-        )
+        v_codes = [held([P, S], I32, "v_codes%d" % a) for a in range(PASSES)]
+        for a, j0, j1 in ((0, 0, S), (1, 0, LEAD), (1, LEAD, S)):
+            nc.vector.tensor_copy(v_codes[a][:, j0:j1].bitcast(U32), tab_w[a][:].bitcast(U32).indirect(listed(pick, j0, j1)))
 
-        v_codes = {}
-        for a in range(PASSES):
-            for half in range(HALVES):
-                picked = held([P, BANK], I32, "v_codes%d_%d" % (a, half))
-                nc.vector.tensor_copy(
-                    picked[:].bitcast(U32),
-                    tab_w[a][:].bitcast(U32).indirect(pick[:, half * HALF_COLS : (half + 1) * HALF_COLS]),
-                )
-                v_codes[a, half] = picked
-
-        h1 = []
-        for t in range(PACK):
-            scores = held([P, S], F32, "h1_%d" % t)
-            for half in range(HALVES):
-                cols = slice(half * BANK, (half + 1) * BANK)
-                acc = bank("h1_acc", "h")
+        def bid_scores(s, scores, j0, j1, width):
+            acc = bank("h1_acc", "h")
+            for n0 in range(j0, j1, width):
+                cols = slice(n0, n0 + width)
                 for a in range(PASSES):
                     nc.tensor.matmul_mx(
-                        out=acc[:],
-                        lhsT=w1_codes[:, a, 2 * P * t : 2 * P * (t + 1)].bitcast(FP4X4),
-                        lhsT_scale=w1_plane[:, a, P * t : P * (t + 1)],
-                        rhs=v_codes[a, half][:].bitcast(FP8X4),
+                        out=acc[:, n0 - j0 : n0 - j0 + width],
+                        lhsT=w1_codes[:, a, 2 * P * s : 2 * P * (s + 1)].bitcast(FP4X4),
+                        lhsT_scale=w1_plane[:, a, P * s : P * (s + 1)],
+                        rhs=v_codes[a][:, cols].bitcast(FP8X4),
                         rhs_scale=(v_plane, v_plane_moved)[a][:, cols],
                         start=(a == 0),
                         stop=(a == PASSES - 1),
                     )
-                nc.scalar.activation(scores[:, cols], acc[:], ACT.Copy, scale=-1.0)
+            nc.scalar.activation(scores[:, j0:j1], acc[:, 0 : j1 - j0], ACT.Copy, scale=-1.0)
+
+        h1 = []
+        for s in range(PACK):
+            scores = held([P, S], F32, "h1_%d" % s)
+            if s == 0:
+                bid_scores(s, scores, 0, LEAD, P)
+                bid_scores(s, scores, LEAD, BANK, P)
+            else:
+                bid_scores(s, scores, 0, BANK, BANK)
+            bid_scores(s, scores, BANK, S, BANK)
             h1.append(scores)
 
-        for name, tag in (("bid_page1", "tab_w1"), ("bid_page2", "h1_0")):
-            late_page = held([P, T2], F32, name, tag=tag)
-            bid_pages.append(late_page)
+        left_t = held([P, T2 // P, 2, P, 2], BF16, "left_t")
 
-        left_t = []
-
-        def place_bid(t):
-            page = bid_pages[t % len(bid_pages)]
-            if t in (1, 2):
-                nc.gpsimd.memset(page[:], 0.0)
-            if t == 0:
-                for half in range(HALVES):
-                    cols = slice(half * BANK, (half + 1) * BANK)
-                    at = bid_at[:, half * HALF_COLS : (half + 1) * HALF_COLS]
-                    nc.vector.tensor_tensor(page[:].indirect(at), h1[t][:, cols], wg1_sb[t][:, cols], ALU.mult)
+        def place_bid(s):
+            page = bid_pages[s % 2]
+            if s == 0:
+                for j0, j1 in ((0, LEAD), (LEAD, S)):
+                    nc.vector.tensor_tensor(
+                        page[:].indirect(listed(bid_at, j0, j1)), h1[s][:, j0:j1], wg1_sb[:, j0:j1], ALU.mult
+                    )
             else:
-                nc.vector.tensor_tensor(page[:].indirect(bid_at[:]), h1[t][:], wg1_sb[t], ALU.mult)
+                nc.vector.tensor_tensor(page[:].indirect(bid_at[:]), h1[s][:], wg1_sb[:], ALU.mult)
 
-        def take_off(t):
-            page = bid_pages[t % len(bid_pages)]
-            turned = held([P, T2], BF16, "left_t%d" % t, tag=(None, "allot0", "allot1", "h2_1")[t])
-            for c in range(CHUNKS):
-                acc = bank("left_acc", "s1")
-                for s, source in enumerate((allot_sb[t], page)):
+        def take_off(s):
+            page = bid_pages[s % 2]
+            accs = [bank("left_acc", "d") for c in range(CHUNKS)]
+            for n_src, source in enumerate((allot_sb[s], page)):
+                for c, acc in enumerate(accs):
                     for i in range(BLOCKS):
                         m0 = c * BANK + i * P
                         nc.tensor.matmul(
                             acc[:, i * P : (i + 1) * P],
                             source[:, m0 : m0 + P],
                             ident[:],
-                            start=(s == 0 and i == 0),
-                            stop=(s == 1 and i == BLOCKS - 1),
+                            start=(n_src == 0 and i == 0),
+                            stop=(n_src == 1 and i == BLOCKS - 1),
                             is_transpose=True,
                         )
-                nc.scalar.copy(turned[:, c * BANK : (c + 1) * BANK], acc[:])
-            left_t.append(turned)
+            for c, acc in enumerate(accs):
+                nc.scalar.copy(
+                    left_t[:, c * BLOCKS : (c + 1) * BLOCKS, :, 32 * s : 32 * (s + 1), :].rearrange("m i u p e -> m u i p e"),
+                    acc[:].rearrange("m (i p u e) -> m u i p e", i=BLOCKS, u=2, e=2),
+                )
 
-        def turn_back(t, g):
-            acc = bank("left", "d", WIDE, BF16)
-            for i in range(WIDE // P):
-                m0 = g * WIDE + i * P
-                nc.tensor.transpose(acc[:, i * P : (i + 1) * P], left_t[t][:, m0 : m0 + P], ident_bf[:])
+        def turn_back(u, c):
+            acc = bank("left", "d")
+            for i in range(BLOCKS):
+                words = left_t[:, c * BLOCKS + i, u, :, :].rearrange("m p e -> m (p e)").bitcast(F32)
+                nc.tensor.transpose(acc[:, i * P : (i + 1) * P], words, ident[:])
             return acc
 
         place_bid(0)
-        take_off(0)
         place_bid(1)
-        take_off(1)
-        place_bid(2)
 
-        w2_codes, w2_plane = [], []
+        w2_bf = []
         for a in range(PASSES):
             rounded = held([P, PACK * H], BF16, "w2_bf%d" % a)
             nc.scalar.copy(
                 rounded[:].rearrange("p (t m j) -> p m t j", t=PACK, j=PACK),
                 w2_raw[a][:].rearrange("p j (m t) -> p m t j", t=PACK),
             )
-            codes = held([P, H], U32, "w2_codes%d" % a, tag=("h1_2" if a == 1 else None))
-            plane = held([P, H], U8, "w2_plane%d" % a)
-            nc.vector.quantize_mx(out=codes[:].bitcast(FP8X4), scales=plane[:], in_=rounded[:])
-            w2_codes.append(codes)
-            w2_plane.append(plane)
+            w2_bf.append(rounded)
         w3_bf = held([P, PACK * N], BF16, "w3_bf")
         nc.scalar.copy(
             w3_bf[:].rearrange("p (g i j) -> p g j i", i=4, j=PACK),
             w3_raw[:].rearrange("p j (g i) -> p g j i", i=4),
         )
-        w3_codes = held([P, N], U32, "w3_codes", tag="wg1_2")
+        take_off(0)
+        place_bid(2)
+        take_off(1)
+        w2_codes, w2_plane = [], []
+        for a in range(PASSES):
+            codes = held([P, H], U32, "w2_codes%d" % a, tag=(None, "allot1")[a])
+            plane = held([P, H], U8, "w2_plane%d" % a)
+            nc.vector.quantize_mx(out=codes[:].bitcast(FP8X4), scales=plane[:], in_=w2_bf[a][:])
+            w2_codes.append(codes)
+            w2_plane.append(plane)
+        w3_codes = held([P, N], U32, "w3_codes")
         w3_plane = held([P, N], U8, "w3_plane")
         for n0, n1 in ((0, 256), (256, N)):
             nc.vector.quantize_mx(
@@ -254,7 +241,7 @@ def tile_list_canal_week_clearing_kernel(
                         out=acc[:],
                         lhsT=w2_codes[a][:, P * t : P * (t + 1)].bitcast(FP8X4),
                         lhsT_scale=w2_plane[a][:, P * t : P * (t + 1)],
-                        rhs=v_codes[a, half][:].bitcast(FP8X4),
+                        rhs=v_codes[a][:, cols].bitcast(FP8X4),
                         rhs_scale=v_plane[4 * a :, cols],
                         start=(a == PASSES - 1),
                         stop=(a == 0),
@@ -262,77 +249,72 @@ def tile_list_canal_week_clearing_kernel(
                 nc.scalar.copy(scores[:, cols], acc[:])
             h2.append(scores)
 
-        place_bid(PACK - 1)
+        place_bid(3)
         take_off(2)
+        take_off(3)
 
-        ask_pages = [held([P, T2], F32, "ask_page0", tag="wg1_0"), held([P, T2], F32, "ask_page1", tag="wg1_3")]
+        ask_pages = [held([P, T2], F32, "ask_page0", tag="tab_w1"), held([P, T2], F32, "ask_page1", tag="tab_w0")]
         for page in ask_pages:
             nc.gpsimd.memset(page[:], 0.0)
 
-        z_low = held([P, 2, T2], BF16, "z_low", tag="wg1_1")
-        z_high = [held([P, 2, BANK], BF16, "z_high%d" % c) for c in range(CHUNKS)]
-        woven_tags = ["w2_raw0", "w2_raw1", "w2_bf0", "w2_bf1"]
-        woven = [held([P, BANK, PACK], BF16, "woven%d" % c, tag=woven_tags[c]) for c in range(CHUNKS)]
-
-        left, floor = [], []
+        floor = [[held([P, BANK, 2], BF16, "floor%d_%d" % (u, c)) for c in range(CHUNKS)] for u in range(2)]
+        pair_tags = ["w2_bf0", "w2_bf1", "w2_raw0", "w2_raw1"]
+        pairs = [held([P, 2, 2 * BANK], BF16, "pairs%d" % c, tag=pair_tags[c]) for c in range(CHUNKS)]
+        woven = [held([P, BANK, 2], U32, "woven%d" % c, tag="h1_%d" % c) for c in range(CHUNKS)]
 
         def place_ask(t):
-            page = ask_pages[t % 2]
-            nc.vector.tensor_tensor(page[:].indirect(ask_at[:]), h2[t][:], wg2_sb[t], ALU.mult)
-            if t == PACK - 1:
-                floor.append(page)
-                return
-            rounded = held([P, T2], BF16, "ask_bf%d" % t, tag="ask_bf%d" % (t % 2))
-            for g in range(T2 // WIDE):
-                nc.scalar.copy(rounded[:, g * WIDE : (g + 1) * WIDE], page[:, g * WIDE : (g + 1) * WIDE])
-            floor.append(rounded)
+            nc.vector.tensor_tensor(ask_pages[t % 2][:].indirect(ask_at[:]), h2[t][:], wg2_sb[t], ALU.mult)
 
-        def clear_wide(t):
-            for g in range(T2 // WIDE):
-                cols = slice(g * WIDE, (g + 1) * WIDE)
-                nc.vector.tensor_tensor(z_low[:, t, cols], left[t][g][:], floor[t][:, cols], ALU.max)
+        def round_ask(t, c):
+            nc.scalar.copy(floor[t // 2][c][:, :, t % 2], ask_pages[t % 2][:, c * BANK : (c + 1) * BANK])
 
-        def clear_high(t, c):
-            half = slice((c % 2) * BANK, (c % 2 + 1) * BANK)
+        def clear(u, c, left):
             nc.vector.tensor_tensor(
-                z_high[c][:, t - 2, :], left[t][c // 2][:, half], floor[t][:, c * BANK : (c + 1) * BANK], ALU.max
+                pairs[c][:, u, :], left[:].bitcast(BF16), floor[u][c][:].rearrange("p m e -> p (m e)"), ALU.max
             )
 
-        def bring_back(t):
-            left.append([turn_back(t, g) for g in range(T2 // WIDE)])
-
-        bring_back(0)
-        bring_back(1)
         place_ask(0)
-        place_ask(1)
-        clear_wide(0)
-        bring_back(2)
-        take_off(3)
-        place_ask(2)
-        clear_wide(1)
-        bring_back(3)
+        low = [turn_back(0, c) for c in range(CHUNKS)]
         for c in range(CHUNKS):
-            nc.scalar.copy(woven[c][:, :, 0:2], z_low[:, :, c * BANK : (c + 1) * BANK].rearrange("p t m -> p m t"))
+            round_ask(0, c)
+        place_ask(1)
+        for c in range(CHUNKS):
+            round_ask(1, c)
+        place_ask(2)
+        for c in range(CHUNKS - 1):
+            clear(0, c, low[c])
+        high = [turn_back(1, c) for c in range(CHUNKS - 1)]
+        for c in range(CHUNKS):
+            round_ask(2, c)
         place_ask(3)
+        clear(0, CHUNKS - 1, low[CHUNKS - 1])
+        high.append(turn_back(1, CHUNKS - 1))
 
-        result_tags = ["h1_0", "h1_1", "h1_2", "h1_3", "h2_0", "h2_1", "h2_2", "h2_3", "allot3", "left_t0", "w3_raw", "w3_bf"]
         z_packed = []
         for c in range(CHUNKS):
-            clear_high(2, c)
-            clear_high(3, c)
-            weave = nc.vector.tensor_copy if c == 0 else nc.scalar.copy
-            weave(woven[c][:, :, 2:4], z_high[c][:].rearrange("p t m -> p m t"))
+            round_ask(3, c)
+        for c in range(CHUNKS):
+            clear(1, c, high[c])
+            if c < 2:
+                nc.vector.tensor_copy(
+                    woven[c][:].bitcast(I32), pairs[c][:].bitcast(I32).rearrange("p u m -> p m u")
+                )
+            else:
+                nc.scalar.copy(woven[c][:], pairs[c][:].bitcast(U32).rearrange("p u m -> p m u"))
             z_codes = held([P, BANK], U32, "z_codes%d" % c)
             z_plane = held([P, BANK], U8, "z_plane%d" % c)
             nc.vector.quantize_mx(
-                out=z_codes[:].bitcast(FP8X4), scales=z_plane[:], in_=woven[c][:].rearrange("p m t -> p (m t)")
+                out=z_codes[:].bitcast(FP8X4),
+                scales=z_plane[:],
+                in_=woven[c][:].rearrange("p m u -> p (m u)").bitcast(BF16),
             )
             z_packed.append((z_codes, z_plane))
         for c in range(CHUNKS):
             z_codes, z_plane = z_packed[c]
+            result = held([P, N_TILES, BANK], F32, "result%d" % c, tag="allot%d" % c)
             for i in range(N_TILES):
                 rows = slice(i * P, (i + 1) * P)
-                bounded = bank("bounded", ("h", "s1")[(c * N_TILES + i) % 2])
+                bounded = bank("bounded", "h")
                 nc.tensor.matmul_mx(
                     out=bounded[:],
                     lhsT=w3_codes[:, rows].bitcast(FP8X4),
@@ -354,6 +336,5 @@ def tile_list_canal_week_clearing_kernel(
                 )
                 squashed = ring.tile([P, BANK], F32, name="squashed")
                 nc.scalar.activation(squashed[:], bounded[:], ACT.Tanh)
-                result = held([P, BANK], F32, "result%d_%d" % (c, i), tag=result_tags[c * N_TILES + i])
-                nc.vector.tensor_tensor(result[:], linear[:], squashed[:], ALU.add)
-                nc.sync.dma_start(out[rows, c * BANK : (c + 1) * BANK], result[:])
+                nc.vector.tensor_tensor(result[:, i, :], linear[:], squashed[:], ALU.add)
+                nc.sync.dma_start(out[rows, c * BANK : (c + 1) * BANK], result[:, i, :])

@@ -59,11 +59,10 @@ def tile_list_canal_week_clearing_kernel(
         nc.vector.memset(w1_plane[:].rearrange("p a c -> p (a c)").bitcast(I32), 0)
         nc.vector.memset(v_plane_moved[:].bitcast(I32), 0)
         nc.vector.memset(w4_plane[:].bitcast(I32), 0)
-        bid_pages = [held([P, T2], F32, "bid_page%d" % i) for i in range(2)]
+        bid_pages = [held([P, T2], F32, "bid_page0")]
         nc.vector.memset(bid_pages[0][:].bitcast(I32), 0)
         ident = held([P, P], F32, "ident")
         make_identity(nc, ident[:])
-        nc.gpsimd.memset(bid_pages[1][:], 0.0)
 
         def load_words(a):
             words = held([P, T], I32, "tab_w%d" % a)
@@ -156,6 +155,10 @@ def tile_list_canal_week_clearing_kernel(
                 bid_scores(s, scores, 0, BANK, BANK)
             bid_scores(s, scores, BANK, S, BANK)
             h1.append(scores)
+
+        second_page = held([P, T2], F32, "bid_page1", tag="tab_w1")
+        nc.gpsimd.memset(second_page[:], 0.0)
+        bid_pages.append(second_page)
 
         left_t = held([P, T2 // P, 2, P, 2], BF16, "left_t")
 
@@ -253,14 +256,15 @@ def tile_list_canal_week_clearing_kernel(
         take_off(2)
         take_off(3)
 
-        ask_pages = [held([P, T2], F32, "ask_page0", tag="tab_w1"), held([P, T2], F32, "ask_page1", tag="tab_w0")]
+        ask_pages = [held([P, T2], F32, "ask_page0", tag="allot0"), held([P, T2], F32, "ask_page1", tag="h1_0")]
         for page in ask_pages:
             nc.gpsimd.memset(page[:], 0.0)
 
         floor = [[held([P, BANK, 2], BF16, "floor%d_%d" % (u, c)) for c in range(CHUNKS)] for u in range(2)]
         pair_tags = ["w2_bf0", "w2_bf1", "w2_raw0", "w2_raw1"]
         pairs = [held([P, 2, 2 * BANK], BF16, "pairs%d" % c, tag=pair_tags[c]) for c in range(CHUNKS)]
-        woven = [held([P, BANK, 2], U32, "woven%d" % c, tag="h1_%d" % c) for c in range(CHUNKS)]
+        woven_tags = ["tab_w0", "h1_1", "h1_2", "h1_3"]
+        woven = [held([P, BANK, 2], U32, "woven%d" % c, tag=woven_tags[c]) for c in range(CHUNKS)]
 
         def place_ask(t):
             nc.vector.tensor_tensor(ask_pages[t % 2][:].indirect(ask_at[:]), h2[t][:], wg2_sb[t], ALU.mult)
@@ -290,11 +294,7 @@ def tile_list_canal_week_clearing_kernel(
         clear(0, CHUNKS - 1, low[CHUNKS - 1])
         high.append(turn_back(1, CHUNKS - 1))
 
-        z_packed = []
-        for c in range(CHUNKS):
-            round_ask(3, c)
-        for c in range(CHUNKS):
-            clear(1, c, high[c])
+        def pack(c):
             if c < 2:
                 nc.vector.tensor_copy(
                     woven[c][:].bitcast(I32), pairs[c][:].bitcast(I32).rearrange("p u m -> p m u")
@@ -308,10 +308,10 @@ def tile_list_canal_week_clearing_kernel(
                 scales=z_plane[:],
                 in_=woven[c][:].rearrange("p m u -> p (m u)").bitcast(BF16),
             )
-            z_packed.append((z_codes, z_plane))
-        for c in range(CHUNKS):
-            z_codes, z_plane = z_packed[c]
-            result = held([P, N_TILES, BANK], F32, "result%d" % c, tag="allot%d" % c)
+            return z_codes, z_plane
+
+        def read_out(c, z_codes, z_plane):
+            result = held([P, N_TILES, BANK], F32, "result%d" % c, tag=("tab_w1", "allot1", "allot2", "allot3")[c])
             for i in range(N_TILES):
                 rows = slice(i * P, (i + 1) * P)
                 bounded = bank("bounded", "h")
@@ -338,3 +338,13 @@ def tile_list_canal_week_clearing_kernel(
                 nc.scalar.activation(squashed[:], bounded[:], ACT.Tanh)
                 nc.vector.tensor_tensor(result[:, i, :], linear[:], squashed[:], ALU.add)
                 nc.sync.dma_start(out[rows, c * BANK : (c + 1) * BANK], result[:, i, :])
+
+        for c in range(CHUNKS):
+            round_ask(3, c)
+        for c in range(CHUNKS):
+            clear(1, c, high[c])
+        z_packed = [pack(c) for c in range(CHUNKS - 1)]
+        read_out(0, *z_packed[0])
+        z_packed.append(pack(CHUNKS - 1))
+        for c in range(1, CHUNKS):
+            read_out(c, *z_packed[c])

@@ -55,14 +55,14 @@ def tile_list_canal_week_clearing_kernel(
         w1_plane = held([P, PASSES, H], U8, "w1_plane")
         v_plane_moved = held([P, S], U8, "v_plane_moved")
         w4_plane = held([P, N], U8, "w4_plane")
-        nc.gpsimd.memset(tab_plane[:].bitcast(I32), 0)
+        nc.vector.memset(tab_plane[:].bitcast(I32), 0)
         nc.vector.memset(w1_plane[:].rearrange("p a c -> p (a c)").bitcast(I32), 0)
         nc.vector.memset(v_plane_moved[:].bitcast(I32), 0)
-        nc.vector.memset(w4_plane[:].bitcast(I32), 0)
         bid_pages = [held([P, T2], F32, "bid_page0")]
         nc.vector.memset(bid_pages[0][:].bitcast(I32), 0)
         ident = held([P, P], F32, "ident")
         make_identity(nc, ident[:])
+        nc.gpsimd.memset(w4_plane[:].bitcast(I32), 0)
 
         def load_words(a):
             words = held([P, T], I32, "tab_w%d" % a)
@@ -89,18 +89,20 @@ def tile_list_canal_week_clearing_kernel(
         nc.sync.dma_start(pick[:], offs)
         nc.sync.dma_start(bid_at[:], offs2)
         nc.sync.dma_start(ask_at[:], offs3)
-        for q in range(QUADS):
+        for r in range(4):
             nc.sync.dma_start(
-                tab_plane[32 * q : 32 * q + 4 * PASSES, :].bitcast(I32), tab_scales[:, 4 * q : 4 * q + 4, :].bitcast(I32)
+                tab_plane[r:P:16, :].bitcast(I32),
+                tab_scales.rearrange("a (q r) t -> r q a t", r=4)[r].bitcast(I32),
             )
-        tab_w = [load_words(0), load_words(1)]
-        w1_codes = held([P, PASSES, 2 * H], U8, "w1_codes")
-        nc.sync.dma_start(w1_codes[:].bitcast(I32), w1_words.rearrange("a p n -> p a n").bitcast(I32))
+        tab_w = [load_words(0)]
         for q in range(QUADS):
             nc.sync.dma_start(
                 w1_plane[32 * q : 32 * q + 4, :, :].bitcast(I32),
                 w1_scales[:, 4 * q : 4 * q + 4, :].rearrange("a r c -> r a c").bitcast(I32),
             )
+        tab_w.append(load_words(1))
+        w1_codes = held([P, PASSES, 2 * H], U8, "w1_codes")
+        nc.sync.dma_start(w1_codes[:].bitcast(I32), w1_words.rearrange("a p n -> p a n").bitcast(I32))
         wg1_sb = held([P, S], F32, "wg1")
         nc.sync.dma_start(wg1_sb[:], wg1)
         allot_sb = [load_allot(0)]
@@ -123,7 +125,7 @@ def tile_list_canal_week_clearing_kernel(
         for half in range(HALVES):
             cols = slice(half * BANK, (half + 1) * BANK)
             nc.vector.tensor_copy(v_plane[:, cols], tab_plane[:].indirect(listed(pick, cols.start, cols.stop)))
-            nc.scalar.dma_start(v_plane_moved[0:112, cols].bitcast(I32), v_plane[4:116, cols].bitcast(I32))
+            nc.scalar.dma_start(v_plane_moved[0:112, cols].bitcast(I32), v_plane[16:P, cols].bitcast(I32))
 
         v_codes = [held([P, S], I32, "v_codes%d" % a) for a in range(PASSES)]
         for a, j0, j1 in ((0, 0, S), (1, 0, LEAD), (1, LEAD, S)):
@@ -245,7 +247,7 @@ def tile_list_canal_week_clearing_kernel(
                         lhsT=w2_codes[a][:, P * t : P * (t + 1)].bitcast(FP8X4),
                         lhsT_scale=w2_plane[a][:, P * t : P * (t + 1)],
                         rhs=v_codes[a][:, cols].bitcast(FP8X4),
-                        rhs_scale=v_plane[4 * a :, cols],
+                        rhs_scale=(v_plane, v_plane_moved)[a][:, cols],
                         start=(a == PASSES - 1),
                         stop=(a == 0),
                     )

@@ -128,7 +128,7 @@ def tile_list_canal_week_clearing_kernel(
             nc.scalar.dma_start(v_plane_moved[0:112, cols].bitcast(I32), v_plane[16:P, cols].bitcast(I32))
 
         v_codes = [held([P, S], I32, "v_codes%d" % a) for a in range(PASSES)]
-        for a, j0, j1 in ((0, 0, S), (1, 0, LEAD), (1, LEAD, S)):
+        for a, j0, j1 in ((0, 0, S), (1, 0, LEAD), (1, LEAD, BANK), (1, BANK, S)):
             nc.vector.tensor_copy(v_codes[a][:, j0:j1].bitcast(U32), tab_w[a][:].bitcast(U32).indirect(listed(pick, j0, j1)))
 
         def bid_scores(s, scores, j0, j1, width):
@@ -196,7 +196,7 @@ def tile_list_canal_week_clearing_kernel(
                 )
 
         def turn_back(u, c):
-            acc = bank("left", "d")
+            acc = bank("left", ("d", "h")[u])
             for i in range(BLOCKS):
                 words = left_t[:, c * BLOCKS + i, u, :, :].rearrange("m p e -> m (p e)").bitcast(F32)
                 nc.tensor.transpose(acc[:, i * P : (i + 1) * P], words, ident[:])
@@ -259,20 +259,21 @@ def tile_list_canal_week_clearing_kernel(
         take_off(3)
 
         ask_pages = [held([P, T2], F32, "ask_page0", tag="allot0"), held([P, T2], F32, "ask_page1", tag="h1_0")]
+        ask_pages.append(held([P, T2], F32, "ask_page2", tag="h1_1"))
         for page in ask_pages:
             nc.gpsimd.memset(page[:], 0.0)
 
         floor = [[held([P, BANK, 2], BF16, "floor%d_%d" % (u, c)) for c in range(CHUNKS)] for u in range(2)]
-        pair_tags = ["w2_bf0", "w2_bf1", "w2_raw0", "w2_raw1"]
+        pair_tags = ["h2_3", "wg2_b", "w2_bf0", "w2_bf1"]
         pairs = [held([P, 2, 2 * BANK], BF16, "pairs%d" % c, tag=pair_tags[c]) for c in range(CHUNKS)]
-        woven_tags = ["tab_w0", "h1_1", "h1_2", "h1_3"]
+        woven_tags = ["tab_w0", "wg1", "h1_2", "h1_3"]
         woven = [held([P, BANK, 2], U32, "woven%d" % c, tag=woven_tags[c]) for c in range(CHUNKS)]
 
         def place_ask(t):
-            nc.vector.tensor_tensor(ask_pages[t % 2][:].indirect(ask_at[:]), h2[t][:], wg2_sb[t], ALU.mult)
+            nc.vector.tensor_tensor(ask_pages[(0, 1, 0, 2)[t]][:].indirect(ask_at[:]), h2[t][:], wg2_sb[t], ALU.mult)
 
         def round_ask(t, c):
-            nc.scalar.copy(floor[t // 2][c][:, :, t % 2], ask_pages[t % 2][:, c * BANK : (c + 1) * BANK])
+            nc.scalar.copy(floor[t // 2][c][:, :, t % 2], ask_pages[(0, 1, 0, 2)[t]][:, c * BANK : (c + 1) * BANK])
 
         def clear(u, c, left):
             nc.vector.tensor_tensor(
@@ -287,17 +288,13 @@ def tile_list_canal_week_clearing_kernel(
         for c in range(CHUNKS):
             round_ask(1, c)
         place_ask(2)
-        for c in range(CHUNKS - 1):
-            clear(0, c, low[c])
-        high = [turn_back(1, c) for c in range(CHUNKS - 1)]
+        high = [turn_back(1, c) for c in range(CHUNKS)]
         for c in range(CHUNKS):
             round_ask(2, c)
         place_ask(3)
-        clear(0, CHUNKS - 1, low[CHUNKS - 1])
-        high.append(turn_back(1, CHUNKS - 1))
 
         def pack(c):
-            if c < 2:
+            if c < 1:
                 nc.vector.tensor_copy(
                     woven[c][:].bitcast(I32), pairs[c][:].bitcast(I32).rearrange("p u m -> p m u")
                 )
@@ -344,6 +341,7 @@ def tile_list_canal_week_clearing_kernel(
         for c in range(CHUNKS):
             round_ask(3, c)
         for c in range(CHUNKS):
+            clear(0, c, low[c])
             clear(1, c, high[c])
         z_packed = [pack(c) for c in range(CHUNKS - 1)]
         read_out(0, *z_packed[0])

@@ -29,6 +29,8 @@ QUADS = 4
 N_TILES = N // P
 LIST_COLS = S // 16
 LEAD = 256
+PIECE = BANK // 2
+PIECES = T2 // PIECE
 
 
 def tile_list_canal_week_clearing_kernel(
@@ -195,11 +197,12 @@ def tile_list_canal_week_clearing_kernel(
                     acc[:].rearrange("m (i p u e) -> m u i p e", i=BLOCKS, u=2, e=2),
                 )
 
-        def turn_back(u, c):
-            acc = bank("left", ("d", "h")[u])
-            for i in range(BLOCKS):
-                words = left_t[:, c * BLOCKS + i, u, :, :].rearrange("m p e -> m (p e)").bitcast(F32)
-                nc.tensor.transpose(acc[:, i * P : (i + 1) * P], words, ident[:])
+        def turn_back(piece):
+            acc = bank("left", ("d", "h")[piece % 2])
+            for u in range(2):
+                for i in range(2):
+                    words = left_t[:, 2 * piece + i, u, :, :].rearrange("m p e -> m (p e)").bitcast(F32)
+                    nc.tensor.transpose(acc[:, (2 * u + i) * P : (2 * u + i + 1) * P], words, ident[:])
             return acc
 
         place_bid(0)
@@ -228,12 +231,6 @@ def tile_list_canal_week_clearing_kernel(
             nc.vector.quantize_mx(out=codes[:].bitcast(FP8X4), scales=plane[:], in_=w2_bf[a][:])
             w2_codes.append(codes)
             w2_plane.append(plane)
-        w3_codes = held([P, N], U32, "w3_codes")
-        w3_plane = held([P, N], U8, "w3_plane")
-        for n0, n1 in ((0, 256), (256, N)):
-            nc.vector.quantize_mx(
-                out=w3_codes[:, n0:n1].bitcast(FP8X4), scales=w3_plane[:, n0:n1], in_=w3_bf[:, PACK * n0 : PACK * n1]
-            )
 
         h2 = []
         for t in range(PACK):
@@ -263,49 +260,51 @@ def tile_list_canal_week_clearing_kernel(
         for page in ask_pages:
             nc.gpsimd.memset(page[:], 0.0)
 
-        floor = [[held([P, BANK, 2], BF16, "floor%d_%d" % (u, c)) for c in range(CHUNKS)] for u in range(2)]
-        pair_tags = ["h2_3", "wg2_b", "w2_bf0", "w2_bf1"]
-        pairs = [held([P, 2, 2 * BANK], BF16, "pairs%d" % c, tag=pair_tags[c]) for c in range(CHUNKS)]
+        floor = [held([P, 2, PIECE, 2], BF16, "floor%d" % piece) for piece in range(PIECES)]
         woven_tags = ["tab_w0", "wg1", "h1_2", "h1_3"]
-        woven = [held([P, BANK, 2], U32, "woven%d" % c, tag=woven_tags[c]) for c in range(CHUNKS)]
+        woven = [held([P, BANK, PACK], BF16, "woven%d" % c, tag=woven_tags[c]) for c in range(CHUNKS)]
 
         def place_ask(t):
             nc.vector.tensor_tensor(ask_pages[(0, 1, 0, 2)[t]][:].indirect(ask_at[:]), h2[t][:], wg2_sb[t], ALU.mult)
 
-        def round_ask(t, c):
-            nc.scalar.copy(floor[t // 2][c][:, :, t % 2], ask_pages[(0, 1, 0, 2)[t]][:, c * BANK : (c + 1) * BANK])
+        def round_ask(t):
+            for piece in range(PIECES):
+                nc.scalar.copy(
+                    floor[piece][:, t // 2, :, t % 2], ask_pages[(0, 1, 0, 2)[t]][:, piece * PIECE : (piece + 1) * PIECE]
+                )
 
-        def clear(u, c, left):
+        def clear(piece):
+            m0 = piece % 2 * PIECE
             nc.vector.tensor_tensor(
-                pairs[c][:, u, :], left[:].bitcast(BF16), floor[u][c][:].rearrange("p m e -> p (m e)"), ALU.max
+                woven[piece // 2][:, m0 : m0 + PIECE, :].rearrange("p m (u e) -> p m u e", u=2),
+                left[piece][:].bitcast(BF16).rearrange("p (u m e) -> p m u e", u=2, e=2),
+                floor[piece][:].rearrange("p u m e -> p m u e"),
+                ALU.max,
             )
 
         place_ask(0)
-        low = [turn_back(0, c) for c in range(CHUNKS)]
-        for c in range(CHUNKS):
-            round_ask(0, c)
+        round_ask(0)
         place_ask(1)
-        for c in range(CHUNKS):
-            round_ask(1, c)
+        left = [turn_back(piece) for piece in range(PIECES)]
+        round_ask(1)
         place_ask(2)
-        high = [turn_back(1, c) for c in range(CHUNKS)]
-        for c in range(CHUNKS):
-            round_ask(2, c)
+        round_ask(2)
         place_ask(3)
 
+        w3_codes = held([P, N], U32, "w3_codes", tag="h2_3")
+        w3_plane = held([P, N], U8, "w3_plane")
+        for n0, n1 in ((0, 256), (256, N)):
+            nc.vector.quantize_mx(
+                out=w3_codes[:, n0:n1].bitcast(FP8X4), scales=w3_plane[:, n0:n1], in_=w3_bf[:, PACK * n0 : PACK * n1]
+            )
+
         def pack(c):
-            if c < 1:
-                nc.vector.tensor_copy(
-                    woven[c][:].bitcast(I32), pairs[c][:].bitcast(I32).rearrange("p u m -> p m u")
-                )
-            else:
-                nc.scalar.copy(woven[c][:], pairs[c][:].bitcast(U32).rearrange("p u m -> p m u"))
             z_codes = held([P, BANK], U32, "z_codes%d" % c)
             z_plane = held([P, BANK], U8, "z_plane%d" % c)
             nc.vector.quantize_mx(
                 out=z_codes[:].bitcast(FP8X4),
                 scales=z_plane[:],
-                in_=woven[c][:].rearrange("p m u -> p (m u)").bitcast(BF16),
+                in_=woven[c][:].rearrange("p m t -> p (m t)"),
             )
             return z_codes, z_plane
 
@@ -338,13 +337,11 @@ def tile_list_canal_week_clearing_kernel(
                 nc.vector.tensor_tensor(result[:, i, :], linear[:], squashed[:], ALU.add)
                 nc.sync.dma_start(out[rows, c * BANK : (c + 1) * BANK], result[:, i, :])
 
+        round_ask(3)
+        z_packed = []
         for c in range(CHUNKS):
-            round_ask(3, c)
+            clear(2 * c)
+            clear(2 * c + 1)
+            z_packed.append(pack(c))
         for c in range(CHUNKS):
-            clear(0, c, low[c])
-            clear(1, c, high[c])
-        z_packed = [pack(c) for c in range(CHUNKS - 1)]
-        read_out(0, *z_packed[0])
-        z_packed.append(pack(CHUNKS - 1))
-        for c in range(1, CHUNKS):
             read_out(c, *z_packed[c])

@@ -31,6 +31,7 @@ LIST_COLS = S // 16
 LEAD = 256
 PIECE = BANK // 2
 PIECES = T2 // PIECE
+BANKED = 5
 
 
 def tile_list_canal_week_clearing_kernel(
@@ -40,14 +41,13 @@ def tile_list_canal_week_clearing_kernel(
     with ExitStack() as ctx:
         lists = ctx.enter_context(tc.tile_pool(name="lists", bufs=1))
         sb = ctx.enter_context(tc.tile_pool(name="sb", bufs=1))
-        ring = ctx.enter_context(tc.tile_pool(name="ring", bufs=4))
         ps = ctx.enter_context(tc.psum_pool(name="ps", bufs=2))
 
         def held(shape, dtype, name, tag=None):
             return sb.tile(shape, dtype, name=name, tag=tag or name, align_bytes=64)
 
         def bank(name, tag, width=BANK, dtype=F32):
-            return ps.tile([P, width], dtype, name=name, tag=tag, bufs=4)
+            return ps.tile([P, width], dtype, name=name, tag=tag, bufs={"h": 3, "d": 5}[tag])
 
         pick = lists.tile([P, LIST_COLS], U16, name="pick")
         bid_at = lists.tile([P, LIST_COLS], U16, name="bid_at")
@@ -197,13 +197,21 @@ def tile_list_canal_week_clearing_kernel(
                     acc[:].rearrange("m (i p u e) -> m u i p e", i=BLOCKS, u=2, e=2),
                 )
 
+        left_tags = ["w2_raw0", "w2_raw1", "w2_bf0"]
+        left_sb = [held([P, BANK, 2], F32, "left%d" % c, tag=left_tags[c]) for c in range(3)]
+
         def turn_back(piece):
-            acc = bank("left", ("d", "h")[piece % 2])
+            acc = bank("left", "d")
             for u in range(2):
                 for i in range(2):
                     words = left_t[:, 2 * piece + i, u, :, :].rearrange("m p e -> m (p e)").bitcast(F32)
                     nc.tensor.transpose(acc[:, (2 * u + i) * P : (2 * u + i + 1) * P], words, ident[:])
-            return acc
+            if piece >= BANKED:
+                return acc[:].bitcast(BF16).rearrange("p (u m e) -> p m u e", u=2, e=2)
+            m0 = piece % 2 * PIECE
+            parked = left_sb[piece // 2][:, m0 : m0 + PIECE, :]
+            nc.scalar.copy(parked, acc[:].rearrange("p (u m) -> p m u", u=2))
+            return parked.rearrange("p m u -> p (m u)").bitcast(BF16).rearrange("p (m u e) -> p m u e", u=2, e=2)
 
         place_bid(0)
         place_bid(1)
@@ -257,6 +265,7 @@ def tile_list_canal_week_clearing_kernel(
 
         ask_pages = [held([P, T2], F32, "ask_page0", tag="allot0"), held([P, T2], F32, "ask_page1", tag="h1_0")]
         ask_pages.append(held([P, T2], F32, "ask_page2", tag="h1_1"))
+        ask_pages.append(held([P, T2], F32, "ask_page3", tag="allot2"))
         for page in ask_pages:
             nc.gpsimd.memset(page[:], 0.0)
 
@@ -265,19 +274,19 @@ def tile_list_canal_week_clearing_kernel(
         woven = [held([P, BANK, PACK], BF16, "woven%d" % c, tag=woven_tags[c]) for c in range(CHUNKS)]
 
         def place_ask(t):
-            nc.vector.tensor_tensor(ask_pages[(0, 1, 0, 2)[t]][:].indirect(ask_at[:]), h2[t][:], wg2_sb[t], ALU.mult)
+            nc.vector.tensor_tensor(ask_pages[t][:].indirect(ask_at[:]), h2[t][:], wg2_sb[t], ALU.mult)
 
         def round_ask(t):
             for piece in range(PIECES):
                 nc.scalar.copy(
-                    floor[piece][:, t // 2, :, t % 2], ask_pages[(0, 1, 0, 2)[t]][:, piece * PIECE : (piece + 1) * PIECE]
+                    floor[piece][:, t // 2, :, t % 2], ask_pages[t][:, piece * PIECE : (piece + 1) * PIECE]
                 )
 
         def clear(piece):
             m0 = piece % 2 * PIECE
             nc.vector.tensor_tensor(
                 woven[piece // 2][:, m0 : m0 + PIECE, :].rearrange("p m (u e) -> p m u e", u=2),
-                left[piece][:].bitcast(BF16).rearrange("p (u m e) -> p m u e", u=2, e=2),
+                left[piece],
                 floor[piece][:].rearrange("p u m e -> p m u e"),
                 ALU.max,
             )
@@ -298,8 +307,20 @@ def tile_list_canal_week_clearing_kernel(
                 out=w3_codes[:, n0:n1].bitcast(FP8X4), scales=w3_plane[:, n0:n1], in_=w3_bf[:, PACK * n0 : PACK * n1]
             )
 
+        unread = bank("unread", "h")
+        for n in range(4):
+            nc.tensor.matmul_mx(
+                out=unread[:],
+                lhsT=w3_codes[:, 0:P].bitcast(FP8X4),
+                lhsT_scale=w3_plane[:, 0:P],
+                rhs=v_codes[0][:, 0:BANK].bitcast(FP8X4),
+                rhs_scale=v_plane[:, 0:BANK],
+                start=True,
+                stop=True,
+            )
+
         def pack(c):
-            z_codes = held([P, BANK], U32, "z_codes%d" % c)
+            z_codes = held([P, BANK], U32, "z_codes%d" % c, tag=(None, None, "copied1", "copied2")[c])
             z_plane = held([P, BANK], U8, "z_plane%d" % c)
             nc.vector.quantize_mx(
                 out=z_codes[:].bitcast(FP8X4),
@@ -308,40 +329,66 @@ def tile_list_canal_week_clearing_kernel(
             )
             return z_codes, z_plane
 
-        def read_out(c, z_codes, z_plane):
-            result = held([P, N_TILES, BANK], F32, "result%d" % c, tag=("tab_w1", "allot1", "allot2", "allot3")[c])
-            for i in range(N_TILES):
-                rows = slice(i * P, (i + 1) * P)
-                bounded = bank("bounded", "h")
-                nc.tensor.matmul_mx(
-                    out=bounded[:],
-                    lhsT=w3_codes[:, rows].bitcast(FP8X4),
-                    lhsT_scale=w3_plane[:, rows],
-                    rhs=z_codes[:].bitcast(FP8X4),
-                    rhs_scale=z_plane[:],
-                    start=True,
-                    stop=True,
-                )
-                linear = bank("linear", "d")
-                nc.tensor.matmul_mx(
-                    out=linear[:],
-                    lhsT=w4_codes[:, 2 * P * i : 2 * P * (i + 1)].bitcast(FP4X4),
-                    lhsT_scale=w4_plane[:, rows],
-                    rhs=z_codes[:].bitcast(FP8X4),
-                    rhs_scale=z_plane[:],
-                    start=True,
-                    stop=True,
-                )
-                squashed = ring.tile([P, BANK], F32, name="squashed")
-                nc.scalar.activation(squashed[:], bounded[:], ACT.Tanh)
-                nc.vector.tensor_tensor(result[:, i, :], linear[:], squashed[:], ALU.add)
-                nc.sync.dma_start(out[rows, c * BANK : (c + 1) * BANK], result[:, i, :])
+        result_tags = ("tab_w1", "allot1", "allot0", "allot3")
+        results = [held([P, N_TILES, BANK], F32, "result%d" % c, tag=result_tags[c]) for c in range(CHUNKS)]
+
+        squash_tags = ("left_t", "wg2_a", "w3_raw", None)
+        squashes = [held([P, N_TILES, BANK], F32, "squashed%d" % c, tag=squash_tags[c]) for c in range(CHUNKS)]
+
+        def read_out(c, i, behind=None):
+            z_codes, z_plane = z_packed[c]
+            rows = slice(i * P, (i + 1) * P)
+            bounded = bank("bounded", "h")
+            nc.tensor.matmul_mx(
+                out=bounded[:],
+                lhsT=w3_codes[:, rows].bitcast(FP8X4),
+                lhsT_scale=w3_plane[:, rows],
+                rhs=z_codes[:].bitcast(FP8X4),
+                rhs_scale=z_plane[:],
+                start=True,
+                stop=True,
+            )
+            linear = bank("linear", "d")
+            nc.tensor.matmul_mx(
+                out=linear[:],
+                lhsT=w4_codes[:, 2 * P * i : 2 * P * (i + 1)].bitcast(FP4X4),
+                lhsT_scale=w4_plane[:, rows],
+                rhs=z_codes[:].bitcast(FP8X4),
+                rhs_scale=z_plane[:],
+                start=True,
+                stop=True,
+            )
+            squashed = squashes[c][:, i, :]
+            nc.scalar.activation(squashed, bounded[:], ACT.Tanh)
+            if behind is None:
+                result = results[c][:, i, :]
+                nc.vector.tensor_tensor(result, linear[:], squashed, ALU.add)
+            else:
+                copied = held([P, BANK], F32, "copied%d" % behind)
+                nc.scalar.copy(copied[:], linear[:])
+                result = held([P, BANK], F32, "late%d" % behind, tag=woven_tags[behind])[:]
+                nc.gpsimd.tensor_tensor(result, copied[:], squashed, ALU.add)
+            nc.sync.dma_start(out[rows, c * BANK : (c + 1) * BANK], result)
 
         round_ask(3)
         z_packed = []
-        for c in range(CHUNKS):
-            clear(2 * c)
-            clear(2 * c + 1)
-            z_packed.append(pack(c))
-        for c in range(CHUNKS):
-            read_out(c, *z_packed[c])
+        clear(0)
+        clear(1)
+        clear(2)
+        z_packed.append(pack(0))
+        clear(3)
+        clear(4)
+        z_packed.append(pack(1))
+        read_out(0, 0, behind=1)
+        clear(5)
+        clear(6)
+        clear(7)
+        read_out(0, 1)
+        z_packed.append(pack(2))
+        read_out(0, 2, behind=2)
+        for i in range(N_TILES):
+            read_out(1, i)
+        z_packed.append(pack(3))
+        for c in range(2, CHUNKS):
+            for i in range(N_TILES):
+                read_out(c, i)

@@ -55,16 +55,15 @@ def tile_list_canal_week_clearing_kernel(
 
         tab_plane = held([P, T], U8, "tab_plane")
         w1_plane = held([P, PASSES, H], U8, "w1_plane")
-        v_plane_moved = held([P, S], U8, "v_plane_moved")
-        w4_plane = held([P, N], U8, "w4_plane")
-        nc.vector.memset(tab_plane[:].bitcast(I32), 0)
+        v_plane = held([P, PASSES, S], U8, "v_plane")
+        nc.vector.memset(tab_plane[0:96, :].bitcast(I32), 0)
         nc.vector.memset(w1_plane[:].rearrange("p a c -> p (a c)").bitcast(I32), 0)
-        nc.vector.memset(v_plane_moved[:].bitcast(I32), 0)
+        nc.vector.memset(v_plane[:].rearrange("p a j -> p (a j)").bitcast(I32), 0)
+        ident = held([P, P], F32, "ident")
+        nc.vector.memset(ident[:], 0.0)
+        make_identity(nc, ident[:], nomemset=True)
         bid_pages = [held([P, T2], F32, "bid_page0")]
         nc.vector.memset(bid_pages[0][:].bitcast(I32), 0)
-        ident = held([P, P], F32, "ident")
-        make_identity(nc, ident[:])
-        nc.gpsimd.memset(w4_plane[:].bitcast(I32), 0)
 
         def load_words(a):
             words = held([P, T], I32, "tab_w%d" % a)
@@ -88,14 +87,8 @@ def tile_list_canal_week_clearing_kernel(
             nc.sync.dma_start(raw[:], w2[512 * a : 512 * (a + 1), :].rearrange("(p j) c -> p j c", j=PACK))
             return raw
 
+        nc.sync.dma_start(tab_plane[96:P, :].bitcast(I32), tab_scales.rearrange("a q t -> q a t").bitcast(I32))
         nc.sync.dma_start(pick[:], offs)
-        nc.sync.dma_start(bid_at[:], offs2)
-        nc.sync.dma_start(ask_at[:], offs3)
-        for r in range(4):
-            nc.sync.dma_start(
-                tab_plane[r:P:16, :].bitcast(I32),
-                tab_scales.rearrange("a (q r) t -> r q a t", r=4)[r].bitcast(I32),
-            )
         tab_w = [load_words(0)]
         for q in range(QUADS):
             nc.sync.dma_start(
@@ -104,9 +97,24 @@ def tile_list_canal_week_clearing_kernel(
             )
         tab_w.append(load_words(1))
         w1_codes = held([P, PASSES, 2 * H], U8, "w1_codes")
-        nc.sync.dma_start(w1_codes[:].bitcast(I32), w1_words.rearrange("a p n -> p a n").bitcast(I32))
+        w1_rows = w1_words.rearrange("a p n -> p a n")
+        nc.sync.dma_start(w1_codes[:, :, 0 : 2 * P].bitcast(I32), w1_rows[:, :, 0 : 2 * P].bitcast(I32))
+
+        def listed(offsets, j0, j1):
+            return offsets[:, j0 // 16 : j1 // 16]
+
+        picked_plane = held([P, S], U8, "picked_plane")
+        nc.vector.tensor_copy(picked_plane[:], tab_plane[:].indirect(pick[:]))
+        for q in range(QUADS):
+            nc.sync.dma_start(
+                v_plane[32 * q : 32 * q + 4, :, :].bitcast(I32), picked_plane[96 + 8 * q : 104 + 8 * q, :].bitcast(I32)
+            )
+
         wg1_sb = held([P, S], F32, "wg1")
-        nc.sync.dma_start(wg1_sb[:], wg1)
+        nc.sync.dma_start(bid_at[:], offs2)
+        nc.sync.dma_start(wg1_sb[:, 0:LEAD], wg1[:, 0:LEAD])
+        nc.sync.dma_start(w1_codes[:, :, 2 * P :].bitcast(I32), w1_rows[:, :, 2 * P :].bitcast(I32))
+        nc.sync.dma_start(wg1_sb[:, LEAD:S], wg1[:, LEAD:S])
         allot_sb = [load_allot(0)]
         w2_raw = [load_w2(0)]
         allot_sb.append(load_allot(1))
@@ -114,20 +122,10 @@ def tile_list_canal_week_clearing_kernel(
         w3_raw = held([P, PACK, N], F32, "w3_raw")
         nc.sync.dma_start(w3_raw[:], w3.rearrange("(p j) n -> p j n", j=PACK))
         allot_sb = allot_sb + [load_allot(2), load_allot(3)]
+        nc.sync.dma_start(ask_at[:], offs3)
         wg2_sb = load_wg2([0, 1, 2], "wg2_a") + load_wg2([3], "wg2_b")
         w4_codes = held([P, 2 * N], U8, "w4_codes")
         nc.sync.dma_start(w4_codes[:].bitcast(I32), w4_words[0].bitcast(I32))
-        for q in range(QUADS):
-            nc.sync.dma_start(w4_plane[32 * q : 32 * q + 4, :].bitcast(I32), w4_scales[0, 4 * q : 4 * q + 4, :].bitcast(I32))
-
-        def listed(offsets, j0, j1):
-            return offsets[:, j0 // 16 : j1 // 16]
-
-        v_plane = held([P, S], U8, "v_plane")
-        for half in range(HALVES):
-            cols = slice(half * BANK, (half + 1) * BANK)
-            nc.vector.tensor_copy(v_plane[:, cols], tab_plane[:].indirect(listed(pick, cols.start, cols.stop)))
-            nc.scalar.dma_start(v_plane_moved[0:112, cols].bitcast(I32), v_plane[16:P, cols].bitcast(I32))
 
         v_codes = [held([P, S], I32, "v_codes%d" % a) for a in range(PASSES)]
         for a, j0, j1 in ((0, 0, S), (1, 0, LEAD), (1, LEAD, BANK), (1, BANK, S)):
@@ -143,7 +141,7 @@ def tile_list_canal_week_clearing_kernel(
                         lhsT=w1_codes[:, a, 2 * P * s : 2 * P * (s + 1)].bitcast(FP4X4),
                         lhsT_scale=w1_plane[:, a, P * s : P * (s + 1)],
                         rhs=v_codes[a][:, cols].bitcast(FP8X4),
-                        rhs_scale=(v_plane, v_plane_moved)[a][:, cols],
+                        rhs_scale=v_plane[:, a, cols],
                         start=(a == 0),
                         stop=(a == PASSES - 1),
                     )
@@ -163,6 +161,11 @@ def tile_list_canal_week_clearing_kernel(
         second_page = held([P, T2], F32, "bid_page1", tag="tab_w1")
         nc.gpsimd.memset(second_page[:], 0.0)
         bid_pages.append(second_page)
+
+        w4_plane = held([P, N], U8, "w4_plane", tag="w1_plane")
+        nc.gpsimd.memset(w4_plane[:].bitcast(I32), 0)
+        for q in range(QUADS):
+            nc.sync.dma_start(w4_plane[32 * q : 32 * q + 4, :].bitcast(I32), w4_scales[0, 4 * q : 4 * q + 4, :].bitcast(I32))
 
         left_t = held([P, T2 // P, 2, P, 2], BF16, "left_t")
 
@@ -252,7 +255,7 @@ def tile_list_canal_week_clearing_kernel(
                         lhsT=w2_codes[a][:, P * t : P * (t + 1)].bitcast(FP8X4),
                         lhsT_scale=w2_plane[a][:, P * t : P * (t + 1)],
                         rhs=v_codes[a][:, cols].bitcast(FP8X4),
-                        rhs_scale=(v_plane, v_plane_moved)[a][:, cols],
+                        rhs_scale=v_plane[:, a, cols],
                         start=(a == PASSES - 1),
                         stop=(a == 0),
                     )
@@ -314,7 +317,7 @@ def tile_list_canal_week_clearing_kernel(
                 lhsT=w3_codes[:, 0:P].bitcast(FP8X4),
                 lhsT_scale=w3_plane[:, 0:P],
                 rhs=v_codes[0][:, 0:BANK].bitcast(FP8X4),
-                rhs_scale=v_plane[:, 0:BANK],
+                rhs_scale=v_plane[:, 0, 0:BANK],
                 start=True,
                 stop=True,
             )

@@ -96,9 +96,10 @@ def tile_list_canal_week_clearing_kernel(
                 w1_scales[:, 4 * q : 4 * q + 4, :].rearrange("a r c -> r a c").bitcast(I32),
             )
         tab_w.append(load_words(1))
-        w1_codes = held([P, PASSES, 2 * H], U8, "w1_codes")
+        w1_lead = held([P, PASSES, 2 * P], U8, "w1_lead")
+        w1_rest = held([P, PASSES, 2 * (H - P)], U8, "w1_rest")
         w1_rows = w1_words.rearrange("a p n -> p a n")
-        nc.sync.dma_start(w1_codes[:, :, 0 : 2 * P].bitcast(I32), w1_rows[:, :, 0 : 2 * P].bitcast(I32))
+        nc.sync.dma_start(w1_lead[:].bitcast(I32), w1_rows[:, :, 0 : 2 * P].bitcast(I32))
 
         def listed(offsets, j0, j1):
             return offsets[:, j0 // 16 : j1 // 16]
@@ -113,7 +114,7 @@ def tile_list_canal_week_clearing_kernel(
         wg1_sb = held([P, S], F32, "wg1")
         nc.sync.dma_start(bid_at[:], offs2)
         nc.sync.dma_start(wg1_sb[:, 0:LEAD], wg1[:, 0:LEAD])
-        nc.sync.dma_start(w1_codes[:, :, 2 * P :].bitcast(I32), w1_rows[:, :, 2 * P :].bitcast(I32))
+        nc.sync.dma_start(w1_rest[:].bitcast(I32), w1_rows[:, :, 2 * P :].bitcast(I32))
         nc.sync.dma_start(wg1_sb[:, LEAD:S], wg1[:, LEAD:S])
         allot_sb = [load_allot(0)]
         w2_raw = [load_w2(0)]
@@ -131,6 +132,9 @@ def tile_list_canal_week_clearing_kernel(
         for a, j0, j1 in ((0, 0, S), (1, 0, LEAD), (1, LEAD, BANK), (1, BANK, S)):
             nc.vector.tensor_copy(v_codes[a][:, j0:j1].bitcast(U32), tab_w[a][:].bitcast(U32).indirect(listed(pick, j0, j1)))
 
+        def w1_words_of(s, a):
+            return w1_lead[:, a, :] if s == 0 else w1_rest[:, a, 2 * P * (s - 1) : 2 * P * s]
+
         def bid_scores(s, scores, j0, j1, width):
             acc = bank("h1_acc", "h")
             for n0 in range(j0, j1, width):
@@ -138,7 +142,7 @@ def tile_list_canal_week_clearing_kernel(
                 for a in range(PASSES):
                     nc.tensor.matmul_mx(
                         out=acc[:, n0 - j0 : n0 - j0 + width],
-                        lhsT=w1_codes[:, a, 2 * P * s : 2 * P * (s + 1)].bitcast(FP4X4),
+                        lhsT=w1_words_of(s, a).bitcast(FP4X4),
                         lhsT_scale=w1_plane[:, a, P * s : P * (s + 1)],
                         rhs=v_codes[a][:, cols].bitcast(FP8X4),
                         rhs_scale=v_plane[:, a, cols],
@@ -310,88 +314,95 @@ def tile_list_canal_week_clearing_kernel(
                 out=w3_codes[:, n0:n1].bitcast(FP8X4), scales=w3_plane[:, n0:n1], in_=w3_bf[:, PACK * n0 : PACK * n1]
             )
 
-        unread = bank("unread", "h")
-        for n in range(4):
-            nc.tensor.matmul_mx(
-                out=unread[:],
-                lhsT=w3_codes[:, 0:P].bitcast(FP8X4),
-                lhsT_scale=w3_plane[:, 0:P],
-                rhs=v_codes[0][:, 0:BANK].bitcast(FP8X4),
-                rhs_scale=v_plane[:, 0, 0:BANK],
-                start=True,
-                stop=True,
-            )
+        z_codes = [held([P, BANK], U32, "z_codes%d" % c, tag=(None, None, "copied1", "copied2")[c]) for c in range(2)]
+        z_plane = [held([P, BANK], U8, "z_plane%d" % c) for c in range(CHUNKS)]
 
-        def pack(c):
-            z_codes = held([P, BANK], U32, "z_codes%d" % c, tag=(None, None, "copied1", "copied2")[c])
-            z_plane = held([P, BANK], U8, "z_plane%d" % c)
+        def pack(c, m0=0, m1=BANK):
+            if c >= 2:
+                z_codes.append(held([P, BANK], U32, "z_codes%d" % c, tag="copied%d" % (c - 1)))
             nc.vector.quantize_mx(
-                out=z_codes[:].bitcast(FP8X4),
-                scales=z_plane[:],
-                in_=woven[c][:].rearrange("p m t -> p (m t)"),
+                out=z_codes[c][:, m0:m1].bitcast(FP8X4),
+                scales=z_plane[c][:, m0:m1],
+                in_=woven[c][:, m0:m1, :].rearrange("p m t -> p (m t)"),
             )
-            return z_codes, z_plane
 
         result_tags = ("tab_w1", "allot1", "allot0", "allot3")
         results = [held([P, N_TILES, BANK], F32, "result%d" % c, tag=result_tags[c]) for c in range(CHUNKS)]
-
         squash_tags = ("left_t", "wg2_a", "w3_raw", None)
         squashes = [held([P, N_TILES, BANK], F32, "squashed%d" % c, tag=squash_tags[c]) for c in range(CHUNKS)]
 
-        def read_out(c, i, behind=None):
-            z_codes, z_plane = z_packed[c]
-            rows = slice(i * P, (i + 1) * P)
-            bounded = bank("bounded", "h")
+        def bounded_pass(acc, c, i, m0=0, m1=BANK):
             nc.tensor.matmul_mx(
-                out=bounded[:],
-                lhsT=w3_codes[:, rows].bitcast(FP8X4),
-                lhsT_scale=w3_plane[:, rows],
-                rhs=z_codes[:].bitcast(FP8X4),
-                rhs_scale=z_plane[:],
+                out=acc[:, m0:m1],
+                lhsT=w3_codes[:, i * P : (i + 1) * P].bitcast(FP8X4),
+                lhsT_scale=w3_plane[:, i * P : (i + 1) * P],
+                rhs=z_codes[c][:, m0:m1].bitcast(FP8X4),
+                rhs_scale=z_plane[c][:, m0:m1],
                 start=True,
                 stop=True,
             )
-            linear = bank("linear", "d")
+
+        def linear_pass(acc, c, i, m0=0, m1=BANK):
             nc.tensor.matmul_mx(
-                out=linear[:],
+                out=acc[:, m0:m1],
                 lhsT=w4_codes[:, 2 * P * i : 2 * P * (i + 1)].bitcast(FP4X4),
-                lhsT_scale=w4_plane[:, rows],
-                rhs=z_codes[:].bitcast(FP8X4),
-                rhs_scale=z_plane[:],
+                lhsT_scale=w4_plane[:, i * P : (i + 1) * P],
+                rhs=z_codes[c][:, m0:m1].bitcast(FP8X4),
+                rhs_scale=z_plane[c][:, m0:m1],
                 start=True,
                 stop=True,
             )
-            squashed = squashes[c][:, i, :]
-            nc.scalar.activation(squashed, bounded[:], ACT.Tanh)
+
+        def squash(c, i, bounded=None):
+            if bounded is None:
+                bounded = bank("bounded", "h")
+                bounded_pass(bounded, c, i)
+            nc.scalar.activation(squashes[c][:, i, :], bounded[:], ACT.Tanh)
+
+        def read_out(c, i, behind=None, linear=None):
+            if linear is None:
+                linear = bank("linear", "d")
+                linear_pass(linear, c, i)
             if behind is None:
                 result = results[c][:, i, :]
-                nc.vector.tensor_tensor(result, linear[:], squashed, ALU.add)
+                nc.vector.tensor_tensor(result, linear[:], squashes[c][:, i, :], ALU.add)
             else:
                 copied = held([P, BANK], F32, "copied%d" % behind)
                 nc.scalar.copy(copied[:], linear[:])
                 result = held([P, BANK], F32, "late%d" % behind, tag=woven_tags[behind])[:]
-                nc.gpsimd.tensor_tensor(result, copied[:], squashed, ALU.add)
-            nc.sync.dma_start(out[rows, c * BANK : (c + 1) * BANK], result)
+                nc.gpsimd.tensor_tensor(result, copied[:], squashes[c][:, i, :], ALU.add)
+            nc.sync.dma_start(out[i * P : (i + 1) * P, c * BANK : (c + 1) * BANK], result)
 
         round_ask(3)
-        z_packed = []
+        first = [bank("bounded", "h"), bank("linear", "d"), bank("bounded", "h")]
         clear(0)
-        clear(1)
-        clear(2)
-        z_packed.append(pack(0))
+        for piece in range(2):
+            clear(piece + 1)
+            m0, m1 = piece * PIECE, (piece + 1) * PIECE
+            pack(0, m0, m1)
+            bounded_pass(first[0], 0, 0, m0, m1)
+            linear_pass(first[1], 0, 0, m0, m1)
+            bounded_pass(first[2], 0, 1, m0, m1)
         clear(3)
         clear(4)
-        z_packed.append(pack(1))
-        read_out(0, 0, behind=1)
+        pack(1)
+        squash(0, 0, first[0])
+        read_out(0, 0, behind=1, linear=first[1])
+        squash(0, 1, first[2])
+        squash(0, 2)
         clear(5)
         clear(6)
         clear(7)
         read_out(0, 1)
-        z_packed.append(pack(2))
+        squash(1, 0)
+        pack(2)
         read_out(0, 2, behind=2)
-        for i in range(N_TILES):
+        read_out(1, 0)
+        for i in range(1, N_TILES):
+            squash(1, i)
             read_out(1, i)
-        z_packed.append(pack(3))
+        pack(3)
         for c in range(2, CHUNKS):
             for i in range(N_TILES):
+                squash(c, i)
                 read_out(c, i)

@@ -19,19 +19,21 @@ ALU = mybir.AluOpType
 
 P = 128
 PACK = 4
-PASSES = K // (P * PACK)
+PASS_ROWS = P * PACK
+PASSES = K // PASS_ROWS
 BANK = 512
 HALVES = S // BANK
 CHUNKS = T2 // BANK
 BLOCKS = BANK // P
-WIDE = 2 * BANK
 QUADS = 4
 N_TILES = N // P
 LIST_COLS = S // 16
+SCALE_AT = 96
 LEAD = 256
 PIECE = BANK // 2
 PIECES = T2 // PIECE
-BANKED = 5
+PARKED = 5
+SCORE_BANKS, LEFT_BANKS = 3, 5
 
 
 def tile_list_canal_week_clearing_kernel(
@@ -46,8 +48,8 @@ def tile_list_canal_week_clearing_kernel(
         def held(shape, dtype, name, tag=None):
             return sb.tile(shape, dtype, name=name, tag=tag or name, align_bytes=64)
 
-        def bank(name, tag, width=BANK, dtype=F32):
-            return ps.tile([P, width], dtype, name=name, tag=tag, bufs={"h": 3, "d": 5}[tag])
+        def bank(name, tag):
+            return ps.tile([P, BANK], F32, name=name, tag=tag, bufs={"h": SCORE_BANKS, "d": LEFT_BANKS}[tag])
 
         pick = lists.tile([P, LIST_COLS], U16, name="pick")
         bid_at = lists.tile([P, LIST_COLS], U16, name="bid_at")
@@ -56,12 +58,12 @@ def tile_list_canal_week_clearing_kernel(
         tab_plane = held([P, T], U8, "tab_plane")
         w1_plane = held([P, PASSES, H], U8, "w1_plane")
         v_plane = held([P, PASSES, S], U8, "v_plane")
-        nc.vector.memset(tab_plane[0:96, :].bitcast(I32), 0)
         nc.vector.memset(w1_plane[:].rearrange("p a c -> p (a c)").bitcast(I32), 0)
-        nc.vector.memset(v_plane[:].rearrange("p a j -> p (a j)").bitcast(I32), 0)
         ident = held([P, P], F32, "ident")
         nc.vector.memset(ident[:], 0.0)
         make_identity(nc, ident[:], nomemset=True)
+        nc.vector.memset(tab_plane[0:SCALE_AT, :].bitcast(I32), 0)
+        nc.vector.memset(v_plane[:].rearrange("p a j -> p (a j)").bitcast(I32), 0)
         bid_pages = [held([P, T2], F32, "bid_page0")]
         nc.vector.memset(bid_pages[0][:].bitcast(I32), 0)
 
@@ -70,8 +72,8 @@ def tile_list_canal_week_clearing_kernel(
             nc.sync.dma_start(words[:], tab_words[a].rearrange("p t i -> p (t i)").bitcast(I32))
             return words
 
-        def load_wg2(slots, name, tag=None):
-            dst = held([P, len(slots), S], F32, name, tag=tag)
+        def load_wg2(slots, name):
+            dst = held([P, len(slots), S], F32, name)
             rows = wg2.rearrange("(q t) j -> q t j", t=PACK)[:, slots[0] : slots[-1] + 1, :]
             for quad in (0, 2, 1, 3):
                 nc.sync.dma_start(dst[32 * quad : 32 * quad + 32, :, :], rows)
@@ -84,10 +86,10 @@ def tile_list_canal_week_clearing_kernel(
 
         def load_w2(a):
             raw = held([P, PACK, H], F32, "w2_raw%d" % a)
-            nc.sync.dma_start(raw[:], w2[512 * a : 512 * (a + 1), :].rearrange("(p j) c -> p j c", j=PACK))
+            nc.sync.dma_start(raw[:], w2[PASS_ROWS * a : PASS_ROWS * (a + 1), :].rearrange("(p j) c -> p j c", j=PACK))
             return raw
 
-        nc.sync.dma_start(tab_plane[96:P, :].bitcast(I32), tab_scales.rearrange("a q t -> q a t").bitcast(I32))
+        nc.sync.dma_start(tab_plane[SCALE_AT:P, :].bitcast(I32), tab_scales.rearrange("a q t -> q a t").bitcast(I32))
         nc.sync.dma_start(pick[:], offs)
         tab_w = [load_words(0)]
         for q in range(QUADS):
@@ -107,9 +109,8 @@ def tile_list_canal_week_clearing_kernel(
         picked_plane = held([P, S], U8, "picked_plane")
         nc.vector.tensor_copy(picked_plane[:], tab_plane[:].indirect(pick[:]))
         for q in range(QUADS):
-            nc.sync.dma_start(
-                v_plane[32 * q : 32 * q + 4, :, :].bitcast(I32), picked_plane[96 + 8 * q : 104 + 8 * q, :].bitcast(I32)
-            )
+            rows = picked_plane[SCALE_AT + 8 * q : SCALE_AT + 8 * (q + 1), :]
+            nc.sync.dma_start(v_plane[32 * q : 32 * q + 4, :, :].bitcast(I32), rows.bitcast(I32))
 
         wg1_sb = held([P, S], F32, "wg1")
         nc.sync.dma_start(bid_at[:], offs2)
@@ -120,11 +121,11 @@ def tile_list_canal_week_clearing_kernel(
         w2_raw = [load_w2(0)]
         allot_sb.append(load_allot(1))
         w2_raw.append(load_w2(1))
-        w3_raw = held([P, PACK, N], F32, "w3_raw")
-        nc.sync.dma_start(w3_raw[:], w3.rearrange("(p j) n -> p j n", j=PACK))
         allot_sb = allot_sb + [load_allot(2), load_allot(3)]
         nc.sync.dma_start(ask_at[:], offs3)
         wg2_sb = load_wg2([0, 1, 2], "wg2_a") + load_wg2([3], "wg2_b")
+        w3_raw = held([P, PACK, N], F32, "w3_raw")
+        nc.sync.dma_start(w3_raw[:], w3.rearrange("(p j) n -> p j n", j=PACK))
         w4_codes = held([P, 2 * N], U8, "w4_codes")
         nc.sync.dma_start(w4_codes[:].bitcast(I32), w4_words[0].bitcast(I32))
 
@@ -205,7 +206,7 @@ def tile_list_canal_week_clearing_kernel(
                 )
 
         left_tags = ["w2_raw0", "w2_raw1", "w2_bf0"]
-        left_sb = [held([P, BANK, 2], F32, "left%d" % c, tag=left_tags[c]) for c in range(3)]
+        left_sb = [held([P, BANK, 2], F32, "left%d" % c, tag=tag) for c, tag in enumerate(left_tags)]
 
         def turn_back(piece):
             acc = bank("left", "d")
@@ -213,7 +214,7 @@ def tile_list_canal_week_clearing_kernel(
                 for i in range(2):
                     words = left_t[:, 2 * piece + i, u, :, :].rearrange("m p e -> m (p e)").bitcast(F32)
                     nc.tensor.transpose(acc[:, (2 * u + i) * P : (2 * u + i + 1) * P], words, ident[:])
-            if piece >= BANKED:
+            if piece >= PARKED:
                 return acc[:].bitcast(BF16).rearrange("p (u m e) -> p m u e", u=2, e=2)
             m0 = piece % 2 * PIECE
             parked = left_sb[piece // 2][:, m0 : m0 + PIECE, :]
@@ -231,11 +232,6 @@ def tile_list_canal_week_clearing_kernel(
                 w2_raw[a][:].rearrange("p j (m t) -> p m t j", t=PACK),
             )
             w2_bf.append(rounded)
-        w3_bf = held([P, PACK * N], BF16, "w3_bf")
-        nc.scalar.copy(
-            w3_bf[:].rearrange("p (g i j) -> p g j i", i=4, j=PACK),
-            w3_raw[:].rearrange("p j (g i) -> p g j i", i=4),
-        )
         take_off(0)
         place_bid(2)
         take_off(1)
@@ -270,9 +266,8 @@ def tile_list_canal_week_clearing_kernel(
         take_off(2)
         take_off(3)
 
-        ask_pages = [held([P, T2], F32, "ask_page0", tag="allot0"), held([P, T2], F32, "ask_page1", tag="h1_0")]
-        ask_pages.append(held([P, T2], F32, "ask_page2", tag="h1_1"))
-        ask_pages.append(held([P, T2], F32, "ask_page3", tag="allot2"))
+        ask_tags = ["allot0", "h1_0", "h1_1", "allot2"]
+        ask_pages = [held([P, T2], F32, "ask_page%d" % t, tag=tag) for t, tag in enumerate(ask_tags)]
         for page in ask_pages:
             nc.gpsimd.memset(page[:], 0.0)
 
@@ -301,6 +296,11 @@ def tile_list_canal_week_clearing_kernel(
         place_ask(0)
         round_ask(0)
         place_ask(1)
+        w3_bf = held([P, PACK * N], BF16, "w3_bf")
+        nc.scalar.copy(
+            w3_bf[:].rearrange("p (g i j) -> p g j i", i=4, j=PACK),
+            w3_raw[:].rearrange("p j (g i) -> p g j i", i=4),
+        )
         left = [turn_back(piece) for piece in range(PIECES)]
         round_ask(1)
         place_ask(2)
@@ -314,11 +314,11 @@ def tile_list_canal_week_clearing_kernel(
                 out=w3_codes[:, n0:n1].bitcast(FP8X4), scales=w3_plane[:, n0:n1], in_=w3_bf[:, PACK * n0 : PACK * n1]
             )
 
-        z_codes = [held([P, BANK], U32, "z_codes%d" % c, tag=(None, None, "copied1", "copied2")[c]) for c in range(2)]
+        z_codes = [held([P, BANK], U32, "z_codes%d" % c) for c in range(2)]
         z_plane = [held([P, BANK], U8, "z_plane%d" % c) for c in range(CHUNKS)]
 
         def pack(c, m0=0, m1=BANK):
-            if c >= 2:
+            if c >= len(z_codes):
                 z_codes.append(held([P, BANK], U32, "z_codes%d" % c, tag="copied%d" % (c - 1)))
             nc.vector.quantize_mx(
                 out=z_codes[c][:, m0:m1].bitcast(FP8X4),
@@ -390,9 +390,8 @@ def tile_list_canal_week_clearing_kernel(
         read_out(0, 0, behind=1, linear=first[1])
         squash(0, 1, first[2])
         squash(0, 2)
-        clear(5)
-        clear(6)
-        clear(7)
+        for piece in range(PARKED, PIECES):
+            clear(piece)
         read_out(0, 1)
         squash(1, 0)
         pack(2)

@@ -55,17 +55,21 @@ def tile_list_canal_week_clearing_kernel(
         bid_at = lists.tile([P, LIST_COLS], U16, name="bid_at")
         ask_at = lists.tile([P, LIST_COLS], U16, name="ask_at")
 
-        tab_plane = held([P, T], U8, "tab_plane")
-        w1_plane = held([P, PASSES, H], U8, "w1_plane")
-        v_plane = held([P, PASSES, S], U8, "v_plane")
-        nc.vector.memset(w1_plane[:].rearrange("p a c -> p (a c)").bitcast(I32), 0)
-        ident = held([P, P], F32, "ident")
-        nc.vector.memset(ident[:], 0.0)
-        make_identity(nc, ident[:], nomemset=True)
-        nc.vector.memset(tab_plane[0:SCALE_AT, :].bitcast(I32), 0)
-        nc.vector.memset(v_plane[:].rearrange("p a j -> p (a j)").bitcast(I32), 0)
         bid_pages = [held([P, T2], F32, "bid_page0")]
-        nc.vector.memset(bid_pages[0][:].bitcast(I32), 0)
+        nc.gpsimd.memset(bid_pages[0][:], 0.0)
+        tab_padded = held([P, T + 4], U8, "tab_plane")
+        w1_padded = held([P, PASSES * H + 4], U8, "w1_plane")
+        v_padded = held([P, PASSES * S + 4], U8, "v_plane")
+        ident_padded = held([P, P + 1], F32, "ident")
+        nc.vector.memset(w1_padded[:].bitcast(I32), 0)
+        nc.vector.memset(tab_padded[0:SCALE_AT, :].bitcast(I32), 0)
+        nc.vector.memset(ident_padded[:], 0.0)
+        nc.vector.memset(v_padded[:].bitcast(I32), 0)
+        tab_plane = tab_padded[:, 0:T]
+        w1_plane = w1_padded[:, 0 : PASSES * H].rearrange("p (a c) -> p a c", a=PASSES)
+        v_plane = v_padded[:, 0 : PASSES * S].rearrange("p (a j) -> p a j", a=PASSES)
+        ident = ident_padded[:, 0:P]
+        make_identity(nc, ident, nomemset=True)
 
         def load_words(a):
             words = held([P, T], I32, "tab_w%d" % a)
@@ -107,7 +111,7 @@ def tile_list_canal_week_clearing_kernel(
             return offsets[:, j0 // 16 : j1 // 16]
 
         picked_plane = held([P, S], U8, "picked_plane")
-        nc.vector.tensor_copy(picked_plane[:], tab_plane[:].indirect(pick[:]))
+        nc.vector.tensor_copy(picked_plane[:], tab_plane.indirect(pick[:]))
         for q in range(QUADS):
             rows = picked_plane[SCALE_AT + 8 * q : SCALE_AT + 8 * (q + 1), :]
             nc.sync.dma_start(v_plane[32 * q : 32 * q + 4, :, :].bitcast(I32), rows.bitcast(I32))
@@ -194,7 +198,7 @@ def tile_list_canal_week_clearing_kernel(
                         nc.tensor.matmul(
                             acc[:, i * P : (i + 1) * P],
                             source[:, m0 : m0 + P],
-                            ident[:],
+                            ident,
                             start=(n_src == 0 and i == 0),
                             stop=(n_src == 1 and i == BLOCKS - 1),
                             is_transpose=True,
@@ -213,7 +217,7 @@ def tile_list_canal_week_clearing_kernel(
             for u in range(2):
                 for i in range(2):
                     words = left_t[:, 2 * piece + i, u, :, :].rearrange("m p e -> m (p e)").bitcast(F32)
-                    nc.tensor.transpose(acc[:, (2 * u + i) * P : (2 * u + i + 1) * P], words, ident[:])
+                    nc.tensor.transpose(acc[:, (2 * u + i) * P : (2 * u + i + 1) * P], words, ident)
             if piece >= PARKED:
                 return acc[:].bitcast(BF16).rearrange("p (u m e) -> p m u e", u=2, e=2)
             m0 = piece % 2 * PIECE
@@ -266,13 +270,13 @@ def tile_list_canal_week_clearing_kernel(
         take_off(2)
         take_off(3)
 
-        ask_tags = ["allot0", "h1_0", "h1_1", "allot2"]
+        ask_tags = ["h1_%d" % t for t in range(PACK)]
         ask_pages = [held([P, T2], F32, "ask_page%d" % t, tag=tag) for t, tag in enumerate(ask_tags)]
         for page in ask_pages:
             nc.gpsimd.memset(page[:], 0.0)
 
         floor = [held([P, 2, PIECE, 2], BF16, "floor%d" % piece) for piece in range(PIECES)]
-        woven_tags = ["tab_w0", "wg1", "h1_2", "h1_3"]
+        woven_tags = ["tab_w0", "wg1", "allot2", "h2_1"]
         woven = [held([P, BANK, PACK], BF16, "woven%d" % c, tag=woven_tags[c]) for c in range(CHUNKS)]
 
         def place_ask(t):

@@ -95,13 +95,17 @@ def tile_list_canal_week_clearing_kernel(
 
         nc.sync.dma_start(tab_plane[SCALE_AT:P, :].bitcast(I32), tab_scales.rearrange("a q t -> q a t").bitcast(I32))
         nc.sync.dma_start(pick[:], offs)
+
+        def load_w1_scales(r):
+            rows = w1_scales.rearrange("a (q r) c -> r q a c", r=4)[r]
+            nc.sync.dma_start(w1_plane[r:P:32, :, :].bitcast(I32), rows.bitcast(I32))
+
         tab_w = [load_words(0)]
-        for q in range(QUADS):
-            nc.sync.dma_start(
-                w1_plane[32 * q : 32 * q + 4, :, :].bitcast(I32),
-                w1_scales[:, 4 * q : 4 * q + 4, :].rearrange("a r c -> r a c").bitcast(I32),
-            )
+        load_w1_scales(0)
+        load_w1_scales(1)
         tab_w.append(load_words(1))
+        load_w1_scales(2)
+        load_w1_scales(3)
         w1_lead = held([P, PASSES, 2 * P], U8, "w1_lead")
         w1_rest = held([P, PASSES, 2 * (H - P)], U8, "w1_rest")
         w1_rows = w1_words.rearrange("a p n -> p a n")
@@ -112,7 +116,7 @@ def tile_list_canal_week_clearing_kernel(
 
         picked_plane = held([P, S], U8, "picked_plane")
         nc.vector.tensor_copy(picked_plane[:], tab_plane.indirect(pick[:]))
-        for q in range(QUADS):
+        for q in (0, 2, 1, 3):
             rows = picked_plane[SCALE_AT + 8 * q : SCALE_AT + 8 * (q + 1), :]
             nc.sync.dma_start(v_plane[32 * q : 32 * q + 4, :, :].bitcast(I32), rows.bitcast(I32))
 
@@ -121,11 +125,10 @@ def tile_list_canal_week_clearing_kernel(
         nc.sync.dma_start(wg1_sb[:, 0:LEAD], wg1[:, 0:LEAD])
         nc.sync.dma_start(w1_rest[:].bitcast(I32), w1_rows[:, :, 2 * P :].bitcast(I32))
         nc.sync.dma_start(wg1_sb[:, LEAD:S], wg1[:, LEAD:S])
-        allot_sb = [load_allot(0)]
         w2_raw = [load_w2(0)]
-        allot_sb.append(load_allot(1))
+        allot_sb = [load_allot(0)]
         w2_raw.append(load_w2(1))
-        allot_sb = allot_sb + [load_allot(2), load_allot(3)]
+        allot_sb = allot_sb + [load_allot(s) for s in range(1, PACK)]
         nc.sync.dma_start(ask_at[:], offs3)
         wg2_sb = load_wg2([0, 1, 2], "wg2_a") + load_wg2([3], "wg2_b")
         w3_raw = held([P, PACK, N], F32, "w3_raw")

@@ -1,7 +1,6 @@
 from contextlib import ExitStack
 
 import concourse.mybir as mybir
-from concourse.masks import make_identity
 
 K, T, S, T2, H, N = 1024, 2048, 1024, 2048, 512, 384
 FLOPS = 2 * (2 * K * H * S + 2 * H * N * T2)
@@ -55,21 +54,21 @@ def tile_list_canal_week_clearing_kernel(
         bid_at = lists.tile([P, LIST_COLS], U16, name="bid_at")
         ask_at = lists.tile([P, LIST_COLS], U16, name="ask_at")
 
+        tab_plane = held([P, T], U8, "tab_plane")
+        w1_plane = held([P, PASSES, H], U8, "w1_plane")
+        v_plane = held([P, PASSES, S], U8, "v_plane")
+        nc.vector.memset(w1_plane[:].rearrange("p a c -> p (a c)").bitcast(I32), 0)
+        nc.vector.memset(tab_plane[0:SCALE_AT, :].bitcast(I32), 0)
+        nc.vector.memset(v_plane[:].rearrange("p a j -> p (a j)").bitcast(I32), 0)
         bid_pages = [held([P, T2], F32, "bid_page0")]
-        nc.gpsimd.memset(bid_pages[0][:], 0.0)
-        tab_padded = held([P, T + 4], U8, "tab_plane")
-        w1_padded = held([P, PASSES * H + 4], U8, "w1_plane")
-        v_padded = held([P, PASSES * S + 4], U8, "v_plane")
-        ident_padded = held([P, P + 1], F32, "ident")
-        nc.vector.memset(w1_padded[:].bitcast(I32), 0)
-        nc.vector.memset(tab_padded[0:SCALE_AT, :].bitcast(I32), 0)
-        nc.vector.memset(ident_padded[:], 0.0)
-        nc.vector.memset(v_padded[:].bitcast(I32), 0)
-        tab_plane = tab_padded[:, 0:T]
-        w1_plane = w1_padded[:, 0 : PASSES * H].rearrange("p (a c) -> p a c", a=PASSES)
-        v_plane = v_padded[:, 0 : PASSES * S].rearrange("p (a j) -> p a j", a=PASSES)
-        ident = ident_padded[:, 0:P]
-        make_identity(nc, ident, nomemset=True)
+        nc.vector.memset(bid_pages[0][:].bitcast(I32), 0)
+
+        offset = held([P, P], F32, "offset")
+        distance = held([P, P], F32, "distance")
+        ident = held([P, P], F32, "ident")[:]
+        nc.gpsimd.iota(offset[:], [[1, P]], base=0, channel_multiplier=-1, allow_small_or_imprecise_dtypes=True)
+        nc.scalar.activation(distance[:], offset[:], ACT.Abs)
+        nc.scalar.activation(ident, distance[:], ACT.Relu, bias=1.0, scale=-1.0)
 
         def load_words(a):
             words = held([P, T], I32, "tab_w%d" % a)
@@ -115,7 +114,7 @@ def tile_list_canal_week_clearing_kernel(
             return offsets[:, j0 // 16 : j1 // 16]
 
         picked_plane = held([P, S], U8, "picked_plane")
-        nc.vector.tensor_copy(picked_plane[:], tab_plane.indirect(pick[:]))
+        nc.vector.tensor_copy(picked_plane[:], tab_plane[:].indirect(pick[:]))
         for q in (0, 2, 1, 3):
             rows = picked_plane[SCALE_AT + 8 * q : SCALE_AT + 8 * (q + 1), :]
             nc.sync.dma_start(v_plane[32 * q : 32 * q + 4, :, :].bitcast(I32), rows.bitcast(I32))

@@ -56,10 +56,10 @@ def tile_list_canal_week_clearing_kernel(
 
         tab_plane = held([P, T], U8, "tab_plane")
         w1_plane = held([P, PASSES, H], U8, "w1_plane")
-        v_plane = held([P, PASSES, S], U8, "v_plane")
+        v_plane = held([P, HALVES, PASSES, BANK], U8, "v_plane")
         nc.vector.memset(w1_plane[:].rearrange("p a c -> p (a c)").bitcast(I32), 0)
         nc.vector.memset(tab_plane[0:SCALE_AT, :].bitcast(I32), 0)
-        nc.vector.memset(v_plane[:].rearrange("p a j -> p (a j)").bitcast(I32), 0)
+        nc.vector.memset(v_plane[:].rearrange("p h a j -> p (h a j)").bitcast(I32), 0)
         bid_pages = [held([P, T2], F32, "bid_page0")]
         nc.vector.memset(bid_pages[0][:].bitcast(I32), 0)
 
@@ -100,6 +100,7 @@ def tile_list_canal_week_clearing_kernel(
             nc.sync.dma_start(w1_plane[r:P:32, :, :].bitcast(I32), rows.bitcast(I32))
 
         tab_w = [load_words(0)]
+        nc.sync.dma_start(bid_at[:], offs2)
         load_w1_scales(0)
         load_w1_scales(1)
         tab_w.append(load_words(1))
@@ -115,15 +116,23 @@ def tile_list_canal_week_clearing_kernel(
 
         picked_plane = held([P, S], U8, "picked_plane")
         nc.vector.tensor_copy(picked_plane[:], tab_plane[:].indirect(pick[:]))
-        for q in (0, 2, 1, 3):
-            rows = picked_plane[SCALE_AT + 8 * q : SCALE_AT + 8 * (q + 1), :]
-            nc.sync.dma_start(v_plane[32 * q : 32 * q + 4, :, :].bitcast(I32), rows.bitcast(I32))
+
+        def move_scales(half):
+            for q in (0, 2, 1, 3):
+                rows = picked_plane[SCALE_AT + 8 * q : SCALE_AT + 8 * (q + 1), half * BANK : (half + 1) * BANK]
+                nc.sync.dma_start(v_plane[32 * q : 32 * q + 4, half, :, :].bitcast(I32), rows.bitcast(I32))
+
+        def v_scales(a, j0, j1):
+            half = j0 // BANK
+            return v_plane[:, half, a, j0 - half * BANK : j1 - half * BANK]
+
+        move_scales(0)
 
         wg1_sb = held([P, S], F32, "wg1")
-        nc.sync.dma_start(bid_at[:], offs2)
         nc.sync.dma_start(wg1_sb[:, 0:LEAD], wg1[:, 0:LEAD])
-        nc.sync.dma_start(w1_rest[:].bitcast(I32), w1_rows[:, :, 2 * P :].bitcast(I32))
+        move_scales(1)
         nc.sync.dma_start(wg1_sb[:, LEAD:S], wg1[:, LEAD:S])
+        nc.sync.dma_start(w1_rest[:].bitcast(I32), w1_rows[:, :, 2 * P :].bitcast(I32))
         w2_raw = [load_w2(0)]
         allot_sb = [load_allot(0)]
         w2_raw.append(load_w2(1))
@@ -152,7 +161,7 @@ def tile_list_canal_week_clearing_kernel(
                         lhsT=w1_words_of(s, a).bitcast(FP4X4),
                         lhsT_scale=w1_plane[:, a, P * s : P * (s + 1)],
                         rhs=v_codes[a][:, cols].bitcast(FP8X4),
-                        rhs_scale=v_plane[:, a, cols],
+                        rhs_scale=v_scales(a, cols.start, cols.stop),
                         start=(a == 0),
                         stop=(a == PASSES - 1),
                     )
@@ -162,7 +171,8 @@ def tile_list_canal_week_clearing_kernel(
         for s in range(PACK):
             scores = held([P, S], F32, "h1_%d" % s)
             if s == 0:
-                bid_scores(s, scores, 0, LEAD, P)
+                for j0 in range(0, LEAD, P):
+                    bid_scores(s, scores, j0, j0 + P, P)
                 bid_scores(s, scores, LEAD, BANK, P)
             else:
                 bid_scores(s, scores, 0, BANK, BANK)
@@ -261,7 +271,7 @@ def tile_list_canal_week_clearing_kernel(
                         lhsT=w2_codes[a][:, P * t : P * (t + 1)].bitcast(FP8X4),
                         lhsT_scale=w2_plane[a][:, P * t : P * (t + 1)],
                         rhs=v_codes[a][:, cols].bitcast(FP8X4),
-                        rhs_scale=v_plane[:, a, cols],
+                        rhs_scale=v_scales(a, cols.start, cols.stop),
                         start=(a == PASSES - 1),
                         stop=(a == 0),
                     )

@@ -106,10 +106,10 @@ def tile_list_canal_week_clearing_kernel(
         tab_w.append(load_words(1))
         load_w1_scales(2)
         load_w1_scales(3)
-        w1_lead = held([P, PASSES, 2 * P], U8, "w1_lead")
-        w1_rest = held([P, PASSES, 2 * (H - P)], U8, "w1_rest")
+        w1_lead = held([P, PASSES, 4 * P], U8, "w1_lead")
+        w1_rest = held([P, PASSES, 2 * H - 4 * P], U8, "w1_rest")
         w1_rows = w1_words.rearrange("a p n -> p a n")
-        nc.sync.dma_start(w1_lead[:].bitcast(I32), w1_rows[:, :, 0 : 2 * P].bitcast(I32))
+        nc.sync.dma_start(w1_lead[:].bitcast(I32), w1_rows[:, :, 0 : 4 * P].bitcast(I32))
 
         def listed(offsets, j0, j1):
             return offsets[:, j0 // 16 : j1 // 16]
@@ -130,9 +130,10 @@ def tile_list_canal_week_clearing_kernel(
 
         wg1_sb = held([P, S], F32, "wg1")
         nc.sync.dma_start(wg1_sb[:, 0:LEAD], wg1[:, 0:LEAD])
+        nc.sync.dma_start(wg1_sb[:, LEAD:BANK], wg1[:, LEAD:BANK])
         move_scales(1)
-        nc.sync.dma_start(wg1_sb[:, LEAD:S], wg1[:, LEAD:S])
-        nc.sync.dma_start(w1_rest[:].bitcast(I32), w1_rows[:, :, 2 * P :].bitcast(I32))
+        nc.sync.dma_start(wg1_sb[:, BANK:S], wg1[:, BANK:S])
+        nc.sync.dma_start(w1_rest[:].bitcast(I32), w1_rows[:, :, 4 * P :].bitcast(I32))
         w2_raw = [load_w2(0)]
         allot_sb = [load_allot(0)]
         w2_raw.append(load_w2(1))
@@ -149,7 +150,7 @@ def tile_list_canal_week_clearing_kernel(
             nc.vector.tensor_copy(v_codes[a][:, j0:j1].bitcast(U32), tab_w[a][:].bitcast(U32).indirect(listed(pick, j0, j1)))
 
         def w1_words_of(s, a):
-            return w1_lead[:, a, :] if s == 0 else w1_rest[:, a, 2 * P * (s - 1) : 2 * P * s]
+            return (w1_lead, w1_rest)[s // 2][:, a, 2 * P * (s % 2) : 2 * P * (s % 2 + 1)]
 
         def bid_scores(s, scores, j0, j1, width):
             acc = bank("h1_acc", "h")
@@ -167,19 +168,17 @@ def tile_list_canal_week_clearing_kernel(
                     )
             nc.scalar.activation(scores[:, j0:j1], acc[:, 0 : j1 - j0], ACT.Copy, scale=-1.0)
 
-        h1 = []
+        h1 = [held([P, S], F32, "h1_%d" % s) for s in range(PACK)]
+        for j0 in range(0, LEAD, P):
+            bid_scores(0, h1[0], j0, j0 + P, P)
+        bid_scores(1, h1[1], 0, BANK, BANK)
+        bid_scores(0, h1[0], LEAD, BANK, BANK - LEAD)
         for s in range(PACK):
-            scores = held([P, S], F32, "h1_%d" % s)
-            if s == 0:
-                for j0 in range(0, LEAD, P):
-                    bid_scores(s, scores, j0, j0 + P, P)
-                bid_scores(s, scores, LEAD, BANK, P)
-            else:
-                bid_scores(s, scores, 0, BANK, BANK)
-            bid_scores(s, scores, BANK, S, BANK)
-            h1.append(scores)
+            if s > 1:
+                bid_scores(s, h1[s], 0, BANK, BANK)
+            bid_scores(s, h1[s], BANK, S, BANK)
 
-        second_page = held([P, T2], F32, "bid_page1", tag="tab_w1")
+        second_page = held([P, T2], F32, "bid_page1", tag="tab_plane")
         nc.gpsimd.memset(second_page[:], 0.0)
         bid_pages.append(second_page)
 
@@ -190,15 +189,9 @@ def tile_list_canal_week_clearing_kernel(
 
         left_t = held([P, T2 // P, 2, P, 2], BF16, "left_t")
 
-        def place_bid(s):
+        def place_bid(s, j0=0, j1=S):
             page = bid_pages[s % 2]
-            if s == 0:
-                for j0, j1 in ((0, LEAD), (LEAD, S)):
-                    nc.vector.tensor_tensor(
-                        page[:].indirect(listed(bid_at, j0, j1)), h1[s][:, j0:j1], wg1_sb[:, j0:j1], ALU.mult
-                    )
-            else:
-                nc.vector.tensor_tensor(page[:].indirect(bid_at[:]), h1[s][:], wg1_sb[:], ALU.mult)
+            nc.vector.tensor_tensor(page[:].indirect(listed(bid_at, j0, j1)), h1[s][:, j0:j1], wg1_sb[:, j0:j1], ALU.mult)
 
         def take_off(s):
             page = bid_pages[s % 2]
@@ -237,8 +230,10 @@ def tile_list_canal_week_clearing_kernel(
             nc.scalar.copy(parked, acc[:].rearrange("p (u m) -> p m u", u=2))
             return parked.rearrange("p m u -> p (m u)").bitcast(BF16).rearrange("p (m u e) -> p m u e", u=2, e=2)
 
-        place_bid(0)
-        place_bid(1)
+        place_bid(0, 0, LEAD)
+        place_bid(1, 0, BANK)
+        place_bid(0, LEAD, S)
+        place_bid(1, BANK, S)
 
         w2_bf = []
         for a in range(PASSES):

@@ -60,8 +60,6 @@ def tile_list_canal_week_clearing_kernel(
         nc.vector.memset(w1_plane[:].rearrange("p a c -> p (a c)").bitcast(I32), 0)
         nc.vector.memset(tab_plane[0:SCALE_AT, :].bitcast(I32), 0)
         nc.vector.memset(v_plane[:].rearrange("p h a j -> p (h a j)").bitcast(I32), 0)
-        bid_pages = [held([P, T2], F32, "bid_page0")]
-        nc.vector.memset(bid_pages[0][:].bitcast(I32), 0)
 
         offset = held([P, P], F32, "offset")
         distance = held([P, P], F32, "distance")
@@ -69,6 +67,9 @@ def tile_list_canal_week_clearing_kernel(
         nc.gpsimd.iota(offset[:], [[1, P]], base=0, channel_multiplier=-1, allow_small_or_imprecise_dtypes=True)
         nc.scalar.activation(distance[:], offset[:], ACT.Abs)
         nc.scalar.activation(ident, distance[:], ACT.Relu, bias=1.0, scale=-1.0)
+
+        bid_pages = [held([P, T2], F32, "bid_page0", tag="offset")]
+        nc.gpsimd.memset(bid_pages[0][:], 0.0)
 
         def load_words(a):
             words = held([P, T], I32, "tab_w%d" % a)
@@ -289,18 +290,17 @@ def tile_list_canal_week_clearing_kernel(
         def place_ask(t):
             nc.vector.tensor_tensor(ask_pages[t][:].indirect(ask_at[:]), h2[t][:], wg2_sb[t], ALU.mult)
 
-        def round_ask(t):
-            for piece in range(PIECES):
-                nc.scalar.copy(
-                    floor[piece][:, t // 2, :, t % 2], ask_pages[t][:, piece * PIECE : (piece + 1) * PIECE]
-                )
+        def round_ask(t, first=PIECE):
+            for m0, m1 in [(m, m + first) for m in range(0, PIECE, first)] + [(m, m + PIECE) for m in range(PIECE, T2, PIECE)]:
+                piece, at = divmod(m0, PIECE)
+                nc.scalar.copy(floor[piece][:, t // 2, at : at + m1 - m0, t % 2], ask_pages[t][:, m0:m1])
 
-        def clear(piece):
-            m0 = piece % 2 * PIECE
+        def clear(piece, m0=0, m1=PIECE):
+            at = piece % 2 * PIECE
             nc.vector.tensor_tensor(
-                woven[piece // 2][:, m0 : m0 + PIECE, :].rearrange("p m (u e) -> p m u e", u=2),
-                left[piece],
-                floor[piece][:].rearrange("p u m e -> p m u e"),
+                woven[piece // 2][:, at + m0 : at + m1, :].rearrange("p m (u e) -> p m u e", u=2),
+                left[piece][:, m0:m1],
+                floor[piece][:, :, m0:m1, :].rearrange("p u m e -> p m u e"),
                 ALU.max,
             )
 
@@ -384,9 +384,10 @@ def tile_list_canal_week_clearing_kernel(
                 nc.gpsimd.tensor_tensor(result, copied[:], squashes[c][:, i, :], ALU.add)
             nc.sync.dma_start(out[i * P : (i + 1) * P, c * BANK : (c + 1) * BANK], result)
 
-        round_ask(3)
+        round_ask(3, first=P)
         first = [bank("bounded", "h"), bank("linear", "d"), bank("bounded", "h")]
-        clear(0)
+        clear(0, 0, P)
+        clear(0, P, PIECE)
         for piece in range(2):
             clear(piece + 1)
             m0, m1 = piece * PIECE, (piece + 1) * PIECE

@@ -17,22 +17,19 @@ ACT = mybir.ActivationFunctionType
 ALU = mybir.AluOpType
 
 P = 128
-PACK = 4
-PASS_ROWS = P * PACK
-PASSES = K // PASS_ROWS
+SLOTS = 4
+PASSES = K // (P * SLOTS)
 BANK = 512
-HALVES = S // BANK
+PIECE = BANK // 2
 CHUNKS = T2 // BANK
-BLOCKS = BANK // P
-QUADS = 4
+PIECES = T2 // PIECE
 N_TILES = N // P
-LIST_COLS = S // 16
 SCALE_AT = 96
 LEAD = 256
-PIECE = BANK // 2
-PIECES = T2 // PIECE
-PARKED = 5
-SCORE_BANKS, LEFT_BANKS = 3, 5
+ASK_ORDER = (2, 0, 1, 3)
+PARKED = (0, 1, 2, 3, 4, 5)
+ROUNDED_ASIDE = ()
+W3_AT = 2
 
 
 def tile_list_canal_week_clearing_kernel(
@@ -42,23 +39,38 @@ def tile_list_canal_week_clearing_kernel(
     with ExitStack() as ctx:
         lists = ctx.enter_context(tc.tile_pool(name="lists", bufs=1))
         sb = ctx.enter_context(tc.tile_pool(name="sb", bufs=1))
-        ps = ctx.enter_context(tc.psum_pool(name="ps", bufs=2))
+        ps = ctx.enter_context(tc.psum_pool(name="ps", bufs=1))
 
         def held(shape, dtype, name, tag=None):
             return sb.tile(shape, dtype, name=name, tag=tag or name, align_bytes=64)
 
-        def bank(name, tag):
-            return ps.tile([P, BANK], F32, name=name, tag=tag, bufs={"h": SCORE_BANKS, "d": LEFT_BANKS}[tag])
+        def bank(name, ring):
+            return ps.tile([P, BANK], F32, name=name, tag=ring, bufs={"three": 3, "five": 5}[ring])
 
-        pick = lists.tile([P, LIST_COLS], U16, name="pick")
-        bid_at = lists.tile([P, LIST_COLS], U16, name="bid_at")
-        ask_at = lists.tile([P, LIST_COLS], U16, name="ask_at")
+        def product(acc, lhs, lhs_scale, rhs, rhs_scale, start=True, stop=True):
+            nc.tensor.matmul_mx(out=acc, lhsT=lhs, lhsT_scale=lhs_scale, rhs=rhs, rhs_scale=rhs_scale, start=start, stop=stop)
 
-        tab_plane = held([P, T], U8, "tab_plane")
+        def quantise(codes, plane, values):
+            nc.vector.quantize_mx(out=codes.bitcast(FP8X4), scales=plane, in_=values)
+
+        def load(dst, src):
+            nc.sync.dma_start(dst, src)
+
+        def load_bytes(dst, src):
+            nc.sync.dma_start(dst.bitcast(I32), src.bitcast(I32))
+
+        def entries(offsets, j0, j1):
+            return offsets[:, j0 // 16 : j1 // 16]
+
+        pick = lists.tile([P, S // 16], U16, name="pick")
+        bid_at = lists.tile([P, S // 16], U16, name="bid_at")
+        ask_at = lists.tile([P, S // 16], U16, name="ask_at")
+
+        tab_rows = held([P, T], U8, "tab_rows")
         w1_plane = held([P, PASSES, H], U8, "w1_plane")
-        v_plane = held([P, HALVES, PASSES, BANK], U8, "v_plane")
+        v_plane = held([P, S // BANK, PASSES, BANK], U8, "v_plane")
         nc.vector.memset(w1_plane[:].rearrange("p a c -> p (a c)").bitcast(I32), 0)
-        nc.vector.memset(tab_plane[0:SCALE_AT, :].bitcast(I32), 0)
+        nc.vector.memset(tab_rows[0:SCALE_AT, :].bitcast(I32), 0)
         nc.vector.memset(v_plane[:].rearrange("p h a j -> p (h a j)").bitcast(I32), 0)
 
         offset = held([P, P], F32, "offset")
@@ -68,232 +80,205 @@ def tile_list_canal_week_clearing_kernel(
         nc.scalar.activation(distance[:], offset[:], ACT.Abs)
         nc.scalar.activation(ident, distance[:], ACT.Relu, bias=1.0, scale=-1.0)
 
-        bid_pages = [held([P, T2], F32, "bid_page0", tag="offset")]
-        nc.gpsimd.memset(bid_pages[0][:], 0.0)
+        def zero_page(name, tag):
+            page = held([P, T2], F32, name, tag=tag)
+            nc.gpsimd.memset(page[:], 0.0)
+            return page
 
-        def load_words(a):
-            words = held([P, T], I32, "tab_w%d" % a)
-            nc.sync.dma_start(words[:], tab_words[a].rearrange("p t i -> p (t i)").bitcast(I32))
-            return words
+        bid_pages = [zero_page("bid_page0", "offset")]
 
-        def load_wg2(slots, name):
-            dst = held([P, len(slots), S], F32, name)
-            rows = wg2.rearrange("(q t) j -> q t j", t=PACK)[:, slots[0] : slots[-1] + 1, :]
-            for quad in (0, 2, 1, 3):
-                nc.sync.dma_start(dst[32 * quad : 32 * quad + 32, :, :], rows)
-            return [dst[:, i, :] for i in range(len(slots))]
-
-        def load_allot(s):
-            dst = held([P, T2], F32, "allot%d" % s)
-            nc.sync.dma_start(dst[:], allot[P * s : P * (s + 1), :])
-            return dst
-
-        def load_w2(a):
-            raw = held([P, PACK, H], F32, "w2_raw%d" % a)
-            nc.sync.dma_start(raw[:], w2[PASS_ROWS * a : PASS_ROWS * (a + 1), :].rearrange("(p j) c -> p j c", j=PACK))
-            return raw
-
-        nc.sync.dma_start(tab_plane[SCALE_AT:P, :].bitcast(I32), tab_scales.rearrange("a q t -> q a t").bitcast(I32))
-        nc.sync.dma_start(pick[:], offs)
-
-        def load_w1_scales(r):
-            rows = w1_scales.rearrange("a (q r) c -> r q a c", r=4)[r]
-            nc.sync.dma_start(w1_plane[r:P:32, :, :].bitcast(I32), rows.bitcast(I32))
-
-        tab_w = [load_words(0)]
-        nc.sync.dma_start(bid_at[:], offs2)
-        load_w1_scales(0)
-        load_w1_scales(1)
-        tab_w.append(load_words(1))
-        load_w1_scales(2)
-        load_w1_scales(3)
-        w1_lead = held([P, PASSES, 4 * P], U8, "w1_lead")
-        w1_rest = held([P, PASSES, 2 * H - 4 * P], U8, "w1_rest")
+        tab_w = [held([P, T], I32, "tab_w%d" % a) for a in range(PASSES)]
+        w1_scale_rows = w1_scales.rearrange("a (q r) c -> r q a c", r=4)
         w1_rows = w1_words.rearrange("a p n -> p a n")
-        nc.sync.dma_start(w1_lead[:].bitcast(I32), w1_rows[:, :, 0 : 4 * P].bitcast(I32))
+        w1_halves = [held([P, PASSES, H], U8, "w1_half%d" % i) for i in range(2)]
+        load_bytes(tab_rows[SCALE_AT:P, :], tab_scales.rearrange("a q t -> q a t"))
+        load(pick[:], offs)
+        load_bytes(tab_w[0][:], tab_words[0].rearrange("p t i -> p (t i)"))
+        load(bid_at[:], offs2)
+        for r in (0, 1):
+            load_bytes(w1_plane[r:P:32, :, :], w1_scale_rows[r])
+        load_bytes(tab_w[1][:], tab_words[1].rearrange("p t i -> p (t i)"))
+        for r in (2, 3):
+            load_bytes(w1_plane[r:P:32, :, :], w1_scale_rows[r])
+        load_bytes(w1_halves[0][:], w1_rows[:, :, 0:H])
 
-        def listed(offsets, j0, j1):
-            return offsets[:, j0 // 16 : j1 // 16]
-
-        picked_plane = held([P, S], U8, "picked_plane")
-        nc.vector.tensor_copy(picked_plane[:], tab_plane[:].indirect(pick[:]))
+        picked_rows = held([P, S], U8, "picked_rows")
+        nc.vector.tensor_copy(picked_rows[:], tab_rows[:].indirect(pick[:]))
 
         def move_scales(half):
             for q in (0, 2, 1, 3):
-                rows = picked_plane[SCALE_AT + 8 * q : SCALE_AT + 8 * (q + 1), half * BANK : (half + 1) * BANK]
-                nc.sync.dma_start(v_plane[32 * q : 32 * q + 4, half, :, :].bitcast(I32), rows.bitcast(I32))
-
-        def v_scales(a, j0, j1):
-            half = j0 // BANK
-            return v_plane[:, half, a, j0 - half * BANK : j1 - half * BANK]
-
-        move_scales(0)
+                rows = picked_rows[SCALE_AT + 8 * q : SCALE_AT + 8 * (q + 1), half * BANK : (half + 1) * BANK]
+                load_bytes(v_plane[32 * q : 32 * q + 4, half, :, :], rows)
 
         wg1_sb = held([P, S], F32, "wg1")
-        nc.sync.dma_start(wg1_sb[:, 0:LEAD], wg1[:, 0:LEAD])
-        nc.sync.dma_start(wg1_sb[:, LEAD:BANK], wg1[:, LEAD:BANK])
+        move_scales(0)
+        load(wg1_sb[:, 0:LEAD], wg1[:, 0:LEAD])
+        load(wg1_sb[:, LEAD:BANK], wg1[:, LEAD:BANK])
         move_scales(1)
-        nc.sync.dma_start(wg1_sb[:, BANK:S], wg1[:, BANK:S])
-        nc.sync.dma_start(w1_rest[:].bitcast(I32), w1_rows[:, :, 4 * P :].bitcast(I32))
-        w2_raw = [load_w2(0)]
-        allot_sb = [load_allot(0)]
-        w2_raw.append(load_w2(1))
-        allot_sb = allot_sb + [load_allot(s) for s in range(1, PACK)]
-        nc.sync.dma_start(ask_at[:], offs3)
-        wg2_sb = load_wg2([0, 1, 2], "wg2_a") + load_wg2([3], "wg2_b")
-        w3_raw = held([P, PACK, N], F32, "w3_raw")
-        nc.sync.dma_start(w3_raw[:], w3.rearrange("(p j) n -> p j n", j=PACK))
-        w4_codes = held([P, 2 * N], U8, "w4_codes")
-        nc.sync.dma_start(w4_codes[:].bitcast(I32), w4_words[0].bitcast(I32))
+        load(wg1_sb[:, BANK:S], wg1[:, BANK:S])
+        load_bytes(w1_halves[1][:], w1_rows[:, :, H:])
+        w2_raw = [held([P, SLOTS, H], F32, "w2_raw%d" % a) for a in range(PASSES)]
+        for a in range(PASSES):
+            load(w2_raw[a][:], w2[a * P * SLOTS : (a + 1) * P * SLOTS, :].rearrange("(p j) c -> p j c", j=SLOTS))
+        allot_sb = [held([P, T2], F32, "allot%d" % s) for s in range(SLOTS)]
+        for s in range(SLOTS):
+            load(allot_sb[s][:], allot[P * s : P * (s + 1), :])
+        load(ask_at[:], offs3)
+        wg2_rows = wg2.rearrange("(q t) j -> q t j", t=SLOTS)
+        wg2_parts = [held([P, 3, S], F32, "wg2_a"), held([P, 1, S], F32, "wg2_b")]
+        for part, t0, t1 in ((wg2_parts[0], 0, 3), (wg2_parts[1], 3, 4)):
+            for quad in (0, 2, 1, 3):
+                load(part[32 * quad : 32 * quad + 32, :, :], wg2_rows[:, t0:t1, :])
+        wg2_sb = [wg2_parts[t // 3][:, t % 3, :] for t in range(SLOTS)]
+        w3_raw = held([P, SLOTS, N], F32, "w3_raw")
+        load(w3_raw[:], w3.rearrange("(p j) n -> p j n", j=SLOTS))
 
         v_codes = [held([P, S], I32, "v_codes%d" % a) for a in range(PASSES)]
         for a, j0, j1 in ((0, 0, S), (1, 0, LEAD), (1, LEAD, BANK), (1, BANK, S)):
-            nc.vector.tensor_copy(v_codes[a][:, j0:j1].bitcast(U32), tab_w[a][:].bitcast(U32).indirect(listed(pick, j0, j1)))
+            nc.vector.tensor_copy(v_codes[a][:, j0:j1].bitcast(U32), tab_w[a][:].bitcast(U32).indirect(entries(pick, j0, j1)))
 
-        def w1_words_of(s, a):
-            return (w1_lead, w1_rest)[s // 2][:, a, 2 * P * (s % 2) : 2 * P * (s % 2 + 1)]
+        def scores(dst, weights, j0, j1, scale):
+            acc = bank("scores", "three")
+            half = j0 // BANK
+            for a in range(PASSES):
+                codes, plane = weights(a)
+                rhs_scale = v_plane[:, half, a, j0 - half * BANK : j1 - half * BANK]
+                product(acc[:, 0 : j1 - j0], codes, plane, v_codes[a][:, j0:j1].bitcast(FP8X4), rhs_scale, a == 0, a == PASSES - 1)
+            nc.scalar.activation(dst[:, j0:j1], acc[:, 0 : j1 - j0], ACT.Copy, scale=scale)
 
-        def bid_scores(s, scores, j0, j1, width):
-            acc = bank("h1_acc", "h")
-            for n0 in range(j0, j1, width):
-                cols = slice(n0, n0 + width)
-                for a in range(PASSES):
-                    nc.tensor.matmul_mx(
-                        out=acc[:, n0 - j0 : n0 - j0 + width],
-                        lhsT=w1_words_of(s, a).bitcast(FP4X4),
-                        lhsT_scale=w1_plane[:, a, P * s : P * (s + 1)],
-                        rhs=v_codes[a][:, cols].bitcast(FP8X4),
-                        rhs_scale=v_scales(a, cols.start, cols.stop),
-                        start=(a == 0),
-                        stop=(a == PASSES - 1),
-                    )
-            nc.scalar.activation(scores[:, j0:j1], acc[:, 0 : j1 - j0], ACT.Copy, scale=-1.0)
+        def bid_scores(s, j0, j1):
+            at = 2 * P * (s % 2)
+            weights = lambda a: (w1_halves[s // 2][:, a, at : at + 2 * P].bitcast(FP4X4), w1_plane[:, a, P * s : P * (s + 1)])
+            scores(h1[s], weights, j0, j1, -1.0)
 
-        h1 = [held([P, S], F32, "h1_%d" % s) for s in range(PACK)]
-        for j0 in range(0, LEAD, P):
-            bid_scores(0, h1[0], j0, j0 + P, P)
-        bid_scores(1, h1[1], 0, BANK, BANK)
-        bid_scores(0, h1[0], LEAD, BANK, BANK - LEAD)
-        for s in range(PACK):
-            if s > 1:
-                bid_scores(s, h1[s], 0, BANK, BANK)
-            bid_scores(s, h1[s], BANK, S, BANK)
+        h1 = [held([P, S], F32, "h1_%d" % s) for s in range(2)]
+        for s, j0, j1 in ((0, 0, P), (0, P, LEAD), (1, 0, BANK), (0, LEAD, BANK), (0, BANK, S), (1, BANK, S)):
+            bid_scores(s, j0, j1)
+        bid_pages.append(zero_page("bid_page1", "tab_rows"))
+        bid_pages.append(zero_page("bid_page2", "tab_w1"))
 
-        second_page = held([P, T2], F32, "bid_page1", tag="tab_plane")
-        nc.gpsimd.memset(second_page[:], 0.0)
-        bid_pages.append(second_page)
+        def place_bid(s, j0=0, j1=S):
+            page = bid_pages[s % len(bid_pages)]
+            nc.vector.tensor_tensor(page[:].indirect(entries(bid_at, j0, j1)), h1[s][:, j0:j1], wg1_sb[:, j0:j1], ALU.mult)
+
+        for s, j0, j1 in ((0, 0, LEAD), (1, 0, BANK), (0, LEAD, S), (1, BANK, S)):
+            place_bid(s, j0, j1)
+
+        w2_bf = held([P, PASSES * SLOTS * H], BF16, "w2_bf")
+        for a in range(PASSES):
+            nc.scalar.copy(
+                w2_bf[:, a * SLOTS * H : (a + 1) * SLOTS * H].rearrange("p (t m j) -> p m t j", t=SLOTS, j=SLOTS),
+                w2_raw[a][:].rearrange("p j (m t) -> p m t j", t=SLOTS),
+            )
+        w2_codes = held([P, PASSES * H], U32, "w2_codes")
+        w2_plane = held([P, PASSES * H], U8, "w2_plane")
+        quantise(w2_codes[:], w2_plane[:], w2_bf[:])
+
+        for s, tag in ((2, "w2_raw1"), (3, None)):
+            h1.append(held([P, S], F32, "h1_%d" % s, tag=tag))
+            for j0 in range(0, S, BANK):
+                bid_scores(s, j0, j0 + BANK)
 
         w4_plane = held([P, N], U8, "w4_plane", tag="w1_plane")
         nc.gpsimd.memset(w4_plane[:].bitcast(I32), 0)
-        for q in range(QUADS):
-            nc.sync.dma_start(w4_plane[32 * q : 32 * q + 4, :].bitcast(I32), w4_scales[0, 4 * q : 4 * q + 4, :].bitcast(I32))
+        for q in range(4):
+            load_bytes(w4_plane[32 * q : 32 * q + 4, :], w4_scales[0, 4 * q : 4 * q + 4, :])
 
         left_t = held([P, T2 // P, 2, P, 2], BF16, "left_t")
 
-        def place_bid(s, j0=0, j1=S):
-            page = bid_pages[s % 2]
-            nc.vector.tensor_tensor(page[:].indirect(listed(bid_at, j0, j1)), h1[s][:, j0:j1], wg1_sb[:, j0:j1], ALU.mult)
-
         def take_off(s):
-            page = bid_pages[s % 2]
-            accs = [bank("left_acc", "d") for c in range(CHUNKS)]
+            page = bid_pages[s % len(bid_pages)]
+            accs = [bank("left_acc", "five") for c in range(CHUNKS)]
+            blocks = BANK // P
             for n_src, source in enumerate((allot_sb[s], page)):
                 for c, acc in enumerate(accs):
-                    for i in range(BLOCKS):
+                    for i in range(blocks):
                         m0 = c * BANK + i * P
+                        first, last = n_src == 0 and i == 0, n_src == 1 and i == blocks - 1
                         nc.tensor.matmul(
-                            acc[:, i * P : (i + 1) * P],
-                            source[:, m0 : m0 + P],
-                            ident,
-                            start=(n_src == 0 and i == 0),
-                            stop=(n_src == 1 and i == BLOCKS - 1),
-                            is_transpose=True,
+                            acc[:, i * P : (i + 1) * P], source[:, m0 : m0 + P], ident, start=first, stop=last, is_transpose=True
                         )
             for c, acc in enumerate(accs):
                 nc.scalar.copy(
-                    left_t[:, c * BLOCKS : (c + 1) * BLOCKS, :, 32 * s : 32 * (s + 1), :].rearrange("m i u p e -> m u i p e"),
-                    acc[:].rearrange("m (i p u e) -> m u i p e", i=BLOCKS, u=2, e=2),
+                    left_t[:, c * blocks : (c + 1) * blocks, :, 32 * s : 32 * (s + 1), :].rearrange("m i u p e -> m u i p e"),
+                    acc[:].rearrange("m (i p u e) -> m u i p e", i=blocks, u=2, e=2),
                 )
 
-        left_tags = ["w2_raw0", "w2_raw1", "w2_bf0"]
-        left_sb = [held([P, BANK, 2], F32, "left%d" % c, tag=tag) for c, tag in enumerate(left_tags)]
-
-        def turn_back(piece):
-            acc = bank("left", "d")
-            for u in range(2):
-                for i in range(2):
-                    words = left_t[:, 2 * piece + i, u, :, :].rearrange("m p e -> m (p e)").bitcast(F32)
-                    nc.tensor.transpose(acc[:, (2 * u + i) * P : (2 * u + i + 1) * P], words, ident)
-            if piece >= PARKED:
-                return acc[:].bitcast(BF16).rearrange("p (u m e) -> p m u e", u=2, e=2)
-            m0 = piece % 2 * PIECE
-            parked = left_sb[piece // 2][:, m0 : m0 + PIECE, :]
-            nc.scalar.copy(parked, acc[:].rearrange("p (u m) -> p m u", u=2))
-            return parked.rearrange("p m u -> p (m u)").bitcast(BF16).rearrange("p (m u e) -> p m u e", u=2, e=2)
-
-        place_bid(0, 0, LEAD)
-        place_bid(1, 0, BANK)
-        place_bid(0, LEAD, S)
-        place_bid(1, BANK, S)
-
-        w2_bf = []
-        for a in range(PASSES):
-            rounded = held([P, PACK * H], BF16, "w2_bf%d" % a)
-            nc.scalar.copy(
-                rounded[:].rearrange("p (t m j) -> p m t j", t=PACK, j=PACK),
-                w2_raw[a][:].rearrange("p j (m t) -> p m t j", t=PACK),
-            )
-            w2_bf.append(rounded)
         take_off(0)
         place_bid(2)
         take_off(1)
-        w2_codes, w2_plane = [], []
-        for a in range(PASSES):
-            codes = held([P, H], U32, "w2_codes%d" % a, tag=(None, "allot1")[a])
-            plane = held([P, H], U8, "w2_plane%d" % a)
-            nc.vector.quantize_mx(out=codes[:].bitcast(FP8X4), scales=plane[:], in_=w2_bf[a][:])
-            w2_codes.append(codes)
-            w2_plane.append(plane)
-
-        h2 = []
-        for t in range(PACK):
-            scores = held([P, S], F32, "h2_%d" % t)
-            for half in range(HALVES):
-                cols = slice(half * BANK, (half + 1) * BANK)
-                acc = bank("h2_acc", "h")
-                for a in reversed(range(PASSES)):
-                    nc.tensor.matmul_mx(
-                        out=acc[:],
-                        lhsT=w2_codes[a][:, P * t : P * (t + 1)].bitcast(FP8X4),
-                        lhsT_scale=w2_plane[a][:, P * t : P * (t + 1)],
-                        rhs=v_codes[a][:, cols].bitcast(FP8X4),
-                        rhs_scale=v_scales(a, cols.start, cols.stop),
-                        start=(a == PASSES - 1),
-                        stop=(a == 0),
-                    )
-                nc.scalar.copy(scores[:, cols], acc[:])
-            h2.append(scores)
-
+        h2 = {}
+        for t in ASK_ORDER:
+            h2[t] = held([P, S], F32, "h2_%d" % t)
+            weights = lambda a: (
+                w2_codes[:, a * H + P * t : a * H + P * (t + 1)].bitcast(FP8X4),
+                w2_plane[:, a * H + P * t : a * H + P * (t + 1)],
+            )
+            for j0 in range(0, S, BANK):
+                scores(h2[t], weights, j0, j0 + BANK, 1.0)
         place_bid(3)
         take_off(2)
         take_off(3)
 
-        ask_tags = ["h1_%d" % t for t in range(PACK)]
-        ask_pages = [held([P, T2], F32, "ask_page%d" % t, tag=tag) for t, tag in enumerate(ask_tags)]
-        for page in ask_pages:
-            nc.gpsimd.memset(page[:], 0.0)
-
+        pages = [zero_page("ask_page%d" % i, tag) for i, tag in enumerate(("h1_0", "w2_bf", "w2_raw1"))]
+        ask_page = {t: pages[n % len(pages)] for n, t in enumerate(ASK_ORDER)}
         floor = [held([P, 2, PIECE, 2], BF16, "floor%d" % piece) for piece in range(PIECES)]
-        woven_tags = ["tab_w0", "wg1", "allot2", "h2_1"]
-        woven = [held([P, BANK, PACK], BF16, "woven%d" % c, tag=woven_tags[c]) for c in range(CHUNKS)]
+        woven_tags = ["tab_w0", "allot2", "allot3", "wg1"]
+        woven = [held([P, BANK, SLOTS], BF16, "woven%d" % c, tag=woven_tags[c]) for c in range(CHUNKS)]
 
         def place_ask(t):
-            nc.vector.tensor_tensor(ask_pages[t][:].indirect(ask_at[:]), h2[t][:], wg2_sb[t], ALU.mult)
+            nc.vector.tensor_tensor(ask_page[t][:].indirect(ask_at[:]), h2[t][:], wg2_sb[t], ALU.mult)
 
-        def round_ask(t, first=PIECE):
-            for m0, m1 in [(m, m + first) for m in range(0, PIECE, first)] + [(m, m + PIECE) for m in range(PIECE, T2, PIECE)]:
-                piece, at = divmod(m0, PIECE)
-                nc.scalar.copy(floor[piece][:, t // 2, at : at + m1 - m0, t % 2], ask_pages[t][:, m0:m1])
+        def rounding(t, piece, m0=0, m1=PIECE):
+            return floor[piece][:, t // 2, m0:m1, t % 2], ask_page[t][:, piece * PIECE + m0 : piece * PIECE + m1]
+
+        def turn_back(piece):
+            acc = bank("left", "five")
+            for u in range(2):
+                for i in range(2):
+                    words = left_t[:, 2 * piece + i, u, :, :].rearrange("m p e -> m (p e)").bitcast(F32)
+                    nc.tensor.transpose(acc[:, (2 * u + i) * P : (2 * u + i + 1) * P], words, ident)
+            if piece not in PARKED:
+                return acc[:].bitcast(BF16).rearrange("p (u m e) -> p m u e", u=2, e=2)
+            parked = held([P, PIECE, 2], F32, "left%d" % piece, tag=("v_codes0", "v_codes1", "h1_1", "h1_3", None, None)[PARKED.index(piece)])
+            nc.scalar.copy(parked[:], acc[:].rearrange("p (u m) -> p m u", u=2))
+            return parked[:].rearrange("p m u -> p (m u)").bitcast(BF16).rearrange("p (m u e) -> p m u e", u=2, e=2)
+
+        left = {}
+        w3_bf = held([P, SLOTS * N], BF16, "w3_bf")
+        for n, t in enumerate(ASK_ORDER[:-1]):
+            place_ask(t)
+            for piece in range(PIECES):
+                if (n, piece) == (2, W3_AT):
+                    nc.scalar.copy(
+                        w3_bf[:].rearrange("p (g i j) -> p g j i", i=4, j=SLOTS),
+                        w3_raw[:].rearrange("p j (g i) -> p g j i", i=4),
+                    )
+                nc.scalar.copy(*rounding(t, piece))
+            if n == 0:
+                for piece in PARKED + tuple(piece for piece in range(PIECES) if piece not in PARKED):
+                    left[piece] = turn_back(piece)
+        last = ASK_ORDER[-1]
+        place_ask(last)
+
+        w4_codes = held([P, 2 * N], U8, "w4_codes", tag="w3_raw")
+        load_bytes(w4_codes[:], w4_words[0])
+        w3_codes = held([P, N], U32, "w3_codes")
+        w3_plane = held([P, N], U8, "w3_plane")
+        for n0, n1 in ((0, 256), (256, N)):
+            quantise(w3_codes[:, n0:n1], w3_plane[:, n0:n1], w3_bf[:, SLOTS * n0 : SLOTS * n1])
+
+        idle = bank("idle", "three")
+        for codes, plane in [(w4_codes[:, 0 : 2 * P].bitcast(FP4X4), w4_plane)] * 3 + [(w3_codes[:, 0:P].bitcast(FP8X4), w3_plane)] * 2:
+            product(idle[:], codes, plane[:, 0:P], w2_codes[:, 0:BANK].bitcast(FP8X4), w2_plane[:, 0:BANK])
+        for m0 in (0, P):
+            nc.scalar.copy(*rounding(last, 0, m0, m0 + P))
+        for piece in range(1, PIECES):
+            dst, src = rounding(last, piece)
+            if piece in ROUNDED_ASIDE:
+                nc.gpsimd.tensor_scalar(dst, src, 1.0, 0.0, op0=ALU.mult, op1=ALU.add)
+            else:
+                nc.scalar.copy(dst, src)
 
         def clear(piece, m0=0, m1=PIECE):
             at = piece % 2 * PIECE
@@ -304,116 +289,80 @@ def tile_list_canal_week_clearing_kernel(
                 ALU.max,
             )
 
-        place_ask(0)
-        round_ask(0)
-        place_ask(1)
-        w3_bf = held([P, PACK * N], BF16, "w3_bf")
-        nc.scalar.copy(
-            w3_bf[:].rearrange("p (g i j) -> p g j i", i=4, j=PACK),
-            w3_raw[:].rearrange("p j (g i) -> p g j i", i=4),
-        )
-        left = [turn_back(piece) for piece in range(PIECES)]
-        round_ask(1)
-        place_ask(2)
-        round_ask(2)
-        place_ask(3)
+        z_codes, z_plane = {}, {}
 
-        w3_codes = held([P, N], U32, "w3_codes", tag="h2_3")
-        w3_plane = held([P, N], U8, "w3_plane")
-        for n0, n1 in ((0, 256), (256, N)):
-            nc.vector.quantize_mx(
-                out=w3_codes[:, n0:n1].bitcast(FP8X4), scales=w3_plane[:, n0:n1], in_=w3_bf[:, PACK * n0 : PACK * n1]
-            )
+        def pack(c, tag=None):
+            z_codes[c] = held([P, BANK], U32, "z_codes%d" % c, tag=tag)
+            z_plane[c] = held([P, BANK], U8, "z_plane%d" % c)
+            for m0 in (0, PIECE):
+                values = woven[c][:, m0 : m0 + PIECE, :].rearrange("p m t -> p (m t)")
+                quantise(z_codes[c][:, m0 : m0 + PIECE], z_plane[c][:, m0 : m0 + PIECE], values)
 
-        z_codes = [held([P, BANK], U32, "z_codes%d" % c) for c in range(2)]
-        z_plane = [held([P, BANK], U8, "z_plane%d" % c) for c in range(CHUNKS)]
-
-        def pack(c, m0=0, m1=BANK):
-            if c >= len(z_codes):
-                z_codes.append(held([P, BANK], U32, "z_codes%d" % c, tag="copied%d" % (c - 1)))
-            nc.vector.quantize_mx(
-                out=z_codes[c][:, m0:m1].bitcast(FP8X4),
-                scales=z_plane[c][:, m0:m1],
-                in_=woven[c][:, m0:m1, :].rearrange("p m t -> p (m t)"),
-            )
-
-        result_tags = ("tab_w1", "allot1", "allot0", "allot3")
-        results = [held([P, N_TILES, BANK], F32, "result%d" % c, tag=result_tags[c]) for c in range(CHUNKS)]
-        squash_tags = ("left_t", "wg2_a", "w3_raw", None)
+        squash_tags = ("left_t", "wg2_a", "w2_raw0", "allot0")
         squashes = [held([P, N_TILES, BANK], F32, "squashed%d" % c, tag=squash_tags[c]) for c in range(CHUNKS)]
+        result_tags = ("tab_w1", "allot1", "offset", "tab_rows")
+        results = [held([P, N_TILES, BANK], F32, "result%d" % c, tag=result_tags[c]) for c in range(CHUNKS)]
 
-        def bounded_pass(acc, c, i, m0=0, m1=BANK):
-            nc.tensor.matmul_mx(
-                out=acc[:, m0:m1],
-                lhsT=w3_codes[:, i * P : (i + 1) * P].bitcast(FP8X4),
-                lhsT_scale=w3_plane[:, i * P : (i + 1) * P],
-                rhs=z_codes[c][:, m0:m1].bitcast(FP8X4),
-                rhs_scale=z_plane[c][:, m0:m1],
-                start=True,
-                stop=True,
-            )
+        def reading(kind, c, i, m0, m1, acc):
+            codes = w3_codes[:, i * P : (i + 1) * P].bitcast(FP8X4) if kind == "bounded" else w4_codes[:, 2 * P * i : 2 * P * (i + 1)].bitcast(FP4X4)
+            plane = (w3_plane if kind == "bounded" else w4_plane)[:, i * P : (i + 1) * P]
+            product(acc[:, m0:m1], codes, plane, z_codes[c][:, m0:m1].bitcast(FP8X4), z_plane[c][:, m0:m1])
 
-        def linear_pass(acc, c, i, m0=0, m1=BANK):
-            nc.tensor.matmul_mx(
-                out=acc[:, m0:m1],
-                lhsT=w4_codes[:, 2 * P * i : 2 * P * (i + 1)].bitcast(FP4X4),
-                lhsT_scale=w4_plane[:, i * P : (i + 1) * P],
-                rhs=z_codes[c][:, m0:m1].bitcast(FP8X4),
-                rhs_scale=z_plane[c][:, m0:m1],
-                start=True,
-                stop=True,
-            )
+        def squash(c, i):
+            acc = bank("bounded", "three")
+            reading("bounded", c, i, 0, BANK, acc)
+            nc.scalar.activation(squashes[c][:, i, :], acc[:], ACT.Tanh)
 
-        def squash(c, i, bounded=None):
-            if bounded is None:
-                bounded = bank("bounded", "h")
-                bounded_pass(bounded, c, i)
-            nc.scalar.activation(squashes[c][:, i, :], bounded[:], ACT.Tanh)
-
-        def read_out(c, i, behind=None, linear=None):
-            if linear is None:
-                linear = bank("linear", "d")
-                linear_pass(linear, c, i)
-            if behind is None:
-                result = results[c][:, i, :]
-                nc.vector.tensor_tensor(result, linear[:], squashes[c][:, i, :], ALU.add)
-            else:
-                copied = held([P, BANK], F32, "copied%d" % behind)
-                nc.scalar.copy(copied[:], linear[:])
-                result = held([P, BANK], F32, "late%d" % behind, tag=woven_tags[behind])[:]
-                nc.gpsimd.tensor_tensor(result, copied[:], squashes[c][:, i, :], ALU.add)
+        def store(c, i, result):
             nc.sync.dma_start(out[i * P : (i + 1) * P, c * BANK : (c + 1) * BANK], result)
 
-        round_ask(3, first=P)
-        first = [bank("bounded", "h"), bank("linear", "d"), bank("bounded", "h")]
-        clear(0, 0, P)
-        clear(0, P, PIECE)
-        for piece in range(2):
-            clear(piece + 1)
-            m0, m1 = piece * PIECE, (piece + 1) * PIECE
-            pack(0, m0, m1)
-            bounded_pass(first[0], 0, 0, m0, m1)
-            linear_pass(first[1], 0, 0, m0, m1)
-            bounded_pass(first[2], 0, 1, m0, m1)
-        clear(3)
-        clear(4)
-        pack(1)
-        squash(0, 0, first[0])
-        read_out(0, 0, behind=1, linear=first[1])
-        squash(0, 1, first[2])
-        squash(0, 2)
-        for piece in range(PARKED, PIECES):
-            clear(piece)
-        read_out(0, 1)
+        def add_up(c, i):
+            acc = bank("linear", "five")
+            reading("linear", c, i, 0, BANK, acc)
+            nc.vector.tensor_tensor(results[c][:, i, :], acc[:], squashes[c][:, i, :], ALU.add)
+            store(c, i, results[c][:, i, :])
+
+        def copy_linear(c, i, name):
+            acc = bank("linear", "five")
+            reading("linear", c, i, 0, BANK, acc)
+            copied = held([P, BANK], F32, name)
+            nc.scalar.copy(copied[:], acc[:])
+            return copied
+
+        def add_aside(c, i, copied, result):
+            nc.gpsimd.tensor_tensor(result, copied[:], squashes[c][:, i, :], ALU.add)
+            store(c, i, result)
+
+        for m0 in (0, P):
+            clear(0, m0, m0 + P)
+        clear(1)
+        pack(0)
+        squash(0, 0)
+        squash(0, 1)
+        first = copy_linear(0, 1, "copied0")
+        for c in (1, 2):
+            clear(2 * c)
+            clear(2 * c + 1)
+            pack(c)
         squash(1, 0)
-        pack(2)
-        read_out(0, 2, behind=2)
-        read_out(1, 0)
-        for i in range(1, N_TILES):
-            squash(1, i)
-            read_out(1, i)
-        pack(3)
-        for c in range(2, CHUNKS):
-            for i in range(N_TILES):
-                squash(c, i)
-                read_out(c, i)
+        squash(0, 2)
+        second = copy_linear(0, 2, "copied1")
+        aside = held([P, 2, BANK], F32, "aside", tag=woven_tags[2])
+        add_up(0, 0)
+        add_aside(0, 1, first, aside[:, 0, :])
+        clear(6)
+        add_up(1, 0)
+        clear(7)
+        squash(1, 1)
+        add_up(1, 1)
+        add_aside(0, 2, second, aside[:, 1, :])
+        squash(1, 2)
+        add_up(1, 2)
+        for i in range(N_TILES):
+            squash(2, i)
+        pack(3, tag="copied1")
+        for i in range(N_TILES):
+            add_up(2, i)
+        for i in range(N_TILES):
+            squash(3, i)
+            add_up(3, i)

@@ -267,10 +267,6 @@ def tile_list_canal_week_clearing_kernel(
         w3_plane = held([P, N], U8, "w3_plane")
         for n0, n1 in ((0, 256), (256, N)):
             quantise(w3_codes[:, n0:n1], w3_plane[:, n0:n1], w3_bf[:, SLOTS * n0 : SLOTS * n1])
-
-        idle = bank("idle", "three")
-        for codes, plane in [(w4_codes[:, 0 : 2 * P].bitcast(FP4X4), w4_plane)] * 3 + [(w3_codes[:, 0:P].bitcast(FP8X4), w3_plane)] * 2:
-            product(idle[:], codes, plane[:, 0:P], w2_codes[:, 0:BANK].bitcast(FP8X4), w2_plane[:, 0:BANK])
         for m0 in (0, P):
             nc.scalar.copy(*rounding(last, 0, m0, m0 + P))
         for piece in range(1, PIECES):

@@ -132,6 +132,8 @@ def tile_list_canal_week_clearing_kernel(
         wg2_sb = [wg2_parts[t // 3][:, t % 3, :] for t in range(SLOTS)]
         w3_raw = held([P, SLOTS, N], F32, "w3_raw")
         load(w3_raw[:], w3.rearrange("(p j) n -> p j n", j=SLOTS))
+        w4_codes = held([P, 2 * N], U8, "w4_codes")
+        load_bytes(w4_codes[:], w4_words[0])
 
         v_codes = [held([P, S], I32, "v_codes%d" % a) for a in range(PASSES)]
         for a, j0, j1 in ((0, 0, S), (1, 0, LEAD), (1, LEAD, BANK), (1, BANK, S)):
@@ -222,7 +224,7 @@ def tile_list_canal_week_clearing_kernel(
 
         pages = [zero_page("ask_page%d" % i, tag) for i, tag in enumerate(("h1_0", "w2_bf", "w2_raw1"))]
         ask_page = {t: pages[n % len(pages)] for n, t in enumerate(ASK_ORDER)}
-        floor = [held([P, 2, PIECE, 2], BF16, "floor%d" % piece) for piece in range(PIECES)]
+        floor = [held([P, 2, BANK, 2], BF16, "floor%d" % c) for c in range(CHUNKS)]
         woven_tags = ["tab_w0", "allot2", "allot3", "wg1"]
         woven = [held([P, BANK, SLOTS], BF16, "woven%d" % c, tag=woven_tags[c]) for c in range(CHUNKS)]
 
@@ -230,7 +232,8 @@ def tile_list_canal_week_clearing_kernel(
             nc.vector.tensor_tensor(ask_page[t][:].indirect(ask_at[:]), h2[t][:], wg2_sb[t], ALU.mult)
 
         def rounding(t, piece, m0=0, m1=PIECE):
-            return floor[piece][:, t // 2, m0:m1, t % 2], ask_page[t][:, piece * PIECE + m0 : piece * PIECE + m1]
+            at = piece % 2 * PIECE
+            return floor[piece // 2][:, t // 2, at + m0 : at + m1, t % 2], ask_page[t][:, piece * PIECE + m0 : piece * PIECE + m1]
 
         def turn_back(piece):
             acc = bank("left", "five")
@@ -240,10 +243,10 @@ def tile_list_canal_week_clearing_kernel(
                     nc.tensor.transpose(acc[:, (2 * u + i) * P : (2 * u + i + 1) * P], words, ident)
             if piece not in PARKED:
                 return acc[:].bitcast(BF16).rearrange("p (u m e) -> p m u e", u=2, e=2)
-            parked = held([P, PIECE, 2], F32, "left%d" % piece, tag=("v_codes0", "v_codes1", "h1_1", "h1_3", None, None)[PARKED.index(piece)])
-            nc.scalar.copy(parked[:], acc[:].rearrange("p (u m) -> p m u", u=2))
-            return parked[:].rearrange("p m u -> p (m u)").bitcast(BF16).rearrange("p (m u e) -> p m u e", u=2, e=2)
+            at = piece % 2 * PIECE
+            nc.scalar.copy(parked[piece // 2][:, at : at + PIECE, :], acc[:].rearrange("p (u m) -> p m u", u=2))
 
+        parked = [held([P, BANK, 2], F32, "left%d" % c, tag=tag) for c, tag in enumerate(("v_codes0", "v_codes1", "h1_1"))]
         left = {}
         w3_bf = held([P, SLOTS * N], BF16, "w3_bf")
         for n, t in enumerate(ASK_ORDER[:-1]):
@@ -261,12 +264,9 @@ def tile_list_canal_week_clearing_kernel(
         last = ASK_ORDER[-1]
         place_ask(last)
 
-        w4_codes = held([P, 2 * N], U8, "w4_codes", tag="w3_raw")
-        load_bytes(w4_codes[:], w4_words[0])
         w3_codes = held([P, N], U32, "w3_codes")
         w3_plane = held([P, N], U8, "w3_plane")
-        for n0, n1 in ((0, 256), (256, N)):
-            quantise(w3_codes[:, n0:n1], w3_plane[:, n0:n1], w3_bf[:, SLOTS * n0 : SLOTS * n1])
+        quantise(w3_codes[:], w3_plane[:], w3_bf[:])
         for m0 in (0, P):
             nc.scalar.copy(*rounding(last, 0, m0, m0 + P))
         for piece in range(1, PIECES):
@@ -276,23 +276,26 @@ def tile_list_canal_week_clearing_kernel(
             else:
                 nc.scalar.copy(dst, src)
 
-        def clear(piece, m0=0, m1=PIECE):
-            at = piece % 2 * PIECE
+        def clear(c, m0=0, m1=BANK):
+            if c < len(parked):
+                pairs = parked[c][:, m0:m1, :].rearrange("p m u -> p (m u)").bitcast(BF16).rearrange("p (m u e) -> p m u e", u=2, e=2)
+            else:
+                pairs = left[2 * c + m0 // PIECE]
             nc.vector.tensor_tensor(
-                woven[piece // 2][:, at + m0 : at + m1, :].rearrange("p m (u e) -> p m u e", u=2),
-                left[piece][:, m0:m1],
-                floor[piece][:, :, m0:m1, :].rearrange("p u m e -> p m u e"),
+                woven[c][:, m0:m1, :].rearrange("p m (u e) -> p m u e", u=2),
+                pairs,
+                floor[c][:, :, m0:m1, :].rearrange("p u m e -> p m u e"),
                 ALU.max,
             )
 
         z_codes, z_plane = {}, {}
 
-        def pack(c, tag=None):
+        def pack(c, width=BANK, tag=None):
             z_codes[c] = held([P, BANK], U32, "z_codes%d" % c, tag=tag)
             z_plane[c] = held([P, BANK], U8, "z_plane%d" % c)
-            for m0 in (0, PIECE):
-                values = woven[c][:, m0 : m0 + PIECE, :].rearrange("p m t -> p (m t)")
-                quantise(z_codes[c][:, m0 : m0 + PIECE], z_plane[c][:, m0 : m0 + PIECE], values)
+            for m0 in range(0, BANK, width):
+                values = woven[c][:, m0 : m0 + width, :].rearrange("p m t -> p (m t)")
+                quantise(z_codes[c][:, m0 : m0 + width], z_plane[c][:, m0 : m0 + width], values)
 
         squash_tags = ("left_t", "wg2_a", "w2_raw0", "allot0")
         squashes = [held([P, N_TILES, BANK], F32, "squashed%d" % c, tag=squash_tags[c]) for c in range(CHUNKS)]
@@ -304,9 +307,10 @@ def tile_list_canal_week_clearing_kernel(
             plane = (w3_plane if kind == "bounded" else w4_plane)[:, i * P : (i + 1) * P]
             product(acc[:, m0:m1], codes, plane, z_codes[c][:, m0:m1].bitcast(FP8X4), z_plane[c][:, m0:m1])
 
-        def squash(c, i):
+        def squash(c, i, width=BANK):
             acc = bank("bounded", "three")
-            reading("bounded", c, i, 0, BANK, acc)
+            for m0 in range(0, BANK, width):
+                reading("bounded", c, i, m0, m0 + width, acc)
             nc.scalar.activation(squashes[c][:, i, :], acc[:], ACT.Tanh)
 
         def store(c, i, result):
@@ -329,26 +333,25 @@ def tile_list_canal_week_clearing_kernel(
             nc.gpsimd.tensor_tensor(result, copied[:], squashes[c][:, i, :], ALU.add)
             store(c, i, result)
 
-        for m0 in (0, P):
-            clear(0, m0, m0 + P)
-        clear(1)
-        pack(0)
-        squash(0, 0)
+        for m0, m1 in ((0, P), (P, PIECE), (PIECE, BANK)):
+            clear(0, m0, m1)
+        pack(0, PIECE)
+        squash(0, 0, PIECE)
         squash(0, 1)
         first = copy_linear(0, 1, "copied0")
         for c in (1, 2):
-            clear(2 * c)
-            clear(2 * c + 1)
-            pack(c)
+            for m0 in (0, PIECE):
+                clear(c, m0, m0 + PIECE)
+            pack(c, PIECE)
         squash(1, 0)
         squash(0, 2)
         second = copy_linear(0, 2, "copied1")
         aside = held([P, 2, BANK], F32, "aside", tag=woven_tags[2])
         add_up(0, 0)
         add_aside(0, 1, first, aside[:, 0, :])
-        clear(6)
+        clear(3, 0, PIECE)
         add_up(1, 0)
-        clear(7)
+        clear(3, PIECE, BANK)
         squash(1, 1)
         add_up(1, 1)
         add_aside(0, 2, second, aside[:, 1, :])

@@ -240,11 +240,11 @@ def tile_list_canal_week_clearing_kernel(
             for u in range(2):
                 for i in range(2):
                     words = left_t[:, 2 * piece + i, u, :, :].rearrange("m p e -> m (p e)").bitcast(F32)
-                    nc.tensor.transpose(acc[:, (2 * u + i) * P : (2 * u + i + 1) * P], words, ident)
+                    nc.tensor.transpose(acc[:].rearrange("p (i m u) -> p i u m", i=2, u=2)[:, i, u, :], words, ident)
             if piece not in PARKED:
-                return acc[:].bitcast(BF16).rearrange("p (u m e) -> p m u e", u=2, e=2)
+                return acc[:].bitcast(BF16).rearrange("p (m u e) -> p m u e", u=2, e=2)
             at = piece % 2 * PIECE
-            nc.scalar.copy(parked[piece // 2][:, at : at + PIECE, :], acc[:].rearrange("p (u m) -> p m u", u=2))
+            nc.scalar.copy(parked[piece // 2][:, at : at + PIECE, :], acc[:].rearrange("p (m u) -> p m u", u=2))
 
         parked = [held([P, BANK, 2], F32, "left%d" % c, tag=tag) for c, tag in enumerate(("v_codes0", "v_codes1", "h1_1"))]
         left = {}

from contextlib import ExitStack

import concourse.mybir as mybir

K, T, S, T2, H, N = 1024, 2048, 1024, 2048, 512, 384
FLOPS = 2 * (2 * K * H * S + 2 * H * N * T2)

F32 = mybir.dt.float32
BF16 = mybir.dt.bfloat16
I32 = mybir.dt.int32
U32 = mybir.dt.uint32
U16 = mybir.dt.uint16
U8 = mybir.dt.uint8
FP8X4 = mybir.dt.float8_e4m3fn_x4
FP4X4 = mybir.dt.float4_e2m1fn_x4
ACT = mybir.ActivationFunctionType
ALU = mybir.AluOpType

P = 128
SLOTS = 4
PASSES = K // (P * SLOTS)
BANK = 512
PIECE = BANK // 2
CHUNKS = T2 // BANK
PIECES = T2 // PIECE
N_TILES = N // P
SCALE_AT = 96
LEAD = 256
ASK_ORDER = (2, 0, 1, 3)
PARKED = (0, 1, 2, 3, 4, 5)
ROUNDED_ASIDE = ()
W3_AT = 2


def tile_list_canal_week_clearing_kernel(
    tc, tab_words, tab_scales, offs, offs2, offs3, w1_words, w1_scales, w2, wg1, wg2, allot, w3, w4_words, w4_scales, out
):
    nc = tc.nc
    with ExitStack() as ctx:
        lists = ctx.enter_context(tc.tile_pool(name="lists", bufs=1))
        sb = ctx.enter_context(tc.tile_pool(name="sb", bufs=1))
        ps = ctx.enter_context(tc.psum_pool(name="ps", bufs=1))

        def held(shape, dtype, name, tag=None):
            return sb.tile(shape, dtype, name=name, tag=tag or name, align_bytes=64)

        def bank(name, ring):
            return ps.tile([P, BANK], F32, name=name, tag=ring, bufs={"three": 3, "five": 5}[ring])

        def product(acc, lhs, lhs_scale, rhs, rhs_scale, start=True, stop=True):
            nc.tensor.matmul_mx(out=acc, lhsT=lhs, lhsT_scale=lhs_scale, rhs=rhs, rhs_scale=rhs_scale, start=start, stop=stop)

        def quantise(codes, plane, values):
            nc.vector.quantize_mx(out=codes.bitcast(FP8X4), scales=plane, in_=values)

        def load(dst, src):
            nc.sync.dma_start(dst, src)

        def load_bytes(dst, src):
            nc.sync.dma_start(dst.bitcast(I32), src.bitcast(I32))

        def entries(offsets, j0, j1):
            return offsets[:, j0 // 16 : j1 // 16]

        pick = lists.tile([P, S // 16], U16, name="pick")
        bid_at = lists.tile([P, S // 16], U16, name="bid_at")
        ask_at = lists.tile([P, S // 16], U16, name="ask_at")

        tab_rows = held([P, T], U8, "tab_rows")
        w1_plane = held([P, PASSES, H], U8, "w1_plane")
        v_plane = held([P, S // BANK, PASSES, BANK], U8, "v_plane")
        nc.vector.memset(w1_plane[:].rearrange("p a c -> p (a c)").bitcast(I32), 0)
        nc.vector.memset(tab_rows[0:SCALE_AT, :].bitcast(I32), 0)
        nc.vector.memset(v_plane[:].rearrange("p h a j -> p (h a j)").bitcast(I32), 0)

        offset = held([P, P], F32, "offset")
        distance = held([P, P], F32, "distance")
        ident = held([P, P], F32, "ident")[:]
        nc.gpsimd.iota(offset[:], [[1, P]], base=0, channel_multiplier=-1, allow_small_or_imprecise_dtypes=True)
        nc.scalar.activation(distance[:], offset[:], ACT.Abs)
        nc.scalar.activation(ident, distance[:], ACT.Relu, bias=1.0, scale=-1.0)

        def zero_page(name, tag):
            page = held([P, T2], F32, name, tag=tag)
            nc.gpsimd.memset(page[:], 0.0)
            return page

        bid_pages = [zero_page("bid_page0", "offset")]

        tab_w = [held([P, T], I32, "tab_w%d" % a) for a in range(PASSES)]
        w1_scale_rows = w1_scales.rearrange("a (q r) c -> r q a c", r=4)
        w1_rows = w1_words.rearrange("a p n -> p a n")
        w1_halves = [held([P, PASSES, H], U8, "w1_half%d" % i) for i in range(2)]
        load_bytes(tab_rows[SCALE_AT:P, :], tab_scales.rearrange("a q t -> q a t"))
        load(pick[:], offs)
        load_bytes(tab_w[0][:], tab_words[0].rearrange("p t i -> p (t i)"))
        load(bid_at[:], offs2)
        for r in (0, 1):
            load_bytes(w1_plane[r:P:32, :, :], w1_scale_rows[r])
        load_bytes(tab_w[1][:], tab_words[1].rearrange("p t i -> p (t i)"))
        for r in (2, 3):
            load_bytes(w1_plane[r:P:32, :, :], w1_scale_rows[r])
        load_bytes(w1_halves[0][:], w1_rows[:, :, 0:H])

        picked_rows = held([P, S], U8, "picked_rows")
        nc.vector.tensor_copy(picked_rows[:], tab_rows[:].indirect(pick[:]))

        def move_scales(half):
            for q in (0, 2, 1, 3):
                rows = picked_rows[SCALE_AT + 8 * q : SCALE_AT + 8 * (q + 1), half * BANK : (half + 1) * BANK]
                load_bytes(v_plane[32 * q : 32 * q + 4, half, :, :], rows)

        wg1_sb = held([P, S], F32, "wg1")
        move_scales(0)
        load(wg1_sb[:, 0:LEAD], wg1[:, 0:LEAD])
        load(wg1_sb[:, LEAD:BANK], wg1[:, LEAD:BANK])
        move_scales(1)
        load(wg1_sb[:, BANK:S], wg1[:, BANK:S])
        load_bytes(w1_halves[1][:], w1_rows[:, :, H:])
        w2_raw = [held([P, SLOTS, H], F32, "w2_raw%d" % a) for a in range(PASSES)]
        for a in range(PASSES):
            load(w2_raw[a][:], w2[a * P * SLOTS : (a + 1) * P * SLOTS, :].rearrange("(p j) c -> p j c", j=SLOTS))
        allot_sb = [held([P, T2], F32, "allot%d" % s) for s in range(SLOTS)]
        for s in range(SLOTS):
            load(allot_sb[s][:], allot[P * s : P * (s + 1), :])
        load(ask_at[:], offs3)
        wg2_rows = wg2.rearrange("(q t) j -> q t j", t=SLOTS)
        wg2_parts = [held([P, 3, S], F32, "wg2_a"), held([P, 1, S], F32, "wg2_b")]
        for part, t0, t1 in ((wg2_parts[0], 0, 3), (wg2_parts[1], 3, 4)):
            for quad in (0, 2, 1, 3):
                load(part[32 * quad : 32 * quad + 32, :, :], wg2_rows[:, t0:t1, :])
        wg2_sb = [wg2_parts[t // 3][:, t % 3, :] for t in range(SLOTS)]
        w3_raw = held([P, SLOTS, N], F32, "w3_raw")
        load(w3_raw[:], w3.rearrange("(p j) n -> p j n", j=SLOTS))
        w4_codes = held([P, 2 * N], U8, "w4_codes")
        load_bytes(w4_codes[:], w4_words[0])

        v_codes = [held([P, S], I32, "v_codes%d" % a) for a in range(PASSES)]
        for a, j0, j1 in ((0, 0, S), (1, 0, LEAD), (1, LEAD, BANK), (1, BANK, S)):
            nc.vector.tensor_copy(v_codes[a][:, j0:j1].bitcast(U32), tab_w[a][:].bitcast(U32).indirect(entries(pick, j0, j1)))

        def scores(dst, weights, j0, j1, scale):
            acc = bank("scores", "three")
            half = j0 // BANK
            for a in range(PASSES):
                codes, plane = weights(a)
                rhs_scale = v_plane[:, half, a, j0 - half * BANK : j1 - half * BANK]
                product(acc[:, 0 : j1 - j0], codes, plane, v_codes[a][:, j0:j1].bitcast(FP8X4), rhs_scale, a == 0, a == PASSES - 1)
            nc.scalar.activation(dst[:, j0:j1], acc[:, 0 : j1 - j0], ACT.Copy, scale=scale)

        def bid_scores(s, j0, j1):
            at = 2 * P * (s % 2)
            weights = lambda a: (w1_halves[s // 2][:, a, at : at + 2 * P].bitcast(FP4X4), w1_plane[:, a, P * s : P * (s + 1)])
            scores(h1[s], weights, j0, j1, -1.0)

        h1 = [held([P, S], F32, "h1_%d" % s) for s in range(2)]
        for s, j0, j1 in ((0, 0, P), (0, P, LEAD), (1, 0, BANK), (0, LEAD, BANK), (0, BANK, S), (1, BANK, S)):
            bid_scores(s, j0, j1)
        bid_pages.append(zero_page("bid_page1", "tab_rows"))
        bid_pages.append(zero_page("bid_page2", "tab_w1"))

        def place_bid(s, j0=0, j1=S):
            page = bid_pages[s % len(bid_pages)]
            nc.vector.tensor_tensor(page[:].indirect(entries(bid_at, j0, j1)), h1[s][:, j0:j1], wg1_sb[:, j0:j1], ALU.mult)

        for s, j0, j1 in ((0, 0, LEAD), (1, 0, BANK), (0, LEAD, S), (1, BANK, S)):
            place_bid(s, j0, j1)

        w2_bf = held([P, PASSES * SLOTS * H], BF16, "w2_bf")
        for a in range(PASSES):
            nc.scalar.copy(
                w2_bf[:, a * SLOTS * H : (a + 1) * SLOTS * H].rearrange("p (t m j) -> p m t j", t=SLOTS, j=SLOTS),
                w2_raw[a][:].rearrange("p j (m t) -> p m t j", t=SLOTS),
            )
        w2_codes = held([P, PASSES * H], U32, "w2_codes")
        w2_plane = held([P, PASSES * H], U8, "w2_plane")
        quantise(w2_codes[:], w2_plane[:], w2_bf[:])

        for s, tag in ((2, "w2_raw1"), (3, None)):
            h1.append(held([P, S], F32, "h1_%d" % s, tag=tag))
            for j0 in range(0, S, BANK):
                bid_scores(s, j0, j0 + BANK)

        w4_plane = held([P, N], U8, "w4_plane", tag="w1_plane")
        nc.gpsimd.memset(w4_plane[:].bitcast(I32), 0)
        for q in range(4):
            load_bytes(w4_plane[32 * q : 32 * q + 4, :], w4_scales[0, 4 * q : 4 * q + 4, :])

        left_t = held([P, T2 // P, 2, P, 2], BF16, "left_t")

        def take_off(s):
            page = bid_pages[s % len(bid_pages)]
            accs = [bank("left_acc", "five") for c in range(CHUNKS)]
            blocks = BANK // P
            for n_src, source in enumerate((allot_sb[s], page)):
                for c, acc in enumerate(accs):
                    for i in range(blocks):
                        m0 = c * BANK + i * P
                        first, last = n_src == 0 and i == 0, n_src == 1 and i == blocks - 1
                        nc.tensor.matmul(
                            acc[:, i * P : (i + 1) * P], source[:, m0 : m0 + P], ident, start=first, stop=last, is_transpose=True
                        )
            for c, acc in enumerate(accs):
                nc.scalar.copy(
                    left_t[:, c * blocks : (c + 1) * blocks, :, 32 * s : 32 * (s + 1), :].rearrange("m i u p e -> m u i p e"),
                    acc[:].rearrange("m (i p u e) -> m u i p e", i=blocks, u=2, e=2),
                )

        take_off(0)
        place_bid(2)
        take_off(1)
        h2 = {}
        for t in ASK_ORDER:
            h2[t] = held([P, S], F32, "h2_%d" % t)
            weights = lambda a: (
                w2_codes[:, a * H + P * t : a * H + P * (t + 1)].bitcast(FP8X4),
                w2_plane[:, a * H + P * t : a * H + P * (t + 1)],
            )
            for j0 in range(0, S, BANK):
                scores(h2[t], weights, j0, j0 + BANK, 1.0)
        place_bid(3)
        take_off(2)
        take_off(3)

        pages = [zero_page("ask_page%d" % i, tag) for i, tag in enumerate(("h1_0", "w2_bf", "w2_raw1"))]
        ask_page = {t: pages[n % len(pages)] for n, t in enumerate(ASK_ORDER)}
        floor = [held([P, 2, BANK, 2], BF16, "floor%d" % c) for c in range(CHUNKS)]
        woven_tags = ["tab_w0", "allot2", "allot3", "wg1"]
        woven = [held([P, BANK, SLOTS], BF16, "woven%d" % c, tag=woven_tags[c]) for c in range(CHUNKS)]

        def place_ask(t):
            nc.vector.tensor_tensor(ask_page[t][:].indirect(ask_at[:]), h2[t][:], wg2_sb[t], ALU.mult)

        def rounding(t, piece, m0=0, m1=PIECE):
            at = piece % 2 * PIECE
            return floor[piece // 2][:, t // 2, at + m0 : at + m1, t % 2], ask_page[t][:, piece * PIECE + m0 : piece * PIECE + m1]

        def turn_back(piece):
            acc = bank("left", "five")
            for u in range(2):
                for i in range(2):
                    words = left_t[:, 2 * piece + i, u, :, :].rearrange("m p e -> m (p e)").bitcast(F32)
                    nc.tensor.transpose(acc[:].rearrange("p (i m u) -> p i u m", i=2, u=2)[:, i, u, :], words, ident)
            if piece not in PARKED:
                return acc[:].bitcast(BF16).rearrange("p (m u e) -> p m u e", u=2, e=2)
            at = piece % 2 * PIECE
            nc.scalar.copy(parked[piece // 2][:, at : at + PIECE, :], acc[:].rearrange("p (m u) -> p m u", u=2))

        parked = [held([P, BANK, 2], F32, "left%d" % c, tag=tag) for c, tag in enumerate(("v_codes0", "v_codes1", "h1_1"))]
        left = {}
        w3_bf = held([P, SLOTS * N], BF16, "w3_bf")
        for n, t in enumerate(ASK_ORDER[:-1]):
            place_ask(t)
            for piece in range(PIECES):
                if (n, piece) == (2, W3_AT):
                    nc.scalar.copy(
                        w3_bf[:].rearrange("p (g i j) -> p g j i", i=4, j=SLOTS),
                        w3_raw[:].rearrange("p j (g i) -> p g j i", i=4),
                    )
                nc.scalar.copy(*rounding(t, piece))
            if n == 0:
                for piece in PARKED + tuple(piece for piece in range(PIECES) if piece not in PARKED):
                    left[piece] = turn_back(piece)
        last = ASK_ORDER[-1]
        place_ask(last)

        w3_codes = held([P, N], U32, "w3_codes")
        w3_plane = held([P, N], U8, "w3_plane")
        quantise(w3_codes[:], w3_plane[:], w3_bf[:])
        for m0 in (0, P):
            nc.scalar.copy(*rounding(last, 0, m0, m0 + P))
        for piece in range(1, PIECES):
            dst, src = rounding(last, piece)
            if piece in ROUNDED_ASIDE:
                nc.gpsimd.tensor_scalar(dst, src, 1.0, 0.0, op0=ALU.mult, op1=ALU.add)
            else:
                nc.scalar.copy(dst, src)

        def clear(c, m0=0, m1=BANK):
            if c < len(parked):
                pairs = parked[c][:, m0:m1, :].rearrange("p m u -> p (m u)").bitcast(BF16).rearrange("p (m u e) -> p m u e", u=2, e=2)
            else:
                pairs = left[2 * c + m0 // PIECE]
            nc.vector.tensor_tensor(
                woven[c][:, m0:m1, :].rearrange("p m (u e) -> p m u e", u=2),
                pairs,
                floor[c][:, :, m0:m1, :].rearrange("p u m e -> p m u e"),
                ALU.max,
            )

        z_codes, z_plane = {}, {}

        def pack(c, width=BANK, tag=None):
            z_codes[c] = held([P, BANK], U32, "z_codes%d" % c, tag=tag)
            z_plane[c] = held([P, BANK], U8, "z_plane%d" % c)
            for m0 in range(0, BANK, width):
                values = woven[c][:, m0 : m0 + width, :].rearrange("p m t -> p (m t)")
                quantise(z_codes[c][:, m0 : m0 + width], z_plane[c][:, m0 : m0 + width], values)

        squash_tags = ("left_t", "wg2_a", "w2_raw0", "allot0")
        squashes = [held([P, N_TILES, BANK], F32, "squashed%d" % c, tag=squash_tags[c]) for c in range(CHUNKS)]
        result_tags = ("tab_w1", "allot1", "offset", "tab_rows")
        results = [held([P, N_TILES, BANK], F32, "result%d" % c, tag=result_tags[c]) for c in range(CHUNKS)]

        def reading(kind, c, i, m0, m1, acc):
            codes = w3_codes[:, i * P : (i + 1) * P].bitcast(FP8X4) if kind == "bounded" else w4_codes[:, 2 * P * i : 2 * P * (i + 1)].bitcast(FP4X4)
            plane = (w3_plane if kind == "bounded" else w4_plane)[:, i * P : (i + 1) * P]
            product(acc[:, m0:m1], codes, plane, z_codes[c][:, m0:m1].bitcast(FP8X4), z_plane[c][:, m0:m1])

        def squash(c, i, width=BANK):
            acc = bank("bounded", "three")
            for m0 in range(0, BANK, width):
                reading("bounded", c, i, m0, m0 + width, acc)
            nc.scalar.activation(squashes[c][:, i, :], acc[:], ACT.Tanh)

        def store(c, i, result):
            nc.sync.dma_start(out[i * P : (i + 1) * P, c * BANK : (c + 1) * BANK], result)

        def add_up(c, i):
            acc = bank("linear", "five")
            reading("linear", c, i, 0, BANK, acc)
            nc.vector.tensor_tensor(results[c][:, i, :], acc[:], squashes[c][:, i, :], ALU.add)
            store(c, i, results[c][:, i, :])

        def copy_linear(c, i, name):
            acc = bank("linear", "five")
            reading("linear", c, i, 0, BANK, acc)
            copied = held([P, BANK], F32, name)
            nc.scalar.copy(copied[:], acc[:])
            return copied

        def add_aside(c, i, copied, result):
            nc.gpsimd.tensor_tensor(result, copied[:], squashes[c][:, i, :], ALU.add)
            store(c, i, result)

        for m0, m1 in ((0, P), (P, PIECE), (PIECE, BANK)):
            clear(0, m0, m1)
        pack(0, PIECE)
        squash(0, 0, PIECE)
        squash(0, 1)
        first = copy_linear(0, 1, "copied0")
        for c in (1, 2):
            for m0 in (0, PIECE):
                clear(c, m0, m0 + PIECE)
            pack(c, PIECE)
        squash(1, 0)
        squash(0, 2)
        second = copy_linear(0, 2, "copied1")
        aside = held([P, 2, BANK], F32, "aside", tag=woven_tags[2])
        add_up(0, 0)
        add_aside(0, 1, first, aside[:, 0, :])
        clear(3, 0, PIECE)
        add_up(1, 0)
        clear(3, PIECE, BANK)
        squash(1, 1)
        add_up(1, 1)
        add_aside(0, 2, second, aside[:, 1, :])
        squash(1, 2)
        add_up(1, 2)
        for i in range(N_TILES):
            squash(2, i)
        pack(3, tag="copied1")
        for i in range(N_TILES):
            add_up(2, i)
        for i in range(N_TILES):
            squash(3, i)
            add_up(3, i)
